import numpy as np
import ml_dtypes


def mxq(x, axis, fmt="e4m3"):
    dtype, down = {"e4m3": (ml_dtypes.float8_e4m3fn, 7), "e5m2": (ml_dtypes.float8_e5m2, 14)}[fmt]
    v = np.moveaxis(np.asarray(x, np.float32).astype(ml_dtypes.bfloat16).astype(np.float64), axis, -1)
    blocks = v.reshape(v.shape[:-1] + (-1, 32))
    amax = np.abs(blocks).max(-1, keepdims=True)
    byte = np.maximum(np.where(amax > 0, np.frexp(amax)[1] - 1 + 127, 0) - down, 1)
    scale = np.exp2(byte - 127.0)
    codes = (blocks / scale).astype(np.float32).astype(dtype).astype(np.float64)
    return np.moveaxis((codes * scale).reshape(v.shape), -1, axis)


WIDE = False


def mx_kscale(k):
    if not WIDE:
        return np.ones(k)
    levels = np.array([10, -10, 5, -5, 0])
    if k % 512:
        return np.exp2(np.random.permutation(np.resize(levels, k // 32))).repeat(32)
    a = np.empty((k // 512, 16))
    for p in range(k // 512):
        a[p, :8] = np.random.permutation(np.resize(levels, 8))
        for g in range(8):
            far = levels[np.abs(levels - a[p, g]) >= 10]
            a[p, g + 8] = far[np.random.randint(len(far))]
    return np.exp2(a.ravel()).repeat(32)


def f64(x):
    return np.asarray(x).astype(np.float64)


def striped(idx):
    return np.tile(idx.reshape(-1, 16).T, (8, 1)).astype(np.uint16)


def unstriped(offs):
    return offs[:16].T.reshape(-1).astype(np.int64)


E2M1 = np.array([0.0, 0.5, 1.0, 1.5, 2.0, 3.0, 4.0, 6.0, -0.0, -0.5, -1.0, -1.5, -2.0, -3.0, -4.0, -6.0])


def pack_weight(w, fmt):
    k, n = w.shape
    w = f64(np.asarray(w, np.float32).astype(ml_dtypes.bfloat16)).reshape(k // 32, 32, n)
    amax = np.abs(w).max(1)
    if fmt == "e4m3":
        byte = np.frexp(amax)[1] - 1 + 127 - 7
    else:
        mant, ex = np.frexp(amax / 6.0)
        byte = np.where(mant > 0.5, ex, ex - 1) + 127
    byte = np.clip(np.where(amax > 0, byte, 1), 1, 254)
    scaled = (w * np.exp2(127.0 - byte)[:, None, :]).reshape(k, n).astype(np.float32)
    by_word = np.ascontiguousarray(scaled.reshape(k // 512, 128, 4, n).transpose(0, 1, 3, 2))
    if fmt == "e4m3":
        words = by_word.astype(ml_dtypes.float8_e4m3fn).view(np.uint8)
    else:
        c = by_word.astype(ml_dtypes.float4_e2m1fn).view(np.uint8) & 0xF
        words = (c[..., 0::2] | (c[..., 1::2] << 4)).reshape(k // 512, 128, 2 * n)
    return np.ascontiguousarray(words), np.ascontiguousarray(byte.astype(np.uint8).reshape(k // 512, 16, n))


def unpack_weight(words, scales, fmt):
    g, _, n = scales.shape
    words = np.ascontiguousarray(words).reshape(g, 128, n, -1)
    if fmt == "e4m3":
        vals = words.view(ml_dtypes.float8_e4m3fn).astype(np.float64)
    else:
        nib = np.empty((g, 128, n, 4), np.uint8)
        nib[..., 0::2] = words & 0xF
        nib[..., 1::2] = words >> 4
        vals = E2M1[nib]
    vals = vals * np.repeat(np.exp2(scales.astype(np.float64) - 127.0), 8, axis=1)[..., None]
    return vals.transpose(0, 1, 3, 2).reshape(g * 512, n)


def d_silu(v):
    s = 1.0 / (1.0 + np.exp(-np.maximum(v, -700.0)))
    return s * (1.0 + v * (1.0 - s))


K, T, E, C, H, N, TOP = 512, 512, 6, 256, 512, 512, 3


def by_expert(wq, xq):
    return np.concatenate([wq[e].T @ xq[:, e * C:(e + 1) * C] for e in range(E)], axis=1)


def setup_inputs():
    n = np.random.standard_normal
    v = mx_kscale(N)
    u = mx_kscale(H)
    deal = np.repeat(np.arange(E), C).reshape(TOP, T)[:, np.random.permutation(T)]
    deal = np.take_along_axis(deal, np.argsort(np.random.rand(TOP, T), axis=0), axis=0)
    for _ in range(8):
        s_, t_ = np.random.permutation(T).reshape(2, -1); r = np.random.randint(TOP, size=T // 2); x, y = deal[r, s_].copy(), deal[r, t_].copy()
        ok = ~((deal[:, s_] == y).any(0) | (deal[:, t_] == x).any(0)); deal[r[ok], s_[ok]] = y[ok]; deal[r[ok], t_[ok]] = x[ok]
    order = np.argsort(deal.reshape(-1) + 0.5 * np.random.rand(TOP * T))
    slot_token = order % T; pos = np.empty(TOP * T, np.int64); pos[order] = np.arange(TOP * T); pos = pos.reshape(TOP, T)
    g = np.random.uniform(0.5, 1.5, (TOP, T)); g = g / g.sum(0)
    w_slot = np.empty(E * C)
    for r in range(TOP): w_slot[pos[r]] = g[r]
    dy = pack_weight(n((N, T)) * v[:, None], "e4m3")
    wt = pack_weight(n((N, K)) / np.sqrt(N) / v[:, None], "e2m1")
    return {
        "dy_words": dy[0],
        "dy_scales": dy[1],
        "wt_words": wt[0],
        "wt_scales": wt[1],
        "wbt": (n((E, N, H)) / np.sqrt(N) / v[None, :, None] * u).astype(np.float32),
        "wat": (n((E, H, K)) / np.sqrt(H) / u[None, :, None]).astype(np.float32),
        "a": (n((H, E * C))).astype(np.float32),
        "gate": (np.tile(w_slot, (128, 1))).astype(np.float32),
        "offs": striped(slot_token),
        "pos1": striped(pos[0]),
        "pos2": striped(pos[1]),
        "pos3": striped(pos[2]),
    }


def reference(dy_words, dy_scales, wt_words, wt_scales, wbt, wat, a, gate, offs, pos1, pos2, pos3):
    wt = unpack_weight(wt_words, wt_scales, "e2m1")
    wbtq = mxq(f64(wbt), 1, "e4m3")
    watq = mxq(f64(wat), 1, "e4m3")
    idx = unstriped(offs)
    dy = unpack_weight(dy_words, dy_scales, "e4m3")
    base = wt.T @ dy
    dh = f64(gate[:1]) * by_expert(wbtq, dy[:, idx]) * d_silu(f64(a))
    dx = by_expert(watq, mxq(dh, 0, "e4m3"))
    c = dx[:, unstriped(pos1)] + dx[:, unstriped(pos2)] + dx[:, unstriped(pos3)]
    return base + c

@@ -1,0 +1,185 @@
+from contextlib import ExitStack
+
+import concourse.mybir as mybir
+
+K, T, E, C, H, N, TOP = 512, 512, 6, 256, 512, 512, 3
+S = E * C
+FLOPS = 2 * N * K * T + 2 * S * (N * H + H * K)
+
+F32 = mybir.dt.float32
+BF16 = mybir.dt.bfloat16
+I32 = mybir.dt.int32
+U32 = mybir.dt.uint32
+U16 = mybir.dt.uint16
+U8 = mybir.dt.uint8
+FP8X4 = mybir.dt.float8_e4m3fn_x4
+FP4X4 = mybir.dt.float4_e2m1fn_x4
+ALU = mybir.AluOpType
+ACT = mybir.ActivationFunctionType
+
+P = 128
+PACK = 4
+KT = K // P
+HALF = C // 2
+
+
+def tile_moe_adb_silu_kernel(
+    tc, dy_words, dy_scales, wt_words, wt_scales, wbt, wat, a, gate, offs, pos1, pos2, pos3, out
+):
+    nc = tc.nc
+    with ExitStack() as ctx:
+        keep = ctx.enter_context(tc.tile_pool(name="keep", bufs=1))
+        ring = ctx.enter_context(tc.tile_pool(name="ring", bufs=3))
+        psum = ctx.enter_context(tc.psum_pool(name="psum", bufs=1))
+
+        def load_plane(plane, scales):
+            rows = scales[0].rearrange("(q r) n -> r q n", r=4)
+            for r in range(4):
+                nc.sync.dma_start(plane[r:P:32, :].bitcast(I32), rows[r].bitcast(I32))
+
+        offs_t = keep.tile([P, S // 16], U16, name="offs_t")
+        nc.sync.dma_start(offs_t[:], offs)
+        dy_w = keep.tile([P, T], U32, name="dy_w", align_bytes=64)
+        nc.sync.dma_start(dy_w[:].bitcast(I32), dy_words[0].rearrange("p t d -> p (t d)").bitcast(I32))
+        dy_s = keep.tile([P, T], U8, name="dy_s", align_bytes=64)
+        nc.vector.memset(dy_s[:].bitcast(I32), 0)
+        load_plane(dy_s, dy_scales)
+
+        a_rows = a.rearrange("(p t) s -> p t s", t=PACK)
+        a_t, wb_raw, wa_raw = [], [], []
+        gate_t = keep.tile([P, S], F32, name="gate_t")
+        for e in range(E):
+            at = keep.tile([P, PACK, C], F32, name="a_%d" % e)
+            nc.sync.dma_start(at[:], a_rows[:, :, e * C:(e + 1) * C])
+            a_t.append(at)
+            wb = ring.tile([P, PACK, H], F32, name="wb_raw", bufs=4)
+            nc.sync.dma_start(wb[:], wbt[e].rearrange("(p j) c -> p j c", j=PACK))
+            wb_raw.append(wb)
+            if e == 0:
+                nc.sync.dma_start(gate_t[:], gate)
+        def load_wa(half):
+            for e in range(E):
+                wa = keep.tile([P, PACK, K // 2], F32, name="wa_raw_%d_%d" % (half, e))
+                nc.sync.dma_start(wa[:], wat[e].rearrange("(p j) c -> p j c", j=PACK)[:, :, half * (K // 2):(half + 1) * (K // 2)])
+                wa_raw.append(wa)
+
+        load_wa(0)
+        wt_w = keep.tile([P, 2 * K], U8, name="wt_w", align_bytes=64)
+        nc.sync.dma_start(wt_w[:].bitcast(I32), wt_words[0].bitcast(I32))
+        wt_s = keep.tile([P, K], U8, name="wt_s", align_bytes=64)
+        nc.vector.memset(wt_s[:].bitcast(I32), 0)
+        load_plane(wt_s, wt_scales)
+        pos_t = []
+        for r, pos in enumerate((pos1, pos2, pos3)):
+            pt = keep.tile([P, T // 16], U16, name="pos_%d" % r)
+            nc.sync.dma_start(pt[:], pos)
+            pos_t.append(pt)
+        load_wa(1)
+
+        g_w, g_s = [], []
+        for e in range(E):
+            cols = offs_t[:, e * (C // 16):(e + 1) * (C // 16)]
+            gw = keep.tile([P, C], U32, name="g_w_%d" % e, align_bytes=64)
+            nc.vector.tensor_copy(gw[:], dy_w[:].indirect(cols))
+            gs = keep.tile([P, C], U8, name="g_s_%d" % e, align_bytes=64)
+            nc.vector.tensor_copy(gs[:], dy_s[:].indirect(cols))
+            g_w.append(gw)
+            g_s.append(gs)
+
+        gate_h = gate_t
+        dh_w, dh_s = [], []
+        for e in range(E):
+            silu_n = ring.tile([P, PACK, C], F32, name="silu_n")
+            nc.scalar.activation(silu_n[:], a_t[e][:], ACT.Silu, scale=-1.0)
+            tanh_h = ring.tile([P, PACK, C], F32, name="tanh_h")
+            nc.scalar.activation(tanh_h[:], a_t[e][:], ACT.Tanh, scale=0.5)
+            if e == 0:
+                nc.scalar.activation(gate_h[:], gate_t[:], ACT.Copy, scale=-0.5)
+
+            wb_bf = ring.tile([P, PACK, P, PACK], BF16, name="wb_bf", align_bytes=64, bufs=2)
+            cast = nc.vector.tensor_copy if e == 1 else nc.scalar.copy
+            cast(
+                wb_bf[:].rearrange("p t m j -> p m j t"),
+                wb_raw[e][:].rearrange("p j (m t) -> p m j t", t=PACK),
+            )
+            wb_w = ring.tile([P, H], U32, name="wb_w", align_bytes=64)
+            wb_s = ring.tile([P, H], U8, name="wb_s", align_bytes=64)
+            nc.vector.quantize_mx(wb_w[:].bitcast(FP8X4), wb_s[:], wb_bf[:].rearrange("p t m j -> p (t m j)"))
+
+            f1 = silu_n
+            nc.vector.scalar_tensor_tensor(
+                f1[:], silu_n[:], 1.0,
+                gate_h[:, e * C:(e + 1) * C].unsqueeze(1).to_broadcast([P, PACK, C]),
+                ALU.subtract, ALU.mult,
+            )
+            f2 = tanh_h
+            nc.vector.scalar_tensor_tensor(f2[:], tanh_h[:], 1.0, f1[:], ALU.add, ALU.mult)
+
+            dh_bf = ring.tile([P, C, PACK], BF16, name="dh_bf", align_bytes=64)
+            for h in range(2):
+                sl = slice(h * HALF, (h + 1) * HALF)
+                bank = psum.tile([P, PACK, HALF], F32, name="s1_%d" % ((2 * e + h) % 4))
+                for t in range(PACK):
+                    nc.tensor.matmul_mx(
+                        bank[:, t, :],
+                        lhsT=wb_w[:, t * P:(t + 1) * P].bitcast(FP8X4), lhsT_scale=wb_s[:, t * P:(t + 1) * P],
+                        rhs=g_w[e][:, sl].bitcast(FP8X4), rhs_scale=g_s[e][:, sl],
+                        start=True, stop=True,
+                    )
+                nc.vector.tensor_tensor(
+                    dh_bf[:, sl, :].rearrange("p (c i) t -> p c t i", i=4),
+                    bank[:].rearrange("p t (c i) -> p c t i", i=4),
+                    f2[:, :, sl].rearrange("p t (c i) -> p c t i", i=4),
+                    ALU.mult,
+                )
+            dw = keep.tile([P, C], U32, name="dh_w_%d" % e, align_bytes=64)
+            ds = keep.tile([P, C], U8, name="dh_s_%d" % e, align_bytes=64)
+            nc.vector.quantize_mx(dw[:].bitcast(FP8X4), ds[:], dh_bf[:].rearrange("p c t -> p (c t)"))
+            dh_w.append(dw)
+            dh_s.append(ds)
+
+        for q in range(KT):
+            kc = slice(q * P, (q + 1) * P)
+            base_ps = psum.tile([P, T], F32, name="base_ps")
+            nc.tensor.matmul_mx(
+                base_ps[:],
+                lhsT=wt_w[:, 2 * q * P:2 * (q + 1) * P].bitcast(FP4X4), lhsT_scale=wt_s[:, kc],
+                rhs=dy_w[:].bitcast(FP8X4), rhs_scale=dy_s[:],
+                start=True, stop=True,
+            )
+            base = keep.tile([P, T], F32, name="base_%d" % q)
+            nc.scalar.copy(base[:], base_ps[:])
+
+            dx = keep.tile([P, S], F32, name="dx_%d" % q)
+            for u in range(E // 2):
+                wa_bf = ring.tile([P, 2, P, PACK], BF16, name="wa_bf", align_bytes=64)
+                for v in range(2):
+                    cast = nc.vector.tensor_copy if q == 0 else nc.scalar.copy
+                    cast(
+                        wa_bf[:, v, :, :].rearrange("p (c i) j -> p c j i", i=4),
+                        wa_raw[(q // 2) * E + 2 * u + v][:, :, (q % 2) * P:(q % 2 + 1) * P].rearrange("p j (c i) -> p c j i", i=4),
+                    )
+                wa_w = ring.tile([P, 2 * P], U32, name="wa_w", align_bytes=64)
+                wa_s = ring.tile([P, 2 * P], U8, name="wa_s", align_bytes=64)
+                nc.vector.quantize_mx(wa_w[:].bitcast(FP8X4), wa_s[:], wa_bf[:].rearrange("p v m j -> p (v m j)"))
+                bank = psum.tile([P, 2 * C], F32, name="s2_%d" % u)
+                for v in range(2):
+                    e = 2 * u + v
+                    nc.tensor.matmul_mx(
+                        bank[:, v * C:(v + 1) * C],
+                        lhsT=wa_w[:, v * P:(v + 1) * P].bitcast(FP8X4), lhsT_scale=wa_s[:, v * P:(v + 1) * P],
+                        rhs=dh_w[e][:].bitcast(FP8X4), rhs_scale=dh_s[e][:],
+                        start=True, stop=True,
+                    )
+                nc.scalar.copy(dx[:, 2 * u * C:2 * (u + 1) * C], bank[:])
+
+            acc = [base[:, 0:T // 2], base[:, T // 2:T]]
+            for r in range(TOP):
+                for h in range(2):
+                    nxt = ring.tile([P, T // 2], F32, name="sum_%d_%d" % (r, h), bufs=2)
+                    nc.vector.tensor_tensor(
+                        nxt[:], dx[:].indirect(pos_t[r][:, h * 16:(h + 1) * 16]), acc[h], ALU.add
+                    )
+                    acc[h] = nxt[:]
+            for h in range(2):
+                nc.sync.dma_start(out[kc, h * (T // 2):(h + 1) * (T // 2)], acc[h])

@@ -21,6 +21,10 @@ P = 128
 PACK = 4
 KT = K // P
 HALF = C // 2
+WB_ENG = "ssssss"
+WA_ENG = "sssvvvssssss"
+GN = 512
+WIN = 704
 
 
 def tile_moe_adb_silu_kernel(
@@ -32,31 +36,46 @@ def tile_moe_adb_silu_kernel(
         ring = ctx.enter_context(tc.tile_pool(name="ring", bufs=3))
         psum = ctx.enter_context(tc.psum_pool(name="psum", bufs=1))
 
+        def cast(eng, dst, src):
+            if eng == "s":
+                nc.scalar.copy(dst, src)
+            elif eng == "v":
+                nc.vector.tensor_copy(dst, src)
+            else:
+                nc.gpsimd.tensor_scalar(dst, src, 1.0, 0.0, ALU.mult, ALU.add)
+
         def load_plane(plane, scales):
             rows = scales[0].rearrange("(q r) n -> r q n", r=4)
             for r in range(4):
-                nc.sync.dma_start(plane[r:P:32, :].bitcast(I32), rows[r].bitcast(I32))
+                nc.sync.dma_start(plane[r:P:32, 0:T].bitcast(I32), rows[r].bitcast(I32))
 
         offs_t = keep.tile([P, S // 16], U16, name="offs_t")
         nc.sync.dma_start(offs_t[:], offs)
-        dy_w = keep.tile([P, T], U32, name="dy_w", align_bytes=64)
-        nc.sync.dma_start(dy_w[:].bitcast(I32), dy_words[0].rearrange("p t d -> p (t d)").bitcast(I32))
-        dy_s = keep.tile([P, T], U8, name="dy_s", align_bytes=64)
+        dy_w = keep.tile([P, WIN], U32, name="dy_w", align_bytes=64)
+        nc.sync.dma_start(dy_w[:, 0:T].bitcast(I32), dy_words[0].rearrange("p t d -> p (t d)").bitcast(I32))
+        dy_s = keep.tile([P, WIN], U8, name="dy_s", align_bytes=64)
         nc.vector.memset(dy_s[:].bitcast(I32), 0)
+        if WIN > T:
+            nc.vector.memset(dy_w[:, T:WIN].bitcast(I32), 0)
         load_plane(dy_s, dy_scales)
 
         a_rows = a.rearrange("(p t) s -> p t s", t=PACK)
         a_t, wb_raw, wa_raw = [], [], []
         gate_t = keep.tile([P, S], F32, name="gate_t")
         for e in range(E):
-            at = keep.tile([P, PACK, C], F32, name="a_%d" % e)
+            at = ring.tile([P, PACK, C], F32, name="a_raw", bufs=3)
             nc.sync.dma_start(at[:], a_rows[:, :, e * C:(e + 1) * C])
             a_t.append(at)
-            wb = ring.tile([P, PACK, H], F32, name="wb_raw", bufs=4)
+            if e == 0 and True:
+                nc.sync.dma_start(gate_t[:, 0:512], gate[:, 0:512])
+            wb = ring.tile([P, PACK, H], F32, name="wb_raw", bufs=3)
             nc.sync.dma_start(wb[:], wbt[e].rearrange("(p j) c -> p j c", j=PACK))
             wb_raw.append(wb)
-            if e == 0:
-                nc.sync.dma_start(gate_t[:], gate)
+            if e == 0 and False:
+                nc.sync.dma_start(gate_t[:, 0:512], gate[:, 0:512])
+            if e == 1 and 512 < S:
+                nc.sync.dma_start(gate_t[:, 512:S], gate[:, 512:S])
+
         def load_wa(half):
             for e in range(E):
                 wa = keep.tile([P, PACK, K // 2], F32, name="wa_raw_%d_%d" % (half, e))
@@ -76,60 +95,58 @@ def tile_moe_adb_silu_kernel(
             pos_t.append(pt)
         load_wa(1)
 
-        g_w, g_s = [], []
-        for e in range(E):
-            cols = offs_t[:, e * (C // 16):(e + 1) * (C // 16)]
-            gw = keep.tile([P, C], U32, name="g_w_%d" % e, align_bytes=64)
-            nc.vector.tensor_copy(gw[:], dy_w[:].indirect(cols))
-            gs = keep.tile([P, C], U8, name="g_s_%d" % e, align_bytes=64)
-            nc.vector.tensor_copy(gs[:], dy_s[:].indirect(cols))
-            g_w.append(gw)
-            g_s.append(gs)
+        g_w = keep.tile([P, S], U32, name="g_w", align_bytes=64)
+        g_s = keep.tile([P, S], U8, name="g_s", align_bytes=64)
+        for c0 in range(0, S, GN):
+            cols = offs_t[:, c0 // 16:(c0 + GN) // 16]
+            nc.vector.tensor_copy(g_w[:, c0:c0 + GN], dy_w[:].indirect(cols))
+            nc.vector.tensor_copy(g_s[:, c0:c0 + GN], dy_s[:].indirect(cols))
 
-        gate_h = gate_t
         dh_w, dh_s = [], []
-        for e in range(E):
-            silu_n = ring.tile([P, PACK, C], F32, name="silu_n")
+
+        def hidden(e):
+            silu_n = ring.tile([P, PACK, C], F32, name="silu_n", bufs=3)
             nc.scalar.activation(silu_n[:], a_t[e][:], ACT.Silu, scale=-1.0)
-            tanh_h = ring.tile([P, PACK, C], F32, name="tanh_h")
+            tanh_h = ring.tile([P, PACK, C], F32, name="tanh_h", bufs=3)
             nc.scalar.activation(tanh_h[:], a_t[e][:], ACT.Tanh, scale=0.5)
             if e == 0:
-                nc.scalar.activation(gate_h[:], gate_t[:], ACT.Copy, scale=-0.5)
+                nc.gpsimd.tensor_scalar(gate_t[:, 0:512], gate_t[:, 0:512], -0.5, 0.0, ALU.mult, ALU.add)
+            if e == 1 and 512 < S:
+                nc.gpsimd.tensor_scalar(gate_t[:, 512:S], gate_t[:, 512:S], -0.5, 0.0, ALU.mult, ALU.add)
 
-            wb_bf = ring.tile([P, PACK, P, PACK], BF16, name="wb_bf", align_bytes=64, bufs=2)
-            cast = nc.vector.tensor_copy if e == 1 else nc.scalar.copy
+            wb_bf = ring.tile([P, 2, 2, P, PACK], BF16, name="wb_bf", align_bytes=64, bufs=2)
             cast(
-                wb_bf[:].rearrange("p t m j -> p m j t"),
-                wb_raw[e][:].rearrange("p j (m t) -> p m j t", t=PACK),
+                WB_ENG[e],
+                wb_bf[:].rearrange("p u t m j -> p u m j t"),
+                wb_raw[e][:].rearrange("p j (m u t) -> p u m j t", u=2, t=2),
             )
-            wb_w = ring.tile([P, H], U32, name="wb_w", align_bytes=64)
-            wb_s = ring.tile([P, H], U8, name="wb_s", align_bytes=64)
-            nc.vector.quantize_mx(wb_w[:].bitcast(FP8X4), wb_s[:], wb_bf[:].rearrange("p t m j -> p (t m j)"))
+            wb_w = ring.tile([P, H], U32, name="wb_w", align_bytes=64, bufs=2)
+            wb_s = ring.tile([P, H], U8, name="wb_s", align_bytes=64, bufs=2)
+            nc.vector.quantize_mx(wb_w[:].bitcast(FP8X4), wb_s[:], wb_bf[:].rearrange("p u t m j -> p (u t m j)"))
 
-            f1 = silu_n
             nc.vector.scalar_tensor_tensor(
-                f1[:], silu_n[:], 1.0,
-                gate_h[:, e * C:(e + 1) * C].unsqueeze(1).to_broadcast([P, PACK, C]),
+                silu_n[:], silu_n[:], 1.0,
+                gate_t[:, e * C:(e + 1) * C].unsqueeze(1).to_broadcast([P, PACK, C]),
                 ALU.subtract, ALU.mult,
             )
-            f2 = tanh_h
-            nc.vector.scalar_tensor_tensor(f2[:], tanh_h[:], 1.0, f1[:], ALU.add, ALU.mult)
+            nc.vector.scalar_tensor_tensor(tanh_h[:], tanh_h[:], 1.0, silu_n[:], ALU.add, ALU.mult)
 
-            dh_bf = ring.tile([P, C, PACK], BF16, name="dh_bf", align_bytes=64)
+            dh_bf = ring.tile([P, C, PACK], BF16, name="dh_bf", align_bytes=64, bufs=2)
             for h in range(2):
                 sl = slice(h * HALF, (h + 1) * HALF)
-                bank = psum.tile([P, PACK, HALF], F32, name="s1_%d" % ((2 * e + h) % 4))
+                gl = slice(e * C + h * HALF, e * C + (h + 1) * HALF)
+                bank = psum.tile([P, PACK, HALF], F32, name="s1", bufs=4)
                 for t in range(PACK):
                     nc.tensor.matmul_mx(
                         bank[:, t, :],
                         lhsT=wb_w[:, t * P:(t + 1) * P].bitcast(FP8X4), lhsT_scale=wb_s[:, t * P:(t + 1) * P],
-                        rhs=g_w[e][:, sl].bitcast(FP8X4), rhs_scale=g_s[e][:, sl],
+                        rhs=g_w[:, gl].bitcast(FP8X4), rhs_scale=g_s[:, gl],
                         start=True, stop=True,
                     )
                 nc.vector.tensor_tensor(
-                    dh_bf[:, sl, :].rearrange("p (c i) t -> p c t i", i=4),
-                    bank[:].rearrange("p t (c i) -> p c t i", i=4),
-                    f2[:, :, sl].rearrange("p t (c i) -> p c t i", i=4),
+                    dh_bf[:, sl, :].rearrange("p (c i) t -> p c t i", i=2),
+                    bank[:].rearrange("p t (c i) -> p c t i", i=2),
+                    tanh_h[:, :, sl].rearrange("p t (c i) -> p c t i", i=2),
                     ALU.mult,
                 )
             dw = keep.tile([P, C], U32, name="dh_w_%d" % e, align_bytes=64)
@@ -138,31 +155,39 @@ def tile_moe_adb_silu_kernel(
             dh_w.append(dw)
             dh_s.append(ds)
 
-        for q in range(KT):
+        wa_q = {}
+
+        def quant_wa(q):
+            for u in range(E // 2):
+                wa_bf = ring.tile([P, 2, P, PACK], BF16, name="wa_bf", align_bytes=64, bufs=6)
+                for v in range(2):
+                    cast(
+                        WA_ENG[3 * q + u],
+                        wa_bf[:, v, :, :].rearrange("p (c i) j -> p c j i", i=2),
+                        wa_raw[(q // 2) * E + 2 * u + v][:, :, (q % 2) * P:(q % 2 + 1) * P].rearrange("p j (c i) -> p c j i", i=2),
+                    )
+                wa_w = ring.tile([P, 2 * P], U32, name="wa_w", align_bytes=64, bufs=12)
+                wa_s = ring.tile([P, 2 * P], U8, name="wa_s", align_bytes=64, bufs=12)
+                nc.vector.quantize_mx(wa_w[:].bitcast(FP8X4), wa_s[:], wa_bf[:].rearrange("p v m j -> p (v m j)"))
+                wa_q[q, u] = (wa_w, wa_s)
+
+        res = {}
+
+        def slots(q):
             kc = slice(q * P, (q + 1) * P)
-            base_ps = psum.tile([P, T], F32, name="base_ps")
+            base_ps = psum.tile([P, T], F32, name="s2", bufs=4)
             nc.tensor.matmul_mx(
                 base_ps[:],
                 lhsT=wt_w[:, 2 * q * P:2 * (q + 1) * P].bitcast(FP4X4), lhsT_scale=wt_s[:, kc],
-                rhs=dy_w[:].bitcast(FP8X4), rhs_scale=dy_s[:],
+                rhs=dy_w[:, 0:T].bitcast(FP8X4), rhs_scale=dy_s[:, 0:T],
                 start=True, stop=True,
             )
-            base = keep.tile([P, T], F32, name="base_%d" % q)
+            base = ring.tile([P, T], F32, name="base", bufs=4)
             nc.scalar.copy(base[:], base_ps[:])
-
             dx = keep.tile([P, S], F32, name="dx_%d" % q)
             for u in range(E // 2):
-                wa_bf = ring.tile([P, 2, P, PACK], BF16, name="wa_bf", align_bytes=64)
-                for v in range(2):
-                    cast = nc.vector.tensor_copy if q == 0 else nc.scalar.copy
-                    cast(
-                        wa_bf[:, v, :, :].rearrange("p (c i) j -> p c j i", i=4),
-                        wa_raw[(q // 2) * E + 2 * u + v][:, :, (q % 2) * P:(q % 2 + 1) * P].rearrange("p j (c i) -> p c j i", i=4),
-                    )
-                wa_w = ring.tile([P, 2 * P], U32, name="wa_w", align_bytes=64)
-                wa_s = ring.tile([P, 2 * P], U8, name="wa_s", align_bytes=64)
-                nc.vector.quantize_mx(wa_w[:].bitcast(FP8X4), wa_s[:], wa_bf[:].rearrange("p v m j -> p (v m j)"))
-                bank = psum.tile([P, 2 * C], F32, name="s2_%d" % u)
+                wa_w, wa_s = wa_q[q, u]
+                bank = psum.tile([P, 2 * C], F32, name="s2", bufs=4)
                 for v in range(2):
                     e = 2 * u + v
                     nc.tensor.matmul_mx(
@@ -172,14 +197,37 @@ def tile_moe_adb_silu_kernel(
                         start=True, stop=True,
                     )
                 nc.scalar.copy(dx[:, 2 * u * C:2 * (u + 1) * C], bank[:])
+            res[q] = (base, dx)
 
+        def combine(q):
+            kc = slice(q * P, (q + 1) * P)
+            base, dx = res[q]
             acc = [base[:, 0:T // 2], base[:, T // 2:T]]
             for r in range(TOP):
                 for h in range(2):
-                    nxt = ring.tile([P, T // 2], F32, name="sum_%d_%d" % (r, h), bufs=2)
+                    nxt = ring.tile([P, T // 2], F32, name="sum_%d_%d" % (r, h), bufs=1 if r < TOP - 1 else 2)
                     nc.vector.tensor_tensor(
                         nxt[:], dx[:].indirect(pos_t[r][:, h * 16:(h + 1) * 16]), acc[h], ALU.add
                     )
                     acc[h] = nxt[:]
             for h in range(2):
                 nc.sync.dma_start(out[kc, h * (T // 2):(h + 1) * (T // 2)], acc[h])
+
+        hidden(0)
+        hidden(1)
+        hidden(2)
+        hidden(3)
+        hidden(4)
+        hidden(5)
+        quant_wa(0)
+        quant_wa(1)
+        slots(0)
+        quant_wa(2)
+        slots(1)
+        combine(0)
+        quant_wa(3)
+        slots(2)
+        combine(1)
+        slots(3)
+        combine(2)
+        combine(3)

@@ -1,6 +1,7 @@
 from contextlib import ExitStack
 
 import concourse.mybir as mybir
+from concourse.masks import make_identity
 
 K, T, E, C, H, N, TOP = 512, 512, 6, 256, 512, 512, 3
 S = E * C
@@ -60,40 +61,74 @@ def tile_moe_adb_silu_kernel(
         load_plane(dy_s, dy_scales)
 
         a_rows = a.rearrange("(p t) s -> p t s", t=PACK)
-        a_t, wb_raw, wa_raw = [], [], []
-        gate_t = keep.tile([P, S], F32, name="gate_t")
-        for e in range(E):
-            at = ring.tile([P, PACK, C], F32, name="a_raw", bufs=3)
-            nc.sync.dma_start(at[:], a_rows[:, :, e * C:(e + 1) * C])
-            a_t.append(at)
-            if e == 0 and True:
-                nc.sync.dma_start(gate_t[:, 0:512], gate[:, 0:512])
-            wb = ring.tile([P, PACK, H], F32, name="wb_raw", bufs=3)
-            nc.sync.dma_start(wb[:], wbt[e].rearrange("(p j) c -> p j c", j=PACK))
-            wb_raw.append(wb)
-            if e == 0 and False:
-                nc.sync.dma_start(gate_t[:, 0:512], gate[:, 0:512])
-            if e == 1 and 512 < S:
-                nc.sync.dma_start(gate_t[:, 512:S], gate[:, 512:S])
-
-        def load_wa(half):
-            for e in range(E):
-                wa = keep.tile([P, PACK, K // 2], F32, name="wa_raw_%d_%d" % (half, e))
-                nc.sync.dma_start(wa[:], wat[e].rearrange("(p j) c -> p j c", j=PACK)[:, :, half * (K // 2):(half + 1) * (K // 2)])
-                wa_raw.append(wa)
-
-        load_wa(0)
+        a_t, wb_raw, wa_raw, pos_t = {}, {}, {}, []
+        gate_r = keep.tile([P, P], F32, name="gate_r")
+        ident = keep.tile([P, P], F32, name="ident")
+        make_identity(nc, ident[:])
         wt_w = keep.tile([P, 2 * K], U8, name="wt_w", align_bytes=64)
-        nc.sync.dma_start(wt_w[:].bitcast(I32), wt_words[0].bitcast(I32))
         wt_s = keep.tile([P, K], U8, name="wt_s", align_bytes=64)
         nc.vector.memset(wt_s[:].bitcast(I32), 0)
-        load_plane(wt_s, wt_scales)
-        pos_t = []
-        for r, pos in enumerate((pos1, pos2, pos3)):
-            pt = keep.tile([P, T // 16], U16, name="pos_%d" % r)
-            nc.sync.dma_start(pt[:], pos)
-            pos_t.append(pt)
-        load_wa(1)
+        wt_rows = wt_scales[0].rearrange("(q r) n -> r q n", r=4)
+
+        def load_a(e0, ne):
+            at = keep.tile([P, PACK, ne * C], F32, name="a_raw_%d" % e0)
+            nc.sync.dma_start(at[:], a_rows[:, :, e0 * C:(e0 + ne) * C])
+            for e in range(e0, e0 + ne):
+                a_t[e] = at[:, :, (e - e0) * C:(e - e0 + 1) * C]
+
+        def load_wb(e):
+            wb = ring.tile([P, PACK, H], F32, name="wb_raw", bufs=3)
+            nc.sync.dma_start(wb[:], wbt[e].rearrange("(p j) c -> p j c", j=PACK))
+            wb_raw[e] = wb
+
+        def load_wa(e, c0, c1):
+            wa = keep.tile([P, PACK, c1 - c0], F32, name="wa_raw_%d_%d" % (e, c0))
+            nc.sync.dma_start(wa[:], wat[e].rearrange("(p j) c -> p j c", j=PACK)[:, :, c0:c1])
+            for q in range(c0 // P, c1 // P):
+                wa_raw[e, q] = wa[:, :, q * P - c0:(q + 1) * P - c0]
+
+        def load_gate(c0, c1):
+            nc.sync.dma_start(gate_r[:], gate.rearrange("r (b p) -> (r b) p", p=P)[0:P, :])
+
+        def load_small(i):
+            if i < 4:
+                nc.sync.dma_start(wt_s[i:P:32, :].bitcast(I32), wt_rows[i].bitcast(I32))
+            elif i == 4:
+                nc.sync.dma_start(wt_w[:].bitcast(I32), wt_words[0].bitcast(I32))
+            else:
+                pt = keep.tile([P, T // 16], U16, name="pos_%d" % (i - 5))
+                nc.sync.dma_start(pt[:], (pos1, pos2, pos3)[i - 5])
+                pos_t.append(pt)
+
+        load_a(0, 1)
+        load_gate(0, 1536)
+        load_wb(0)
+        load_a(1, 1)
+        load_wb(1)
+        load_a(2, 2)
+        load_wb(2)
+        load_wb(3)
+        load_a(4, 2)
+        load_wb(4)
+        load_wb(5)
+        load_wa(0, 0, 512)
+        load_small(0)
+        load_wa(1, 0, 512)
+        load_small(1)
+        load_wa(2, 0, 256)
+        load_small(2)
+        load_wa(3, 0, 256)
+        load_small(3)
+        load_wa(4, 0, 256)
+        load_small(4)
+        load_wa(5, 0, 256)
+        load_small(5)
+        load_wa(2, 256, 512)
+        load_small(6)
+        load_wa(3, 256, 512)
+        load_small(7)
+        load_wa(4, 256, 512)
+        load_wa(5, 256, 512)
 
         g_w = keep.tile([P, S], U32, name="g_w", align_bytes=64)
         g_s = keep.tile([P, S], U8, name="g_s", align_bytes=64)
@@ -103,16 +138,23 @@ def tile_moe_adb_silu_kernel(
             nc.vector.tensor_copy(g_s[:, c0:c0 + GN], dy_s[:].indirect(cols))
 
         dh_w, dh_s = [], []
+        gate_ps = psum.tile([P, P], F32, name="s2", bufs=4)
+        nc.tensor.transpose(gate_ps[:], gate_r[:], ident[:])
+        gate_c = keep.tile([P, S // P], F32, name="gate_c")
+        nc.vector.tensor_scalar(gate_c[:], gate_ps[:, 0:S // P], -0.5, None, ALU.mult)
+        gate_b = []
+        for u in range(E // 2):
+            gb = psum.tile([P, 2 * C], F32, name="s2", bufs=4)
+            for j in range(2 * C // P):
+                b = u * (2 * C // P) + j
+                nc.tensor.transpose(gb[:, j * P:(j + 1) * P], gate_c[:, b:b + 1].to_broadcast([P, P]), ident[:])
+            gate_b.append(gb)
 
         def hidden(e):
             silu_n = ring.tile([P, PACK, C], F32, name="silu_n", bufs=3)
-            nc.scalar.activation(silu_n[:], a_t[e][:], ACT.Silu, scale=-1.0)
+            nc.scalar.activation(silu_n[:], a_t[e], ACT.Silu, scale=-1.0)
             tanh_h = ring.tile([P, PACK, C], F32, name="tanh_h", bufs=3)
-            nc.scalar.activation(tanh_h[:], a_t[e][:], ACT.Tanh, scale=0.5)
-            if e == 0:
-                nc.gpsimd.tensor_scalar(gate_t[:, 0:512], gate_t[:, 0:512], -0.5, 0.0, ALU.mult, ALU.add)
-            if e == 1 and 512 < S:
-                nc.gpsimd.tensor_scalar(gate_t[:, 512:S], gate_t[:, 512:S], -0.5, 0.0, ALU.mult, ALU.add)
+            nc.scalar.activation(tanh_h[:], a_t[e], ACT.Tanh, scale=0.5)
 
             wb_bf = ring.tile([P, 2, 2, P, PACK], BF16, name="wb_bf", align_bytes=64, bufs=2)
             cast(
@@ -126,7 +168,7 @@ def tile_moe_adb_silu_kernel(
 
             nc.vector.scalar_tensor_tensor(
                 silu_n[:], silu_n[:], 1.0,
-                gate_t[:, e * C:(e + 1) * C].unsqueeze(1).to_broadcast([P, PACK, C]),
+                gate_b[e // 2][:, (e % 2) * C:(e % 2 + 1) * C].unsqueeze(1).to_broadcast([P, PACK, C]),
                 ALU.subtract, ALU.mult,
             )
             nc.vector.scalar_tensor_tensor(tanh_h[:], tanh_h[:], 1.0, silu_n[:], ALU.add, ALU.mult)
@@ -159,12 +201,12 @@ def tile_moe_adb_silu_kernel(
 
         def quant_wa(q):
             for u in range(E // 2):
-                wa_bf = ring.tile([P, 2, P, PACK], BF16, name="wa_bf", align_bytes=64, bufs=6)
+                wa_bf = ring.tile([P, 2, P, PACK], BF16, name="wa_bf", align_bytes=64, bufs=8)
                 for v in range(2):
                     cast(
                         WA_ENG[3 * q + u],
                         wa_bf[:, v, :, :].rearrange("p (c i) j -> p c j i", i=2),
-                        wa_raw[(q // 2) * E + 2 * u + v][:, :, (q % 2) * P:(q % 2 + 1) * P].rearrange("p j (c i) -> p c j i", i=2),
+                        wa_raw[2 * u + v, q].rearrange("p j (c i) -> p c j i", i=2),
                     )
                 wa_w = ring.tile([P, 2 * P], U32, name="wa_w", align_bytes=64, bufs=12)
                 wa_s = ring.tile([P, 2 * P], U8, name="wa_s", align_bytes=64, bufs=12)

@@ -20,12 +20,12 @@ ACT = mybir.ActivationFunctionType
 
 P = 128
 PACK = 4
-KT = K // P
+LIST_COL = 16
+K_TILES = K // P
+PAIRS = E // 2
 HALF = C // 2
-WB_ENG = "ssssss"
-WA_ENG = "sssvvvssssss"
-GN = 512
-WIN = 704
+GATHER = 2 * C
+WINDOW = 704
 
 
 def tile_moe_adb_silu_kernel(
@@ -37,198 +37,162 @@ def tile_moe_adb_silu_kernel(
         ring = ctx.enter_context(tc.tile_pool(name="ring", bufs=3))
         psum = ctx.enter_context(tc.psum_pool(name="psum", bufs=1))
 
-        def cast(eng, dst, src):
-            if eng == "s":
-                nc.scalar.copy(dst, src)
-            elif eng == "v":
-                nc.vector.tensor_copy(dst, src)
-            else:
-                nc.gpsimd.tensor_scalar(dst, src, 1.0, 0.0, ALU.mult, ALU.add)
-
-        def load_plane(plane, scales):
+        def load_scale_rows(plane, scales, r):
             rows = scales[0].rearrange("(q r) n -> r q n", r=4)
-            for r in range(4):
-                nc.sync.dma_start(plane[r:P:32, 0:T].bitcast(I32), rows[r].bitcast(I32))
+            nc.sync.dma_start(plane[r:P:32, 0:T].bitcast(I32), rows[r].bitcast(I32))
 
-        offs_t = keep.tile([P, S // 16], U16, name="offs_t")
+        offs_t = keep.tile([P, S // LIST_COL], U16, name="offs_t")
         nc.sync.dma_start(offs_t[:], offs)
-        dy_w = keep.tile([P, WIN], U32, name="dy_w", align_bytes=64)
+        dy_w = keep.tile([P, WINDOW], U32, name="dy_w", align_bytes=64)
         nc.sync.dma_start(dy_w[:, 0:T].bitcast(I32), dy_words[0].rearrange("p t d -> p (t d)").bitcast(I32))
-        dy_s = keep.tile([P, WIN], U8, name="dy_s", align_bytes=64)
+        dy_s = keep.tile([P, WINDOW], U8, name="dy_s", align_bytes=64)
         nc.vector.memset(dy_s[:].bitcast(I32), 0)
-        if WIN > T:
-            nc.vector.memset(dy_w[:, T:WIN].bitcast(I32), 0)
-        load_plane(dy_s, dy_scales)
+        nc.vector.memset(dy_w[:, T:WINDOW].bitcast(I32), 0)
+        for r in range(4):
+            load_scale_rows(dy_s, dy_scales, r)
 
-        a_rows = a.rearrange("(p t) s -> p t s", t=PACK)
-        a_t, wb_raw, wa_raw, pos_t = {}, {}, {}, []
-        gate_r = keep.tile([P, P], F32, name="gate_r")
+        gate_rows = keep.tile([P, P], F32, name="gate_r")
         ident = keep.tile([P, P], F32, name="ident")
         make_identity(nc, ident[:])
         wt_w = keep.tile([P, 2 * K], U8, name="wt_w", align_bytes=64)
         wt_s = keep.tile([P, K], U8, name="wt_s", align_bytes=64)
         nc.vector.memset(wt_s[:].bitcast(I32), 0)
-        wt_rows = wt_scales[0].rearrange("(q r) n -> r q n", r=4)
 
-        def load_a(e0, ne):
-            at = keep.tile([P, PACK, ne * C], F32, name="a_raw_%d" % e0)
-            nc.sync.dma_start(at[:], a_rows[:, :, e0 * C:(e0 + ne) * C])
-            for e in range(e0, e0 + ne):
-                a_t[e] = at[:, :, (e - e0) * C:(e - e0 + 1) * C]
+        a_rows = a.rearrange("(p t) s -> p t s", t=PACK)
+        a_t, wb_raw = {}, {}
+        for e in range(E):
+            if e < 2 or e % 2 == 0:
+                count = 1 if e < 2 else 2
+                a_tile = keep.tile([P, PACK, count * C], F32, name="a_raw_%d" % e)
+                nc.sync.dma_start(a_tile[:], a_rows[:, :, e * C:(e + count) * C])
+                for j in range(count):
+                    a_t[e + j] = a_tile[:, :, j * C:(j + 1) * C]
+            if e == 0:
+                nc.sync.dma_start(gate_rows[:], gate.rearrange("r (b p) -> (r b) p", p=P)[0:P, :])
+            wb_tile = ring.tile([P, PACK, H], F32, name="wb_raw", bufs=3)
+            nc.sync.dma_start(wb_tile[:], wbt[e].rearrange("(p j) c -> p j c", j=PACK))
+            wb_raw[e] = wb_tile
 
-        def load_wb(e):
-            wb = ring.tile([P, PACK, H], F32, name="wb_raw", bufs=3)
-            nc.sync.dma_start(wb[:], wbt[e].rearrange("(p j) c -> p j c", j=PACK))
-            wb_raw[e] = wb
+        wa_raw, pos_t = {}, []
 
-        def load_wa(e, c0, c1):
-            wa = keep.tile([P, PACK, c1 - c0], F32, name="wa_raw_%d_%d" % (e, c0))
-            nc.sync.dma_start(wa[:], wat[e].rearrange("(p j) c -> p j c", j=PACK)[:, :, c0:c1])
+        def load_list(pos):
+            list_tile = keep.tile([P, T // LIST_COL], U16, name="pos_%d" % len(pos_t))
+            nc.sync.dma_start(list_tile[:], pos)
+            pos_t.append(list_tile)
+
+        small_loads = [lambda r=r: load_scale_rows(wt_s, wt_scales, r) for r in range(4)]
+        small_loads.append(lambda: nc.sync.dma_start(wt_w[:].bitcast(I32), wt_words[0].bitcast(I32)))
+        small_loads.extend(lambda pos=pos: load_list(pos) for pos in (pos1, pos2, pos3))
+        wa_pieces = [(e, 0, K) for e in range(2)]
+        wa_pieces.extend((e, c0, c0 + K // 2) for c0 in (0, K // 2) for e in range(2, E))
+        for i, (e, c0, c1) in enumerate(wa_pieces):
+            wa_tile = keep.tile([P, PACK, c1 - c0], F32, name="wa_raw_%d_%d" % (e, c0))
+            nc.sync.dma_start(wa_tile[:], wat[e].rearrange("(p j) c -> p j c", j=PACK)[:, :, c0:c1])
             for q in range(c0 // P, c1 // P):
-                wa_raw[e, q] = wa[:, :, q * P - c0:(q + 1) * P - c0]
+                wa_raw[e, q] = wa_tile[:, :, q * P - c0:(q + 1) * P - c0]
+            if i < len(small_loads):
+                small_loads[i]()
 
-        def load_gate(c0, c1):
-            nc.sync.dma_start(gate_r[:], gate.rearrange("r (b p) -> (r b) p", p=P)[0:P, :])
+        slot_w = keep.tile([P, S], U32, name="g_w", align_bytes=64)
+        slot_s = keep.tile([P, S], U8, name="g_s", align_bytes=64)
+        for c0 in range(0, S, GATHER):
+            offsets = offs_t[:, c0 // LIST_COL:(c0 + GATHER) // LIST_COL]
+            nc.vector.tensor_copy(slot_w[:, c0:c0 + GATHER], dy_w[:].indirect(offsets))
+            nc.vector.tensor_copy(slot_s[:, c0:c0 + GATHER], dy_s[:].indirect(offsets))
 
-        def load_small(i):
-            if i < 4:
-                nc.sync.dma_start(wt_s[i:P:32, :].bitcast(I32), wt_rows[i].bitcast(I32))
-            elif i == 4:
-                nc.sync.dma_start(wt_w[:].bitcast(I32), wt_words[0].bitcast(I32))
-            else:
-                pt = keep.tile([P, T // 16], U16, name="pos_%d" % (i - 5))
-                nc.sync.dma_start(pt[:], (pos1, pos2, pos3)[i - 5])
-                pos_t.append(pt)
-
-        load_a(0, 1)
-        load_gate(0, 1536)
-        load_wb(0)
-        load_a(1, 1)
-        load_wb(1)
-        load_a(2, 2)
-        load_wb(2)
-        load_wb(3)
-        load_a(4, 2)
-        load_wb(4)
-        load_wb(5)
-        load_wa(0, 0, 512)
-        load_small(0)
-        load_wa(1, 0, 512)
-        load_small(1)
-        load_wa(2, 0, 256)
-        load_small(2)
-        load_wa(3, 0, 256)
-        load_small(3)
-        load_wa(4, 0, 256)
-        load_small(4)
-        load_wa(5, 0, 256)
-        load_small(5)
-        load_wa(2, 256, 512)
-        load_small(6)
-        load_wa(3, 256, 512)
-        load_small(7)
-        load_wa(4, 256, 512)
-        load_wa(5, 256, 512)
-
-        g_w = keep.tile([P, S], U32, name="g_w", align_bytes=64)
-        g_s = keep.tile([P, S], U8, name="g_s", align_bytes=64)
-        for c0 in range(0, S, GN):
-            cols = offs_t[:, c0 // 16:(c0 + GN) // 16]
-            nc.vector.tensor_copy(g_w[:, c0:c0 + GN], dy_w[:].indirect(cols))
-            nc.vector.tensor_copy(g_s[:, c0:c0 + GN], dy_s[:].indirect(cols))
+        gate_ps = psum.tile([P, P], F32, name="s2", bufs=4)
+        nc.tensor.transpose(gate_ps[:], gate_rows[:], ident[:])
+        gate_cols = keep.tile([P, S // P], F32, name="gate_c")
+        nc.vector.tensor_scalar(gate_cols[:], gate_ps[:, 0:S // P], -0.5, None, ALU.mult)
+        gate_banks = []
+        blocks_per_bank = 2 * C // P
+        for u in range(PAIRS):
+            gate_bank = psum.tile([P, 2 * C], F32, name="s2", bufs=4)
+            for j in range(blocks_per_bank):
+                b = u * blocks_per_bank + j
+                nc.tensor.transpose(
+                    gate_bank[:, j * P:(j + 1) * P], gate_cols[:, b:b + 1].to_broadcast([P, P]), ident[:]
+                )
+            gate_banks.append(gate_bank)
 
         dh_w, dh_s = [], []
-        gate_ps = psum.tile([P, P], F32, name="s2", bufs=4)
-        nc.tensor.transpose(gate_ps[:], gate_r[:], ident[:])
-        gate_c = keep.tile([P, S // P], F32, name="gate_c")
-        nc.vector.tensor_scalar(gate_c[:], gate_ps[:, 0:S // P], -0.5, None, ALU.mult)
-        gate_b = []
-        for u in range(E // 2):
-            gb = psum.tile([P, 2 * C], F32, name="s2", bufs=4)
-            for j in range(2 * C // P):
-                b = u * (2 * C // P) + j
-                nc.tensor.transpose(gb[:, j * P:(j + 1) * P], gate_c[:, b:b + 1].to_broadcast([P, P]), ident[:])
-            gate_b.append(gb)
 
-        def hidden(e):
-            silu_n = ring.tile([P, PACK, C], F32, name="silu_n", bufs=3)
-            nc.scalar.activation(silu_n[:], a_t[e], ACT.Silu, scale=-1.0)
-            tanh_h = ring.tile([P, PACK, C], F32, name="tanh_h", bufs=3)
-            nc.scalar.activation(tanh_h[:], a_t[e], ACT.Tanh, scale=0.5)
+        def stage_1(e):
+            silu_neg = ring.tile([P, PACK, C], F32, name="silu_n", bufs=3)
+            nc.scalar.activation(silu_neg[:], a_t[e], ACT.Silu, scale=-1.0)
+            tanh_half = ring.tile([P, PACK, C], F32, name="tanh_h", bufs=3)
+            nc.scalar.activation(tanh_half[:], a_t[e], ACT.Tanh, scale=0.5)
 
             wb_bf = ring.tile([P, 2, 2, P, PACK], BF16, name="wb_bf", align_bytes=64, bufs=2)
-            cast(
-                WB_ENG[e],
-                wb_bf[:].rearrange("p u t m j -> p u m j t"),
-                wb_raw[e][:].rearrange("p j (m u t) -> p u m j t", u=2, t=2),
+            nc.scalar.copy(
+                wb_bf[:].rearrange("p u w m j -> p u m j w"),
+                wb_raw[e][:].rearrange("p j (m u w) -> p u m j w", u=2, w=2),
             )
             wb_w = ring.tile([P, H], U32, name="wb_w", align_bytes=64, bufs=2)
             wb_s = ring.tile([P, H], U8, name="wb_s", align_bytes=64, bufs=2)
-            nc.vector.quantize_mx(wb_w[:].bitcast(FP8X4), wb_s[:], wb_bf[:].rearrange("p u t m j -> p (u t m j)"))
+            nc.vector.quantize_mx(wb_w[:].bitcast(FP8X4), wb_s[:], wb_bf[:].rearrange("p u w m j -> p (u w m j)"))
 
             nc.vector.scalar_tensor_tensor(
-                silu_n[:], silu_n[:], 1.0,
-                gate_b[e // 2][:, (e % 2) * C:(e % 2 + 1) * C].unsqueeze(1).to_broadcast([P, PACK, C]),
+                silu_neg[:], silu_neg[:], 1.0,
+                gate_banks[e // 2][:, (e % 2) * C:(e % 2 + 1) * C].unsqueeze(1).to_broadcast([P, PACK, C]),
                 ALU.subtract, ALU.mult,
             )
-            nc.vector.scalar_tensor_tensor(tanh_h[:], tanh_h[:], 1.0, silu_n[:], ALU.add, ALU.mult)
+            nc.vector.scalar_tensor_tensor(tanh_half[:], tanh_half[:], 1.0, silu_neg[:], ALU.add, ALU.mult)
 
             dh_bf = ring.tile([P, C, PACK], BF16, name="dh_bf", align_bytes=64, bufs=2)
             for h in range(2):
-                sl = slice(h * HALF, (h + 1) * HALF)
-                gl = slice(e * C + h * HALF, e * C + (h + 1) * HALF)
+                own = slice(h * HALF, (h + 1) * HALF)
+                slots = slice(e * C + h * HALF, e * C + (h + 1) * HALF)
                 bank = psum.tile([P, PACK, HALF], F32, name="s1", bufs=4)
                 for t in range(PACK):
                     nc.tensor.matmul_mx(
                         bank[:, t, :],
                         lhsT=wb_w[:, t * P:(t + 1) * P].bitcast(FP8X4), lhsT_scale=wb_s[:, t * P:(t + 1) * P],
-                        rhs=g_w[:, gl].bitcast(FP8X4), rhs_scale=g_s[:, gl],
+                        rhs=slot_w[:, slots].bitcast(FP8X4), rhs_scale=slot_s[:, slots],
                         start=True, stop=True,
                     )
                 nc.vector.tensor_tensor(
-                    dh_bf[:, sl, :].rearrange("p (c i) t -> p c t i", i=2),
+                    dh_bf[:, own, :].rearrange("p (c i) t -> p c t i", i=2),
                     bank[:].rearrange("p t (c i) -> p c t i", i=2),
-                    tanh_h[:, :, sl].rearrange("p t (c i) -> p c t i", i=2),
+                    tanh_half[:, :, own].rearrange("p t (c i) -> p c t i", i=2),
                     ALU.mult,
                 )
-            dw = keep.tile([P, C], U32, name="dh_w_%d" % e, align_bytes=64)
-            ds = keep.tile([P, C], U8, name="dh_s_%d" % e, align_bytes=64)
-            nc.vector.quantize_mx(dw[:].bitcast(FP8X4), ds[:], dh_bf[:].rearrange("p c t -> p (c t)"))
-            dh_w.append(dw)
-            dh_s.append(ds)
+            words = keep.tile([P, C], U32, name="dh_w_%d" % e, align_bytes=64)
+            plane = keep.tile([P, C], U8, name="dh_s_%d" % e, align_bytes=64)
+            nc.vector.quantize_mx(words[:].bitcast(FP8X4), plane[:], dh_bf[:].rearrange("p c t -> p (c t)"))
+            dh_w.append(words)
+            dh_s.append(plane)
 
-        wa_q = {}
+        wa_mx = {}
 
-        def quant_wa(q):
-            for u in range(E // 2):
+        def quantise_wat(q):
+            for u in range(PAIRS):
                 wa_bf = ring.tile([P, 2, P, PACK], BF16, name="wa_bf", align_bytes=64, bufs=8)
                 for v in range(2):
-                    cast(
-                        WA_ENG[3 * q + u],
+                    nc.scalar.copy(
                         wa_bf[:, v, :, :].rearrange("p (c i) j -> p c j i", i=2),
                         wa_raw[2 * u + v, q].rearrange("p j (c i) -> p c j i", i=2),
                     )
-                wa_w = ring.tile([P, 2 * P], U32, name="wa_w", align_bytes=64, bufs=12)
-                wa_s = ring.tile([P, 2 * P], U8, name="wa_s", align_bytes=64, bufs=12)
+                wa_w = ring.tile([P, 2 * P], U32, name="wa_w", align_bytes=64, bufs=K_TILES * PAIRS)
+                wa_s = ring.tile([P, 2 * P], U8, name="wa_s", align_bytes=64, bufs=K_TILES * PAIRS)
                 nc.vector.quantize_mx(wa_w[:].bitcast(FP8X4), wa_s[:], wa_bf[:].rearrange("p v m j -> p (v m j)"))
-                wa_q[q, u] = (wa_w, wa_s)
+                wa_mx[q, u] = (wa_w, wa_s)
 
-        res = {}
+        results = {}
 
-        def slots(q):
-            kc = slice(q * P, (q + 1) * P)
+        def stage_2(q):
             base_ps = psum.tile([P, T], F32, name="s2", bufs=4)
             nc.tensor.matmul_mx(
                 base_ps[:],
-                lhsT=wt_w[:, 2 * q * P:2 * (q + 1) * P].bitcast(FP4X4), lhsT_scale=wt_s[:, kc],
+                lhsT=wt_w[:, 2 * q * P:2 * (q + 1) * P].bitcast(FP4X4), lhsT_scale=wt_s[:, q * P:(q + 1) * P],
                 rhs=dy_w[:, 0:T].bitcast(FP8X4), rhs_scale=dy_s[:, 0:T],
                 start=True, stop=True,
             )
-            base = ring.tile([P, T], F32, name="base", bufs=4)
+            base = ring.tile([P, T], F32, name="base", bufs=K_TILES)
             nc.scalar.copy(base[:], base_ps[:])
             dx = keep.tile([P, S], F32, name="dx_%d" % q)
-            for u in range(E // 2):
-                wa_w, wa_s = wa_q[q, u]
+            for u in range(PAIRS):
+                wa_w, wa_s = wa_mx[q, u]
                 bank = psum.tile([P, 2 * C], F32, name="s2", bufs=4)
                 for v in range(2):
                     e = 2 * u + v
@@ -239,37 +203,32 @@ def tile_moe_adb_silu_kernel(
                         start=True, stop=True,
                     )
                 nc.scalar.copy(dx[:, 2 * u * C:2 * (u + 1) * C], bank[:])
-            res[q] = (base, dx)
+            results[q] = (base, dx)
+
+        token_halves = [slice(h * (T // 2), (h + 1) * (T // 2)) for h in range(2)]
+        list_halves = [slice(h * (T // 2 // LIST_COL), (h + 1) * (T // 2 // LIST_COL)) for h in range(2)]
 
         def combine(q):
-            kc = slice(q * P, (q + 1) * P)
-            base, dx = res[q]
-            acc = [base[:, 0:T // 2], base[:, T // 2:T]]
+            rows = slice(q * P, (q + 1) * P)
+            base, dx = results[q]
+            total = [base[:, cols] for cols in token_halves]
             for r in range(TOP):
                 for h in range(2):
-                    nxt = ring.tile([P, T // 2], F32, name="sum_%d_%d" % (r, h), bufs=1 if r < TOP - 1 else 2)
+                    summed = ring.tile([P, T // 2], F32, name="sum_%d_%d" % (r, h), bufs=1 if r < TOP - 1 else 2)
                     nc.vector.tensor_tensor(
-                        nxt[:], dx[:].indirect(pos_t[r][:, h * 16:(h + 1) * 16]), acc[h], ALU.add
+                        summed[:], dx[:].indirect(pos_t[r][:, list_halves[h]]), total[h], ALU.add
                     )
-                    acc[h] = nxt[:]
+                    total[h] = summed[:]
             for h in range(2):
-                nc.sync.dma_start(out[kc, h * (T // 2):(h + 1) * (T // 2)], acc[h])
+                nc.sync.dma_start(out[rows, token_halves[h]], total[h])
 
-        hidden(0)
-        hidden(1)
-        hidden(2)
-        hidden(3)
-        hidden(4)
-        hidden(5)
-        quant_wa(0)
-        quant_wa(1)
-        slots(0)
-        quant_wa(2)
-        slots(1)
-        combine(0)
-        quant_wa(3)
-        slots(2)
-        combine(1)
-        slots(3)
-        combine(2)
-        combine(3)
+        for e in range(E):
+            stage_1(e)
+        quantise_wat(0)
+        for q in range(K_TILES):
+            if q + 1 < K_TILES:
+                quantise_wat(q + 1)
+            stage_2(q)
+            if q > 0:
+                combine(q - 1)
+        combine(K_TILES - 1)

@@ -24,6 +24,10 @@ LIST_COL = 16
 K_TILES = K // P
 PAIRS = E // 2
 HALF = C // 2
+PIECE = PACK * C
+SHARED = (3, 4, 5)
+SPARE = C
+DX_HOSTS = ("wa_raw_4", "wa_bf_1_2", "a_raw_4", "wa_bf_3_2")
 GATHER = 2 * C
 WINDOW = 704
 
@@ -59,39 +63,30 @@ def tile_moe_adb_silu_kernel(
         nc.vector.memset(wt_s[:].bitcast(I32), 0)
 
         a_rows = a.rearrange("(p t) s -> p t s", t=PACK)
-        a_t, wb_raw = {}, {}
-        for e in range(E):
-            if e < 2 or e % 2 == 0:
-                count = 1 if e < 2 else 2
-                a_tile = keep.tile([P, PACK, count * C], F32, name="a_raw_%d" % e)
-                nc.sync.dma_start(a_tile[:], a_rows[:, :, e * C:(e + count) * C])
-                for j in range(count):
-                    a_t[e + j] = a_tile[:, :, j * C:(j + 1) * C]
-            if e == 0:
-                nc.sync.dma_start(gate_rows[:], gate.rearrange("r (b p) -> (r b) p", p=P)[0:P, :])
-            wb_tile = ring.tile([P, PACK, H], F32, name="wb_raw", bufs=3)
-            nc.sync.dma_start(wb_tile[:], wbt[e].rearrange("(p j) c -> p j c", j=PACK))
-            wb_raw[e] = wb_tile
+        a_t, wb_tiles, wb_raw, spent = {}, {}, {}, []
 
-        wa_raw, pos_t = {}, []
+        def load_a(e, count):
+            a_tile = keep.tile([P, count * PIECE], F32, name="a_raw_%d" % e, align_bytes=64)
+            a_view = a_tile[:].rearrange("p (t s) -> p t s", t=PACK)
+            nc.sync.dma_start(a_view, a_rows[:, :, e * C:(e + count) * C])
+            for j in range(count):
+                a_t[e + j] = a_view[:, :, j * C:(j + 1) * C]
+                spent.append(a_tile[:, j * PIECE:(j + 1) * PIECE])
 
-        def load_list(pos):
-            list_tile = keep.tile([P, T // LIST_COL], U16, name="pos_%d" % len(pos_t))
-            nc.sync.dma_start(list_tile[:], pos)
-            pos_t.append(list_tile)
+        def load_wbt(e):
+            wb_tile = ring.tile([P, PACK * H], F32, name="wide", bufs=E)
+            wb_tiles[e] = wb_tile
+            wb_raw[e] = wb_tile[:].rearrange("p (j c) -> p j c", j=PACK)
+            nc.sync.dma_start(wb_raw[e], wbt[e].rearrange("(p j) c -> p j c", j=PACK))
 
-        small_loads = [lambda r=r: load_scale_rows(wt_s, wt_scales, r) for r in range(4)]
-        small_loads.append(lambda: nc.sync.dma_start(wt_w[:].bitcast(I32), wt_words[0].bitcast(I32)))
-        small_loads.extend(lambda pos=pos: load_list(pos) for pos in (pos1, pos2, pos3))
-        wa_pieces = [(e, 0, K) for e in range(2)]
-        wa_pieces.extend((e, c0, c0 + K // 2) for c0 in (0, K // 2) for e in range(2, E))
-        for i, (e, c0, c1) in enumerate(wa_pieces):
-            wa_tile = keep.tile([P, PACK, c1 - c0], F32, name="wa_raw_%d_%d" % (e, c0))
-            nc.sync.dma_start(wa_tile[:], wat[e].rearrange("(p j) c -> p j c", j=PACK)[:, :, c0:c1])
-            for q in range(c0 // P, c1 // P):
-                wa_raw[e, q] = wa_tile[:, :, q * P - c0:(q + 1) * P - c0]
-            if i < len(small_loads):
-                small_loads[i]()
+        load_a(0, 1)
+        nc.sync.dma_start(gate_rows[:], gate.rearrange("r (b p) -> (r b) p", p=P)[0:P, :])
+        load_wbt(0)
+        load_wbt(1)
+        for e in range(1, E - 1):
+            load_wbt(e + 1)
+            if e == 1 or e % 2 == 0:
+                load_a(e, 1 if e == 1 else 2)
 
         slot_w = keep.tile([P, S], U32, name="g_w", align_bytes=64)
         slot_s = keep.tile([P, S], U8, name="g_s", align_bytes=64)
@@ -103,7 +98,7 @@ def tile_moe_adb_silu_kernel(
         gate_ps = psum.tile([P, P], F32, name="s2", bufs=4)
         nc.tensor.transpose(gate_ps[:], gate_rows[:], ident[:])
         gate_cols = keep.tile([P, S // P], F32, name="gate_c")
-        nc.vector.tensor_scalar(gate_cols[:], gate_ps[:, 0:S // P], -0.5, None, ALU.mult)
+        nc.scalar.mul(gate_cols[:], gate_ps[:, 0:S // P], -0.5)
         gate_banks = []
         blocks_per_bank = 2 * C // P
         for u in range(PAIRS):
@@ -116,30 +111,48 @@ def tile_moe_adb_silu_kernel(
             gate_banks.append(gate_bank)
 
         dh_w, dh_s = [], []
+        wb_bf, wb_mx, factors = {}, {}, {}
 
-        def stage_1(e):
-            silu_neg = ring.tile([P, PACK, C], F32, name="silu_n", bufs=3)
-            nc.scalar.activation(silu_neg[:], a_t[e], ACT.Silu, scale=-1.0)
-            tanh_half = ring.tile([P, PACK, C], F32, name="tanh_h", bufs=3)
-            nc.scalar.activation(tanh_half[:], a_t[e], ACT.Tanh, scale=0.5)
+        def activations(e):
+            pairs = a_t[e].rearrange("p t (c i) -> p c t i", i=2)
+            silu_neg = ring.tile([P, C, PACK], F32, name="silu_n", bufs=4)
+            tanh_half = ring.tile([P, C, PACK], F32, name="tanh_h", bufs=4)
+            calls = [(tanh_half, ACT.Tanh, 0.5), (silu_neg, ACT.Silu, -1.0)]
+            for tile, func, scale in (calls if e > 0 else reversed(calls)):
+                nc.scalar.activation(tile[:].rearrange("p (c i) t -> p c t i", i=2), pairs, func, scale=scale)
+            factors[e] = (silu_neg, tanh_half)
 
-            wb_bf = ring.tile([P, 2, 2, P, PACK], BF16, name="wb_bf", align_bytes=64, bufs=2)
-            nc.scalar.copy(
-                wb_bf[:].rearrange("p u w m j -> p u m j w"),
-                wb_raw[e][:].rearrange("p j (m u w) -> p u m j w", u=2, w=2),
+        def round_wbt_half(e, u, copy):
+            copy(
+                wb_bf[e][:, SPARE:].rearrange("p (u w m j) -> p u m j w", u=2, w=2, j=PACK)[:, u],
+                wb_raw[e].rearrange("p j (m u w) -> p u m j w", u=2, w=2)[:, u],
             )
-            wb_w = ring.tile([P, H], U32, name="wb_w", align_bytes=64, bufs=2)
-            wb_s = ring.tile([P, H], U8, name="wb_s", align_bytes=64, bufs=2)
-            nc.vector.quantize_mx(wb_w[:].bitcast(FP8X4), wb_s[:], wb_bf[:].rearrange("p u w m j -> p (u w m j)"))
 
+        def round_wbt(e):
+            staged = ring.tile([P, SPARE + H * PACK], BF16, name="wb_bf", align_bytes=64, bufs=4)
+            wb_bf[e] = staged
+            round_wbt_half(e, 0, nc.scalar.copy)
+            if e not in SHARED:
+                round_wbt_half(e, 1, nc.scalar.copy)
+
+        def quantise_wbt(e):
+            wb_w = ring.tile([P, H], U32, name="wb_w", align_bytes=64, bufs=3)
+            wb_s = ring.tile([P, H], U8, name="wb_s", align_bytes=64, bufs=3)
+            nc.vector.quantize_mx(wb_w[:].bitcast(FP8X4), wb_s[:], wb_bf[e][:, SPARE:])
+            wb_mx[e] = (wb_w, wb_s)
+
+        def products_from_psum(e):
+            silu_neg, tanh_half = factors[e]
+            wb_w, wb_s = wb_mx[e]
+            host = wb_tiles[0 if e == 0 else e + 1 if e + 1 < E else E - 2]
+            gated = host[:, 0:PIECE].rearrange("p (c t) -> p c t", t=PACK)
+            summed = host[:, PIECE:2 * PIECE].rearrange("p (c t) -> p c t", t=PACK)
+            factors[e] = (host[:, 0:PIECE], host[:, PIECE:2 * PIECE])
             nc.vector.scalar_tensor_tensor(
-                silu_neg[:], silu_neg[:], 1.0,
-                gate_banks[e // 2][:, (e % 2) * C:(e % 2 + 1) * C].unsqueeze(1).to_broadcast([P, PACK, C]),
-                ALU.subtract, ALU.mult,
+                gated, tanh_half[:], 1.0,
+                gate_banks[e // 2][:, (e % 2) * C:(e % 2 + 1) * C].unsqueeze(2).to_broadcast([P, C, PACK]),
+                ALU.add, ALU.mult,
             )
-            nc.vector.scalar_tensor_tensor(tanh_half[:], tanh_half[:], 1.0, silu_neg[:], ALU.add, ALU.mult)
-
-            dh_bf = ring.tile([P, C, PACK], BF16, name="dh_bf", align_bytes=64, bufs=2)
             for h in range(2):
                 own = slice(h * HALF, (h + 1) * HALF)
                 slots = slice(e * C + h * HALF, e * C + (h + 1) * HALF)
@@ -151,32 +164,88 @@ def tile_moe_adb_silu_kernel(
                         rhs=slot_w[:, slots].bitcast(FP8X4), rhs_scale=slot_s[:, slots],
                         start=True, stop=True,
                     )
-                nc.vector.tensor_tensor(
-                    dh_bf[:, own, :].rearrange("p (c i) t -> p c t i", i=2),
-                    bank[:].rearrange("p t (c i) -> p c t i", i=2),
-                    tanh_half[:, :, own].rearrange("p t (c i) -> p c t i", i=2),
-                    ALU.mult,
+                nc.vector.scalar_tensor_tensor(
+                    summed[:, own, :], silu_neg[:, own, :], 1.0, bank[:].rearrange("p t c -> p c t"),
+                    ALU.subtract, ALU.mult,
                 )
+
+        dh_bf = {}
+
+        def round_dh(e, engine, c0, c1):
+            gated, summed = factors[e]
+            engine.tensor_tensor(dh_bf[e][:, c0:c1], gated[:, c0:c1], summed[:, c0:c1], ALU.mult)
+
+        def quantise_dh(e):
             words = keep.tile([P, C], U32, name="dh_w_%d" % e, align_bytes=64)
             plane = keep.tile([P, C], U8, name="dh_s_%d" % e, align_bytes=64)
-            nc.vector.quantize_mx(words[:].bitcast(FP8X4), plane[:], dh_bf[:].rearrange("p c t -> p (c t)"))
+            nc.vector.quantize_mx(words[:].bitcast(FP8X4), plane[:], dh_bf[e])
             dh_w.append(words)
             dh_s.append(plane)
 
-        wa_mx = {}
+        activations(0)
+        for e in range(2):
+            round_wbt(e)
+            quantise_wbt(e)
+        for e in range(E):
+            if e + 2 < E:
+                round_wbt(e + 2)
+            if e + 1 < E:
+                activations(e + 1)
+            products_from_psum(e)
+            if e == E - 1:
+                round_dh(e - 1, nc.vector, 0, SPARE)
+            if e + 1 < E:
+                dh_bf[e] = wb_bf[min(e + 2, E - 1)][:, 0:C * PACK]
+            else:
+                dh_bf[e] = keep.tile([P, C * PACK], BF16, name="dh_last", align_bytes=64)[:]
+            if e != E - 2:
+                round_dh(e, nc.vector, 0, SPARE if e + 1 < E else C * PACK)
+            if e > 0:
+                quantise_dh(e - 1)
+            if e + 2 in SHARED:
+                round_wbt_half(e + 2, 1, nc.vector.tensor_copy)
+            if e + 2 < E:
+                quantise_wbt(e + 2)
+            if e + 1 < E:
+                round_dh(e, nc.gpsimd, SPARE, C * PACK)
 
-        def quantise_wat(q):
-            for u in range(PAIRS):
-                wa_bf = ring.tile([P, 2, P, PACK], BF16, name="wa_bf", align_bytes=64, bufs=8)
+        wa_raw, pos_t = {}, []
+
+        def load_list(pos):
+            list_tile = keep.tile([P, T // LIST_COL], U16, name="pos_%d" % len(pos_t))
+            nc.sync.dma_start(list_tile[:], pos)
+            pos_t.append(list_tile)
+
+        small_loads = [lambda r=r: load_scale_rows(wt_s, wt_scales, r) for r in range(4)]
+        small_loads.append(lambda: nc.sync.dma_start(wt_w[:].bitcast(I32), wt_words[0].bitcast(I32)))
+        small_loads.extend(lambda pos=pos: load_list(pos) for pos in (pos1, pos2, pos3))
+        wa_pieces = [(e, c0, c0 + K // 2) for c0 in (0, K // 2) for e in range(E)]
+        for i, (e, c0, c1) in enumerate(wa_pieces):
+            if i < E and e % 2 == 0:
+                pair_tile = keep.tile([P, 2 * PIECE], F32, name="wa_raw_%d" % e, align_bytes=64)
+            wa_tile = pair_tile[:, e % 2 * PIECE:(e % 2 + 1) * PIECE] if i < E else spent[i - E]
+            wa_view = wa_tile.rearrange("p (j c) -> p j c", j=PACK)
+            nc.sync.dma_start(wa_view, wat[e].rearrange("(p j) c -> p j c", j=PACK)[:, :, c0:c1])
+            for q in range(c0 // P, c1 // P):
+                wa_raw[e, q] = wa_view[:, :, q * P - c0:(q + 1) * P - c0]
+            if i < len(small_loads):
+                small_loads[i]()
+
+        wa_mx, wa_staged = {}, {}
+
+        def quantise_wat(q, pairs, copy):
+            for u in pairs:
+                wa_bf = keep.tile([P, 2, P, PACK], BF16, name="wa_bf_%d_%d" % (q, u), align_bytes=64)
                 for v in range(2):
-                    nc.scalar.copy(
+                    copy(
                         wa_bf[:, v, :, :].rearrange("p (c i) j -> p c j i", i=2),
                         wa_raw[2 * u + v, q].rearrange("p j (c i) -> p c j i", i=2),
                     )
-                wa_w = ring.tile([P, 2 * P], U32, name="wa_w", align_bytes=64, bufs=K_TILES * PAIRS)
-                wa_s = ring.tile([P, 2 * P], U8, name="wa_s", align_bytes=64, bufs=K_TILES * PAIRS)
+                wa_w = keep.tile([P, 2 * P], U32, name="wa_w_%d_%d" % (q, u), align_bytes=64)
+                wa_s = keep.tile([P, 2 * P], U8, name="wa_s_%d_%d" % (q, u), align_bytes=64)
                 nc.vector.quantize_mx(wa_w[:].bitcast(FP8X4), wa_s[:], wa_bf[:].rearrange("p v m j -> p (v m j)"))
                 wa_mx[q, u] = (wa_w, wa_s)
+                wa_staged[q, u] = wa_bf[:].rearrange("p v m j -> p (v m j)").bitcast(F32)
 
         results = {}
 
@@ -188,9 +257,9 @@ def tile_moe_adb_silu_kernel(
                 rhs=dy_w[:, 0:T].bitcast(FP8X4), rhs_scale=dy_s[:, 0:T],
                 start=True, stop=True,
             )
-            base = ring.tile([P, T], F32, name="base", bufs=K_TILES)
-            nc.scalar.copy(base[:], base_ps[:])
-            dx = keep.tile([P, S], F32, name="dx_%d" % q)
+            base = wb_tiles[0][:, q * T:(q + 1) * T]
+            nc.scalar.copy(base, base_ps[:])
+            dx = keep.tile([P, S], F32, name=DX_HOSTS[q], align_bytes=64)
             for u in range(PAIRS):
                 wa_w, wa_s = wa_mx[q, u]
                 bank = psum.tile([P, 2 * C], F32, name="s2", bufs=4)
@@ -214,21 +283,26 @@ def tile_moe_adb_silu_kernel(
             total = [base[:, cols] for cols in token_halves]
             for r in range(TOP):
                 for h in range(2):
-                    summed = ring.tile([P, T // 2], F32, name="sum_%d_%d" % (r, h), bufs=1 if r < TOP - 1 else 2)
-                    nc.vector.tensor_tensor(
-                        summed[:], dx[:].indirect(pos_t[r][:, list_halves[h]]), total[h], ALU.add
-                    )
-                    total[h] = summed[:]
+                    if (q, r) == (1, 1):
+                        summed = wa_staged[2, 2][:, token_halves[h]]
+                    else:
+                        summed = ring.tile([P, T // 2], F32, name="sum_%d_%d" % (r, h), bufs=1 if r < TOP - 1 else 2)[:]
+                    nc.vector.tensor_tensor(summed, dx[:].indirect(pos_t[r][:, list_halves[h]]), total[h], ALU.add)
+                    total[h] = summed
             for h in range(2):
                 nc.sync.dma_start(out[rows, token_halves[h]], total[h])
 
-        for e in range(E):
-            stage_1(e)
-        quantise_wat(0)
-        for q in range(K_TILES):
-            if q + 1 < K_TILES:
-                quantise_wat(q + 1)
-            stage_2(q)
-            if q > 0:
-                combine(q - 1)
-        combine(K_TILES - 1)
+        quantise_wat(0, (0, 1, 2), nc.scalar.copy)
+        quantise_dh(E - 1)
+        quantise_wat(1, (0, 1, 2), nc.scalar.copy)
+        stage_2(0)
+        quantise_wat(2, (0, 1, 2), nc.scalar.copy)
+        quantise_wat(3, (1, 2), nc.vector.tensor_copy)
+        stage_2(1)
+        quantise_wat(3, (0,), nc.scalar.copy)
+        combine(0)
+        stage_2(2)
+        combine(1)
+        stage_2(3)
+        combine(2)
+        combine(3)

@@ -25,11 +25,13 @@ K_TILES = K // P
 PAIRS = E // 2
 HALF = C // 2
 PIECE = PACK * C
-SHARED = (3, 4, 5)
+SHARED = (2, 4)
 SPARE = C
-DX_HOSTS = ("wa_raw_4", "wa_bf_1_2", "a_raw_4", "wa_bf_3_2")
-GATHER = 2 * C
-WINDOW = 704
+DX_HOSTS = ("wa_raw_4", "a_raw_2", "a_raw_4", "wa_bf_2_2")
+STAGE_HOSTS = {(2, 0): (0, 2)}
+PIN_FROM = 0
+SUM_HOSTS = {(1, 0): 1, (1, 1): 2}
+WINDOW = 2048
 
 
 def tile_moe_adb_silu_kernel(
@@ -66,12 +68,12 @@ def tile_moe_adb_silu_kernel(
         a_t, wb_tiles, wb_raw, spent = {}, {}, {}, []
 
         def load_a(e, count):
-            a_tile = keep.tile([P, count * PIECE], F32, name="a_raw_%d" % e, align_bytes=64)
-            a_view = a_tile[:].rearrange("p (t s) -> p t s", t=PACK)
+            if e % 2 == 0:
+                spent.append(keep.tile([P, 2 * PIECE], F32, name="a_raw_%d" % e, align_bytes=64))
+            a_view = spent[e // 2][:, e % 2 * PIECE:(e % 2 + count) * PIECE].rearrange("p (t s) -> p t s", t=PACK)
             nc.sync.dma_start(a_view, a_rows[:, :, e * C:(e + count) * C])
             for j in range(count):
                 a_t[e + j] = a_view[:, :, j * C:(j + 1) * C]
-                spent.append(a_tile[:, j * PIECE:(j + 1) * PIECE])
 
         def load_wbt(e):
             wb_tile = ring.tile([P, PACK * H], F32, name="wide", bufs=E)
@@ -83,17 +85,17 @@ def tile_moe_adb_silu_kernel(
         nc.sync.dma_start(gate_rows[:], gate.rearrange("r (b p) -> (r b) p", p=P)[0:P, :])
         load_wbt(0)
         load_wbt(1)
-        for e in range(1, E - 1):
+        load_a(1, 1)
+        load_wbt(2)
+        for e in range(2, E - 1):
             load_wbt(e + 1)
-            if e == 1 or e % 2 == 0:
-                load_a(e, 1 if e == 1 else 2)
+            if e % 2 == 0:
+                load_a(e, 2)
 
         slot_w = keep.tile([P, S], U32, name="g_w", align_bytes=64)
         slot_s = keep.tile([P, S], U8, name="g_s", align_bytes=64)
-        for c0 in range(0, S, GATHER):
-            offsets = offs_t[:, c0 // LIST_COL:(c0 + GATHER) // LIST_COL]
-            nc.vector.tensor_copy(slot_w[:, c0:c0 + GATHER], dy_w[:].indirect(offsets))
-            nc.vector.tensor_copy(slot_s[:, c0:c0 + GATHER], dy_s[:].indirect(offsets))
+        for slots, window in ((slot_w, dy_w), (slot_s, dy_s)):
+            nc.vector.tensor_copy(slots[:], window[:].indirect(offs_t[:]))
 
         gate_ps = psum.tile([P, P], F32, name="s2", bufs=4)
         nc.tensor.transpose(gate_ps[:], gate_rows[:], ident[:])
@@ -131,9 +133,7 @@ def tile_moe_adb_silu_kernel(
         def round_wbt(e):
             staged = ring.tile([P, SPARE + H * PACK], BF16, name="wb_bf", align_bytes=64, bufs=4)
             wb_bf[e] = staged
-            round_wbt_half(e, 0, nc.scalar.copy)
-            if e not in SHARED:
-                round_wbt_half(e, 1, nc.scalar.copy)
+            round_wbt_half(e, slice(0, 1 if e in SHARED else 2), nc.scalar.copy)
 
         def quantise_wbt(e):
             wb_w = ring.tile([P, H], U32, name="wb_w", align_bytes=64, bufs=3)
@@ -185,6 +185,8 @@ def tile_moe_adb_silu_kernel(
         activations(0)
         for e in range(2):
             round_wbt(e)
+            if e in SHARED:
+                round_wbt_half(e, slice(1, 2), nc.vector.tensor_copy)
             quantise_wbt(e)
         for e in range(E):
             if e + 2 < E:
@@ -203,7 +205,7 @@ def tile_moe_adb_silu_kernel(
             if e > 0:
                 quantise_dh(e - 1)
             if e + 2 in SHARED:
-                round_wbt_half(e + 2, 1, nc.vector.tensor_copy)
+                round_wbt_half(e + 2, slice(1, 2), nc.vector.tensor_copy)
             if e + 2 < E:
                 quantise_wbt(e + 2)
             if e + 1 < E:
@@ -219,33 +221,42 @@ def tile_moe_adb_silu_kernel(
         small_loads = [lambda r=r: load_scale_rows(wt_s, wt_scales, r) for r in range(4)]
         small_loads.append(lambda: nc.sync.dma_start(wt_w[:].bitcast(I32), wt_words[0].bitcast(I32)))
         small_loads.extend(lambda pos=pos: load_list(pos) for pos in (pos1, pos2, pos3))
-        wa_pieces = [(e, c0, c0 + K // 2) for c0 in (0, K // 2) for e in range(E)]
-        for i, (e, c0, c1) in enumerate(wa_pieces):
-            if i < E and e % 2 == 0:
-                pair_tile = keep.tile([P, 2 * PIECE], F32, name="wa_raw_%d" % e, align_bytes=64)
-            wa_tile = pair_tile[:, e % 2 * PIECE:(e % 2 + 1) * PIECE] if i < E else spent[i - E]
-            wa_view = wa_tile.rearrange("p (j c) -> p j c", j=PACK)
-            nc.sync.dma_start(wa_view, wat[e].rearrange("(p j) c -> p j c", j=PACK)[:, :, c0:c1])
-            for q in range(c0 // P, c1 // P):
-                wa_raw[e, q] = wa_view[:, :, q * P - c0:(q + 1) * P - c0]
+        wa_pieces = [(e, 0, 2) for e in range(2)]
+        wa_pieces.extend((e, half, 1) for half in range(2) for e in range(2, E))
+        for i, (e, half, halves) in enumerate(wa_pieces):
+            if e == 0 or (half == 1 and e % 2 == 0):
+                host = spent[e // 2]
+            elif e == 1 or e % 2 == 0:
+                host = keep.tile([P, 2 * PIECE], F32, name="wa_raw_%d" % e, align_bytes=64)
+            first = 0 if halves == 2 else e % 2 * PIECE
+            piece = host[:, first:first + halves * PIECE].rearrange("p (j c) -> p j c", j=PACK)
+            columns = slice(half * (K // 2), (half + halves) * (K // 2))
+            nc.sync.dma_start(piece, wat[e].rearrange("(p j) c -> p j c", j=PACK)[:, :, columns])
+            for j in range(halves):
+                wa_raw[half + j, e] = piece[:, :, j * (K // 2):(j + 1) * (K // 2)]
             if i < len(small_loads):
                 small_loads[i]()
 
         wa_mx, wa_staged = {}, {}
 
-        def quantise_wat(q, pairs, copy):
-            for u in pairs:
-                wa_bf = keep.tile([P, 2, P, PACK], BF16, name="wa_bf_%d_%d" % (q, u), align_bytes=64)
-                for v in range(2):
-                    copy(
-                        wa_bf[:, v, :, :].rearrange("p (c i) j -> p c j i", i=2),
-                        wa_raw[2 * u + v, q].rearrange("p j (c i) -> p c j i", i=2),
-                    )
-                wa_w = keep.tile([P, 2 * P], U32, name="wa_w_%d_%d" % (q, u), align_bytes=64)
-                wa_s = keep.tile([P, 2 * P], U8, name="wa_s_%d_%d" % (q, u), align_bytes=64)
-                nc.vector.quantize_mx(wa_w[:].bitcast(FP8X4), wa_s[:], wa_bf[:].rearrange("p v m j -> p (v m j)"))
-                wa_mx[q, u] = (wa_w, wa_s)
-                wa_staged[q, u] = wa_bf[:].rearrange("p v m j -> p (v m j)").bitcast(F32)
+        def quantise_wat(q0, tiles, u, copy):
+            half, width = q0 // 2, tiles * P
+            columns = slice(q0 % 2 * P, q0 % 2 * P + width)
+            wa_bf = keep.tile([P, 2, width, PACK], BF16, name="wa_bf_%d_%d" % STAGE_HOSTS.get((q0, u), (q0, u)), align_bytes=64)
+            for v in range(2):
+                copy(
+                    wa_bf[:, v, :, :].rearrange("p (c i) j -> p c j i", i=2),
+                    wa_raw[half, 2 * u + v][:, :, columns].rearrange("p j (c i) -> p c j i", i=2),
+                )
+            wa_w = keep.tile([P, 2 * width], U32, name="wa_w_%d_%d" % (q0, u), align_bytes=64)
+            wa_s = keep.tile([P, 2 * width], U8, name="wa_s_%d_%d" % (q0, u), align_bytes=64)
+            staged = wa_bf[:].rearrange("p v m j -> p (v m j)")
+            nc.vector.quantize_mx(wa_w[:].bitcast(FP8X4), wa_s[:], staged)
+            for v in range(2):
+                for j in range(tiles):
+                    own = slice(v * width + j * P, v * width + (j + 1) * P)
+                    wa_mx[q0 + j, 2 * u + v] = (wa_w[:, own], wa_s[:, own])
+            wa_staged[q0, u] = staged.bitcast(F32)
 
         results = {}
 
@@ -261,13 +272,13 @@ def tile_moe_adb_silu_kernel(
             nc.scalar.copy(base, base_ps[:])
             dx = keep.tile([P, S], F32, name=DX_HOSTS[q], align_bytes=64)
             for u in range(PAIRS):
-                wa_w, wa_s = wa_mx[q, u]
                 bank = psum.tile([P, 2 * C], F32, name="s2", bufs=4)
                 for v in range(2):
                     e = 2 * u + v
+                    wa_w, wa_s = wa_mx[q, e]
                     nc.tensor.matmul_mx(
                         bank[:, v * C:(v + 1) * C],
-                        lhsT=wa_w[:, v * P:(v + 1) * P].bitcast(FP8X4), lhsT_scale=wa_s[:, v * P:(v + 1) * P],
+                        lhsT=wa_w.bitcast(FP8X4), lhsT_scale=wa_s,
                         rhs=dh_w[e][:].bitcast(FP8X4), rhs_scale=dh_s[e][:],
                         start=True, stop=True,
                     )
@@ -283,8 +294,8 @@ def tile_moe_adb_silu_kernel(
             total = [base[:, cols] for cols in token_halves]
             for r in range(TOP):
                 for h in range(2):
-                    if (q, r) == (1, 1):
-                        summed = wa_staged[2, 2][:, token_halves[h]]
+                    if h >= PIN_FROM and (q, r) in SUM_HOSTS:
+                        summed = wa_staged[2, SUM_HOSTS[q, r]][:, token_halves[h]]
                     else:
                         summed = ring.tile([P, T // 2], F32, name="sum_%d_%d" % (r, h), bufs=1 if r < TOP - 1 else 2)[:]
                     nc.vector.tensor_tensor(summed, dx[:].indirect(pos_t[r][:, list_halves[h]]), total[h], ALU.add)
@@ -292,14 +303,15 @@ def tile_moe_adb_silu_kernel(
             for h in range(2):
                 nc.sync.dma_start(out[rows, token_halves[h]], total[h])
 
-        quantise_wat(0, (0, 1, 2), nc.scalar.copy)
         quantise_dh(E - 1)
-        quantise_wat(1, (0, 1, 2), nc.scalar.copy)
+        for q in range(2):
+            for u in range(PAIRS):
+                quantise_wat(q, 1, u, nc.scalar.copy)
+        quantise_wat(2, 2, 0, nc.vector.tensor_copy)
         stage_2(0)
-        quantise_wat(2, (0, 1, 2), nc.scalar.copy)
-        quantise_wat(3, (1, 2), nc.vector.tensor_copy)
+        quantise_wat(2, 2, 1, nc.scalar.copy)
         stage_2(1)
-        quantise_wat(3, (0,), nc.scalar.copy)
+        quantise_wat(2, 2, 2, nc.scalar.copy)
         combine(0)
         stage_2(2)
         combine(1)

@@ -21,17 +21,13 @@ ACT = mybir.ActivationFunctionType
 P = 128
 PACK = 4
 LIST_COL = 16
-K_TILES = K // P
 PAIRS = E // 2
+LAST_PAIR = PAIRS - 1
 HALF = C // 2
 PIECE = PACK * C
-SHARED = (2, 4)
-SPARE = C
-DX_HOSTS = ("wa_raw_4", "a_raw_2", "a_raw_4", "wa_bf_2_2")
-STAGE_HOSTS = {(2, 0): (0, 2)}
-PIN_FROM = 0
-SUM_HOSTS = {(1, 0): 1, (1, 1): 2}
 WINDOW = 2048
+VECTOR_DH = PIECE // 4
+SHARED = (2, 4)
 
 
 def tile_moe_adb_silu_kernel(
@@ -40,8 +36,8 @@ def tile_moe_adb_silu_kernel(
     nc = tc.nc
     with ExitStack() as ctx:
         keep = ctx.enter_context(tc.tile_pool(name="keep", bufs=1))
-        ring = ctx.enter_context(tc.tile_pool(name="ring", bufs=3))
-        psum = ctx.enter_context(tc.psum_pool(name="psum", bufs=1))
+        ring = ctx.enter_context(tc.tile_pool(name="ring", bufs=4))
+        psum = ctx.enter_context(tc.psum_pool(name="psum", bufs=4))
 
         def load_scale_rows(plane, scales, r):
             rows = scales[0].rearrange("(q r) n -> r q n", r=4)
@@ -65,21 +61,21 @@ def tile_moe_adb_silu_kernel(
         nc.vector.memset(wt_s[:].bitcast(I32), 0)
 
         a_rows = a.rearrange("(p t) s -> p t s", t=PACK)
-        a_t, wb_tiles, wb_raw, spent = {}, {}, {}, []
+        a_tiles, a_t, wb_tiles = [], {}, {}
 
         def load_a(e, count):
             if e % 2 == 0:
-                spent.append(keep.tile([P, 2 * PIECE], F32, name="a_raw_%d" % e, align_bytes=64))
-            a_view = spent[e // 2][:, e % 2 * PIECE:(e % 2 + count) * PIECE].rearrange("p (t s) -> p t s", t=PACK)
-            nc.sync.dma_start(a_view, a_rows[:, :, e * C:(e + count) * C])
+                a_tiles.append(keep.tile([P, 2 * PIECE], F32, name="a_raw_%d" % e, align_bytes=64))
+            view = a_tiles[e // 2][:, e % 2 * PIECE:(e % 2 + count) * PIECE].rearrange("p (t s) -> p t s", t=PACK)
+            nc.sync.dma_start(view, a_rows[:, :, e * C:(e + count) * C])
             for j in range(count):
-                a_t[e + j] = a_view[:, :, j * C:(j + 1) * C]
+                a_t[e + j] = view[:, :, j * C:(j + 1) * C]
 
         def load_wbt(e):
-            wb_tile = ring.tile([P, PACK * H], F32, name="wide", bufs=E)
-            wb_tiles[e] = wb_tile
-            wb_raw[e] = wb_tile[:].rearrange("p (j c) -> p j c", j=PACK)
-            nc.sync.dma_start(wb_raw[e], wbt[e].rearrange("(p j) c -> p j c", j=PACK))
+            wb_tiles[e] = ring.tile([P, PACK * H], F32, name="wide", bufs=E)
+            nc.sync.dma_start(
+                wb_tiles[e][:].rearrange("p (j c) -> p j c", j=PACK), wbt[e].rearrange("(p j) c -> p j c", j=PACK)
+            )
 
         load_a(0, 1)
         nc.sync.dma_start(gate_rows[:], gate.rearrange("r (b p) -> (r b) p", p=P)[0:P, :])
@@ -94,17 +90,17 @@ def tile_moe_adb_silu_kernel(
 
         slot_w = keep.tile([P, S], U32, name="g_w", align_bytes=64)
         slot_s = keep.tile([P, S], U8, name="g_s", align_bytes=64)
-        for slots, window in ((slot_w, dy_w), (slot_s, dy_s)):
-            nc.vector.tensor_copy(slots[:], window[:].indirect(offs_t[:]))
+        nc.vector.tensor_copy(slot_w[:], dy_w[:].indirect(offs_t[:]))
+        nc.vector.tensor_copy(slot_s[:], dy_s[:].indirect(offs_t[:]))
 
-        gate_ps = psum.tile([P, P], F32, name="s2", bufs=4)
+        gate_ps = psum.tile([P, P], F32, name="s2")
         nc.tensor.transpose(gate_ps[:], gate_rows[:], ident[:])
         gate_cols = keep.tile([P, S // P], F32, name="gate_c")
         nc.scalar.mul(gate_cols[:], gate_ps[:, 0:S // P], -0.5)
         gate_banks = []
         blocks_per_bank = 2 * C // P
         for u in range(PAIRS):
-            gate_bank = psum.tile([P, 2 * C], F32, name="s2", bufs=4)
+            gate_bank = psum.tile([P, 2 * C], F32, name="s2")
             for j in range(blocks_per_bank):
                 b = u * blocks_per_bank + j
                 nc.tensor.transpose(
@@ -112,51 +108,46 @@ def tile_moe_adb_silu_kernel(
                 )
             gate_banks.append(gate_bank)
 
-        dh_w, dh_s = [], []
-        wb_bf, wb_mx, factors = {}, {}, {}
+        activated, wb_bf, wb_mx, brackets, dh_bf, dh_mx = {}, {}, {}, {}, {}, {}
 
         def activations(e):
             pairs = a_t[e].rearrange("p t (c i) -> p c t i", i=2)
-            silu_neg = ring.tile([P, C, PACK], F32, name="silu_n", bufs=4)
-            tanh_half = ring.tile([P, C, PACK], F32, name="tanh_h", bufs=4)
+            silu_neg = ring.tile([P, C, PACK], F32, name="silu_n")
+            tanh_half = ring.tile([P, C, PACK], F32, name="tanh_h")
             calls = [(tanh_half, ACT.Tanh, 0.5), (silu_neg, ACT.Silu, -1.0)]
-            for tile, func, scale in (calls if e > 0 else reversed(calls)):
-                nc.scalar.activation(tile[:].rearrange("p (c i) t -> p c t i", i=2), pairs, func, scale=scale)
-            factors[e] = (silu_neg, tanh_half)
+            for target, func, scale in (calls if e > 0 else reversed(calls)):
+                nc.scalar.activation(target[:].rearrange("p (c i) t -> p c t i", i=2), pairs, func, scale=scale)
+            activated[e] = (silu_neg, tanh_half)
 
-        def round_wbt_half(e, u, copy):
+        def round_wbt(e, groups, copy):
             copy(
-                wb_bf[e][:, SPARE:].rearrange("p (u w m j) -> p u m j w", u=2, w=2, j=PACK)[:, u],
-                wb_raw[e].rearrange("p j (m u w) -> p u m j w", u=2, w=2)[:, u],
+                wb_bf[e][:, VECTOR_DH:].rearrange("p (u w m j) -> p u m j w", u=2, w=2, j=PACK)[:, groups],
+                wb_tiles[e][:].rearrange("p (j m u w) -> p u m j w", j=PACK, u=2, w=2)[:, groups],
             )
 
-        def round_wbt(e):
-            staged = ring.tile([P, SPARE + H * PACK], BF16, name="wb_bf", align_bytes=64, bufs=4)
-            wb_bf[e] = staged
-            round_wbt_half(e, slice(0, 1 if e in SHARED else 2), nc.scalar.copy)
+        def round_wbt_on_scalar(e):
+            wb_bf[e] = ring.tile([P, VECTOR_DH + PACK * H], BF16, name="wb_bf", align_bytes=64)
+            round_wbt(e, slice(0, 1 if e in SHARED else 2), nc.scalar.copy)
 
         def quantise_wbt(e):
             wb_w = ring.tile([P, H], U32, name="wb_w", align_bytes=64, bufs=3)
             wb_s = ring.tile([P, H], U8, name="wb_s", align_bytes=64, bufs=3)
-            nc.vector.quantize_mx(wb_w[:].bitcast(FP8X4), wb_s[:], wb_bf[e][:, SPARE:])
+            nc.vector.quantize_mx(wb_w[:].bitcast(FP8X4), wb_s[:], wb_bf[e][:, VECTOR_DH:])
             wb_mx[e] = (wb_w, wb_s)
 
-        def products_from_psum(e):
-            silu_neg, tanh_half = factors[e]
+        def make_brackets(e, spent):
+            silu_neg, tanh_half = activated[e]
             wb_w, wb_s = wb_mx[e]
-            host = wb_tiles[0 if e == 0 else e + 1 if e + 1 < E else E - 2]
-            gated = host[:, 0:PIECE].rearrange("p (c t) -> p c t", t=PACK)
-            summed = host[:, PIECE:2 * PIECE].rearrange("p (c t) -> p c t", t=PACK)
-            factors[e] = (host[:, 0:PIECE], host[:, PIECE:2 * PIECE])
+            gated, summed = spent[:, 0:PIECE], spent[:, PIECE:2 * PIECE]
             nc.vector.scalar_tensor_tensor(
-                gated, tanh_half[:], 1.0,
+                gated.rearrange("p (c t) -> p c t", t=PACK), tanh_half[:], 1.0,
                 gate_banks[e // 2][:, (e % 2) * C:(e % 2 + 1) * C].unsqueeze(2).to_broadcast([P, C, PACK]),
                 ALU.add, ALU.mult,
             )
             for h in range(2):
                 own = slice(h * HALF, (h + 1) * HALF)
                 slots = slice(e * C + h * HALF, e * C + (h + 1) * HALF)
-                bank = psum.tile([P, PACK, HALF], F32, name="s1", bufs=4)
+                bank = psum.tile([P, PACK, HALF], F32, name="s1")
                 for t in range(PACK):
                     nc.tensor.matmul_mx(
                         bank[:, t, :],
@@ -165,51 +156,48 @@ def tile_moe_adb_silu_kernel(
                         start=True, stop=True,
                     )
                 nc.vector.scalar_tensor_tensor(
-                    summed[:, own, :], silu_neg[:, own, :], 1.0, bank[:].rearrange("p t c -> p c t"),
-                    ALU.subtract, ALU.mult,
+                    summed.rearrange("p (c t) -> p c t", t=PACK)[:, own, :], silu_neg[:, own, :], 1.0,
+                    bank[:].rearrange("p t c -> p c t"), ALU.subtract, ALU.mult,
                 )
-
-        dh_bf = {}
+            brackets[e] = (gated, summed)
 
         def round_dh(e, engine, c0, c1):
-            gated, summed = factors[e]
+            gated, summed = brackets[e]
             engine.tensor_tensor(dh_bf[e][:, c0:c1], gated[:, c0:c1], summed[:, c0:c1], ALU.mult)
 
         def quantise_dh(e):
             words = keep.tile([P, C], U32, name="dh_w_%d" % e, align_bytes=64)
             plane = keep.tile([P, C], U8, name="dh_s_%d" % e, align_bytes=64)
             nc.vector.quantize_mx(words[:].bitcast(FP8X4), plane[:], dh_bf[e])
-            dh_w.append(words)
-            dh_s.append(plane)
+            dh_mx[e] = (words, plane)
 
         activations(0)
         for e in range(2):
-            round_wbt(e)
-            if e in SHARED:
-                round_wbt_half(e, slice(1, 2), nc.vector.tensor_copy)
+            round_wbt_on_scalar(e)
             quantise_wbt(e)
-        for e in range(E):
-            if e + 2 < E:
-                round_wbt(e + 2)
-            if e + 1 < E:
-                activations(e + 1)
-            products_from_psum(e)
-            if e == E - 1:
-                round_dh(e - 1, nc.vector, 0, SPARE)
-            if e + 1 < E:
-                dh_bf[e] = wb_bf[min(e + 2, E - 1)][:, 0:C * PACK]
-            else:
-                dh_bf[e] = keep.tile([P, C * PACK], BF16, name="dh_last", align_bytes=64)[:]
-            if e != E - 2:
-                round_dh(e, nc.vector, 0, SPARE if e + 1 < E else C * PACK)
+        for e in range(E - 2):
+            round_wbt_on_scalar(e + 2)
+            activations(e + 1)
+            make_brackets(e, wb_tiles[e + 1 if e > 0 else 0])
+            dh_bf[e] = wb_bf[e + 2][:, 0:PIECE]
+            round_dh(e, nc.vector, 0, VECTOR_DH)
+            if e + 2 in SHARED:
+                round_wbt(e + 2, slice(1, 2), nc.vector.tensor_copy)
             if e > 0:
                 quantise_dh(e - 1)
-            if e + 2 in SHARED:
-                round_wbt_half(e + 2, slice(1, 2), nc.vector.tensor_copy)
-            if e + 2 < E:
-                quantise_wbt(e + 2)
-            if e + 1 < E:
-                round_dh(e, nc.gpsimd, SPARE, C * PACK)
+            quantise_wbt(e + 2)
+            round_dh(e, nc.gpsimd, VECTOR_DH, PIECE)
+        before, last = E - 2, E - 1
+        activations(last)
+        make_brackets(before, wb_tiles[last])
+        dh_bf[before] = dh_bf[before - 1]
+        quantise_dh(before - 1)
+        round_dh(before, nc.gpsimd, VECTOR_DH, PIECE)
+        make_brackets(last, wb_tiles[before])
+        round_dh(before, nc.vector, 0, VECTOR_DH)
+        dh_bf[last] = keep.tile([P, PIECE], BF16, name="dh_last", align_bytes=64)[:]
+        round_dh(last, nc.vector, 0, PIECE)
+        quantise_dh(before)
 
         wa_raw, pos_t = {}, []
 
@@ -225,7 +213,7 @@ def tile_moe_adb_silu_kernel(
         wa_pieces.extend((e, half, 1) for half in range(2) for e in range(2, E))
         for i, (e, half, halves) in enumerate(wa_pieces):
             if e == 0 or (half == 1 and e % 2 == 0):
-                host = spent[e // 2]
+                host = a_tiles[e // 2]
             elif e == 1 or e % 2 == 0:
                 host = keep.tile([P, 2 * PIECE], F32, name="wa_raw_%d" % e, align_bytes=64)
             first = 0 if halves == 2 else e % 2 * PIECE
@@ -237,31 +225,29 @@ def tile_moe_adb_silu_kernel(
             if i < len(small_loads):
                 small_loads[i]()
 
-        wa_mx, wa_staged = {}, {}
+        wa_mx = {}
 
-        def quantise_wat(q0, tiles, u, copy):
-            half, width = q0 // 2, tiles * P
+        def quantise_wat(q0, tiles, u, copy, tag):
+            width = tiles * P
             columns = slice(q0 % 2 * P, q0 % 2 * P + width)
-            wa_bf = keep.tile([P, 2, width, PACK], BF16, name="wa_bf_%d_%d" % STAGE_HOSTS.get((q0, u), (q0, u)), align_bytes=64)
+            wa_bf = keep.tile([P, 2, width, PACK], BF16, name=tag, align_bytes=64)
             for v in range(2):
                 copy(
                     wa_bf[:, v, :, :].rearrange("p (c i) j -> p c j i", i=2),
-                    wa_raw[half, 2 * u + v][:, :, columns].rearrange("p j (c i) -> p c j i", i=2),
+                    wa_raw[q0 // 2, 2 * u + v][:, :, columns].rearrange("p j (c i) -> p c j i", i=2),
                 )
             wa_w = keep.tile([P, 2 * width], U32, name="wa_w_%d_%d" % (q0, u), align_bytes=64)
             wa_s = keep.tile([P, 2 * width], U8, name="wa_s_%d_%d" % (q0, u), align_bytes=64)
-            staged = wa_bf[:].rearrange("p v m j -> p (v m j)")
-            nc.vector.quantize_mx(wa_w[:].bitcast(FP8X4), wa_s[:], staged)
+            nc.vector.quantize_mx(wa_w[:].bitcast(FP8X4), wa_s[:], wa_bf[:].rearrange("p v m j -> p (v m j)"))
             for v in range(2):
                 for j in range(tiles):
                     own = slice(v * width + j * P, v * width + (j + 1) * P)
                     wa_mx[q0 + j, 2 * u + v] = (wa_w[:, own], wa_s[:, own])
-            wa_staged[q0, u] = staged.bitcast(F32)
 
         results = {}
 
-        def stage_2(q):
-            base_ps = psum.tile([P, T], F32, name="s2", bufs=4)
+        def stage_2(q, tag):
+            base_ps = psum.tile([P, T], F32, name="s2")
             nc.tensor.matmul_mx(
                 base_ps[:],
                 lhsT=wt_w[:, 2 * q * P:2 * (q + 1) * P].bitcast(FP4X4), lhsT_scale=wt_s[:, q * P:(q + 1) * P],
@@ -270,16 +256,16 @@ def tile_moe_adb_silu_kernel(
             )
             base = wb_tiles[0][:, q * T:(q + 1) * T]
             nc.scalar.copy(base, base_ps[:])
-            dx = keep.tile([P, S], F32, name=DX_HOSTS[q], align_bytes=64)
+            dx = keep.tile([P, S], F32, name=tag, align_bytes=64)
             for u in range(PAIRS):
-                bank = psum.tile([P, 2 * C], F32, name="s2", bufs=4)
+                bank = psum.tile([P, 2 * C], F32, name="s2")
                 for v in range(2):
-                    e = 2 * u + v
-                    wa_w, wa_s = wa_mx[q, e]
+                    wa_w, wa_s = wa_mx[q, 2 * u + v]
+                    words, plane = dh_mx[2 * u + v]
                     nc.tensor.matmul_mx(
                         bank[:, v * C:(v + 1) * C],
                         lhsT=wa_w.bitcast(FP8X4), lhsT_scale=wa_s,
-                        rhs=dh_w[e][:].bitcast(FP8X4), rhs_scale=dh_s[e][:],
+                        rhs=words[:].bitcast(FP8X4), rhs_scale=plane[:],
                         start=True, stop=True,
                     )
                 nc.scalar.copy(dx[:, 2 * u * C:2 * (u + 1) * C], bank[:])
@@ -288,33 +274,33 @@ def tile_moe_adb_silu_kernel(
         token_halves = [slice(h * (T // 2), (h + 1) * (T // 2)) for h in range(2)]
         list_halves = [slice(h * (T // 2 // LIST_COL), (h + 1) * (T // 2 // LIST_COL)) for h in range(2)]
 
-        def combine(q):
-            rows = slice(q * P, (q + 1) * P)
+        def combine(q, middle=None):
             base, dx = results[q]
             total = [base[:, cols] for cols in token_halves]
             for r in range(TOP):
                 for h in range(2):
-                    if h >= PIN_FROM and (q, r) in SUM_HOSTS:
-                        summed = wa_staged[2, SUM_HOSTS[q, r]][:, token_halves[h]]
+                    if r == 1 and middle is not None:
+                        sums = middle[:, token_halves[h]]
                     else:
-                        summed = ring.tile([P, T // 2], F32, name="sum_%d_%d" % (r, h), bufs=1 if r < TOP - 1 else 2)[:]
-                    nc.vector.tensor_tensor(summed, dx[:].indirect(pos_t[r][:, list_halves[h]]), total[h], ALU.add)
-                    total[h] = summed
+                        sums = ring.tile([P, T // 2], F32, name="sum_%d_%d" % (r, h), bufs=1 if r < TOP - 1 else 2)[:]
+                    nc.vector.tensor_tensor(sums, dx[:].indirect(pos_t[r][:, list_halves[h]]), total[h], ALU.add)
+                    total[h] = sums
             for h in range(2):
-                nc.sync.dma_start(out[rows, token_halves[h]], total[h])
+                nc.sync.dma_start(out[q * P:(q + 1) * P, token_halves[h]], total[h])
 
-        quantise_dh(E - 1)
+        quantise_dh(last)
+        for u in range(LAST_PAIR):
+            quantise_wat(0, 2, u, nc.scalar.copy, "wa_bf_0_%d" % u)
         for q in range(2):
-            for u in range(PAIRS):
-                quantise_wat(q, 1, u, nc.scalar.copy)
-        quantise_wat(2, 2, 0, nc.vector.tensor_copy)
-        stage_2(0)
-        quantise_wat(2, 2, 1, nc.scalar.copy)
-        stage_2(1)
-        quantise_wat(2, 2, 2, nc.scalar.copy)
+            quantise_wat(q, 1, LAST_PAIR, nc.scalar.copy, "wa_bf_%d_2" % q)
+        quantise_wat(2, 2, 0, nc.vector.tensor_copy, "wa_bf_0_2")
+        stage_2(0, "wa_raw_4")
+        quantise_wat(2, 2, 1, nc.scalar.copy, "wa_bf_2_1")
+        stage_2(1, "a_raw_2")
+        quantise_wat(2, 2, LAST_PAIR, nc.scalar.copy, "wa_bf_2_2")
         combine(0)
-        stage_2(2)
-        combine(1)
-        stage_2(3)
+        stage_2(2, "wa_bf_2_2")
+        combine(1, a_tiles[LAST_PAIR][:, PIECE:PIECE + T])
+        stage_2(3, "a_raw_4")
         combine(2)
         combine(3)

@@ -112,8 +112,8 @@ def tile_moe_adb_silu_kernel(
 
         def activations(e):
             pairs = a_t[e].rearrange("p t (c i) -> p c t i", i=2)
-            silu_neg = ring.tile([P, C, PACK], F32, name="silu_n")
-            tanh_half = ring.tile([P, C, PACK], F32, name="tanh_h")
+            silu_neg = ring.tile([P, C, PACK], F32, name="silu_n", bufs=3)
+            tanh_half = ring.tile([P, C, PACK], F32, name="tanh_h", bufs=3)
             calls = [(tanh_half, ACT.Tanh, 0.5), (silu_neg, ACT.Silu, -1.0)]
             for target, func, scale in (calls if e > 0 else reversed(calls)):
                 nc.scalar.activation(target[:].rearrange("p (c i) t -> p c t i", i=2), pairs, func, scale=scale)
@@ -199,7 +199,7 @@ def tile_moe_adb_silu_kernel(
         round_dh(last, nc.vector, 0, PIECE)
         quantise_dh(before)
 
-        wa_raw, pos_t = {}, []
+        wa_raw, pos_t = [[] for e in range(E)], []
 
         def load_list(pos):
             list_tile = keep.tile([P, T // LIST_COL], U16, name="pos_%d" % len(pos_t))
@@ -209,19 +209,19 @@ def tile_moe_adb_silu_kernel(
         small_loads = [lambda r=r: load_scale_rows(wt_s, wt_scales, r) for r in range(4)]
         small_loads.append(lambda: nc.sync.dma_start(wt_w[:].bitcast(I32), wt_words[0].bitcast(I32)))
         small_loads.extend(lambda pos=pos: load_list(pos) for pos in (pos1, pos2, pos3))
-        wa_pieces = [(e, 0, 2) for e in range(2)]
-        wa_pieces.extend((e, half, 1) for half in range(2) for e in range(2, E))
-        for i, (e, half, halves) in enumerate(wa_pieces):
-            if e == 0 or (half == 1 and e % 2 == 0):
+        wa_pieces = [(e, 0, 4) for e in range(2)]
+        wa_pieces.extend((e, 0, 2) for e in range(2, E))
+        wa_pieces.extend((e, 2, 2) for e in range(2, last))
+        wa_pieces.extend((last, q, 1) for q in (2, 3))
+        for i, (e, q0, tiles) in enumerate(wa_pieces):
+            if e == 0 or (q0 == 2 and e % 2 == 0):
                 host = a_tiles[e // 2]
             elif e == 1 or e % 2 == 0:
                 host = keep.tile([P, 2 * PIECE], F32, name="wa_raw_%d" % e, align_bytes=64)
-            first = 0 if halves == 2 else e % 2 * PIECE
-            piece = host[:, first:first + halves * PIECE].rearrange("p (j c) -> p j c", j=PACK)
-            columns = slice(half * (K // 2), (half + halves) * (K // 2))
-            nc.sync.dma_start(piece, wat[e].rearrange("(p j) c -> p j c", j=PACK)[:, :, columns])
-            for j in range(halves):
-                wa_raw[half + j, e] = piece[:, :, j * (K // 2):(j + 1) * (K // 2)]
+            first = 0 if tiles == 4 else e % 2 * PIECE + q0 % 2 * PACK * P
+            piece = host[:, first:first + tiles * PACK * P].rearrange("p (j c) -> p j c", j=PACK)
+            nc.sync.dma_start(piece, wat[e].rearrange("(p j) c -> p j c", j=PACK)[:, :, q0 * P:(q0 + tiles) * P])
+            wa_raw[e].append((q0, tiles, piece))
             if i < len(small_loads):
                 small_loads[i]()
 
@@ -229,12 +229,12 @@ def tile_moe_adb_silu_kernel(
 
         def quantise_wat(q0, tiles, u, copy, tag):
             width = tiles * P
-            columns = slice(q0 % 2 * P, q0 % 2 * P + width)
             wa_bf = keep.tile([P, 2, width, PACK], BF16, name=tag, align_bytes=64)
             for v in range(2):
+                start, piece = [(first, x) for first, count, x in wa_raw[2 * u + v] if first <= q0 < first + count][0]
                 copy(
                     wa_bf[:, v, :, :].rearrange("p (c i) j -> p c j i", i=2),
-                    wa_raw[q0 // 2, 2 * u + v][:, :, columns].rearrange("p j (c i) -> p c j i", i=2),
+                    piece[:, :, (q0 - start) * P:(q0 - start) * P + width].rearrange("p j (c i) -> p c j i", i=2),
                 )
             wa_w = keep.tile([P, 2 * width], U32, name="wa_w_%d_%d" % (q0, u), align_bytes=64)
             wa_s = keep.tile([P, 2 * width], U8, name="wa_s_%d_%d" % (q0, u), align_bytes=64)
@@ -295,12 +295,14 @@ def tile_moe_adb_silu_kernel(
             quantise_wat(q, 1, LAST_PAIR, nc.scalar.copy, "wa_bf_%d_2" % q)
         quantise_wat(2, 2, 0, nc.vector.tensor_copy, "wa_bf_0_2")
         stage_2(0, "wa_raw_4")
-        quantise_wat(2, 2, 1, nc.scalar.copy, "wa_bf_2_1")
-        stage_2(1, "a_raw_2")
-        quantise_wat(2, 2, LAST_PAIR, nc.scalar.copy, "wa_bf_2_2")
+        quantise_wat(2, 1, 1, nc.scalar.copy, "wa_bf_2_1")
+        stage_2(1, "wa_bf_1_2")
+        quantise_wat(2, 1, LAST_PAIR, nc.scalar.copy, "wa_bf_2_2")
         combine(0)
         stage_2(2, "wa_bf_2_2")
+        quantise_wat(3, 1, 1, nc.scalar.copy, "wa_bf_3_1")
+        quantise_wat(3, 1, LAST_PAIR, nc.scalar.copy, "wa_bf_3_2")
         combine(1, a_tiles[LAST_PAIR][:, PIECE:PIECE + T])
-        stage_2(3, "a_raw_4")
-        combine(2)
+        stage_2(3, "wa_bf_3_2")
+        combine(2, a_tiles[LAST_PAIR][:, PIECE + T:PIECE + 2 * T])
         combine(3)

@@ -26,8 +26,8 @@ LAST_PAIR = PAIRS - 1
 HALF = C // 2
 PIECE = PACK * C
 WINDOW = 2048
-VECTOR_DH = PIECE // 4
-SHARED = (2, 4)
+VECTOR_DH = 3 * PIECE // 16
+SHARED = (2, 4, 5)
 
 
 def tile_moe_adb_silu_kernel(
@@ -81,8 +81,8 @@ def tile_moe_adb_silu_kernel(
         nc.sync.dma_start(gate_rows[:], gate.rearrange("r (b p) -> (r b) p", p=P)[0:P, :])
         load_wbt(0)
         load_wbt(1)
-        load_a(1, 1)
         load_wbt(2)
+        load_a(1, 1)
         for e in range(2, E - 1):
             load_wbt(e + 1)
             if e % 2 == 0:

@@ -26,8 +26,8 @@ LAST_PAIR = PAIRS - 1
 HALF = C // 2
 PIECE = PACK * C
 WINDOW = 2048
-VECTOR_DH = 3 * PIECE // 16
-SHARED = (2, 4, 5)
+SHARED = (3, 4, 5)
+GPSIMD_COLS = 72
 
 
 def tile_moe_adb_silu_kernel(
@@ -80,13 +80,12 @@ def tile_moe_adb_silu_kernel(
         load_a(0, 1)
         nc.sync.dma_start(gate_rows[:], gate.rearrange("r (b p) -> (r b) p", p=P)[0:P, :])
         load_wbt(0)
-        load_wbt(1)
-        load_wbt(2)
         load_a(1, 1)
-        for e in range(2, E - 1):
-            load_wbt(e + 1)
+        load_wbt(1)
+        for e in range(2, E):
             if e % 2 == 0:
                 load_a(e, 2)
+            load_wbt(e)
 
         slot_w = keep.tile([P, S], U32, name="g_w", align_bytes=64)
         slot_s = keep.tile([P, S], U8, name="g_s", align_bytes=64)
@@ -108,37 +107,36 @@ def tile_moe_adb_silu_kernel(
                 )
             gate_banks.append(gate_bank)
 
-        activated, wb_bf, wb_mx, brackets, dh_bf, dh_mx = {}, {}, {}, {}, {}, {}
+        activated, wb_bf, wb_mx, brackets, dh_mx = {}, {}, {}, {}, {}
 
         def activations(e):
             pairs = a_t[e].rearrange("p t (c i) -> p c t i", i=2)
             silu_neg = ring.tile([P, C, PACK], F32, name="silu_n", bufs=3)
-            tanh_half = ring.tile([P, C, PACK], F32, name="tanh_h", bufs=3)
-            calls = [(tanh_half, ACT.Tanh, 0.5), (silu_neg, ACT.Silu, -1.0)]
-            for target, func, scale in (calls if e > 0 else reversed(calls)):
+            tanh_half = keep.tile([P, C, PACK], F32, name="tanh_h_%d" % e, align_bytes=64)
+            for target, func, scale in ((silu_neg, ACT.Silu, -1.0), (tanh_half, ACT.Tanh, 0.5)):
                 nc.scalar.activation(target[:].rearrange("p (c i) t -> p c t i", i=2), pairs, func, scale=scale)
             activated[e] = (silu_neg, tanh_half)
 
-        def round_wbt(e, groups, copy):
+        def round_wbt(e, groups, cols, copy):
             copy(
-                wb_bf[e][:, VECTOR_DH:].rearrange("p (u w m j) -> p u m j w", u=2, w=2, j=PACK)[:, groups],
-                wb_tiles[e][:].rearrange("p (j m u w) -> p u m j w", j=PACK, u=2, w=2)[:, groups],
+                wb_bf[e][:].rearrange("p (u w m j) -> p u m j w", u=2, w=2, j=PACK)[:, groups, cols],
+                wb_tiles[e][:].rearrange("p (j m u w) -> p u m j w", j=PACK, u=2, w=2)[:, groups, cols],
             )
 
         def round_wbt_on_scalar(e):
-            wb_bf[e] = ring.tile([P, VECTOR_DH + PACK * H], BF16, name="wb_bf", align_bytes=64)
-            round_wbt(e, slice(0, 1 if e in SHARED else 2), nc.scalar.copy)
+            wb_bf[e] = keep.tile([P, PACK * H], BF16, name="wb_bf_%d" % (max(e - 1, 0) % 3), align_bytes=64)
+            round_wbt(e, slice(0, 1 if e in SHARED else 2), slice(GPSIMD_COLS if e == 1 else 0, P), nc.scalar.copy)
 
         def quantise_wbt(e):
-            wb_w = ring.tile([P, H], U32, name="wb_w", align_bytes=64, bufs=3)
-            wb_s = ring.tile([P, H], U8, name="wb_s", align_bytes=64, bufs=3)
-            nc.vector.quantize_mx(wb_w[:].bitcast(FP8X4), wb_s[:], wb_bf[e][:, VECTOR_DH:])
+            wb_w = ring.tile([P, H], U32, name="wb_w", align_bytes=64, bufs=2)
+            wb_s = ring.tile([P, H], U8, name="wb_s", align_bytes=64, bufs=2)
+            nc.vector.quantize_mx(wb_w[:].bitcast(FP8X4), wb_s[:], wb_bf[e][:])
             wb_mx[e] = (wb_w, wb_s)
 
-        def make_brackets(e, spent):
+        def make_brackets(e):
             silu_neg, tanh_half = activated[e]
             wb_w, wb_s = wb_mx[e]
-            gated, summed = spent[:, 0:PIECE], spent[:, PIECE:2 * PIECE]
+            gated, summed = wb_tiles[e][:, 0:PIECE], wb_tiles[e][:, PIECE:2 * PIECE]
             nc.vector.scalar_tensor_tensor(
                 gated.rearrange("p (c t) -> p c t", t=PACK), tanh_half[:], 1.0,
                 gate_banks[e // 2][:, (e % 2) * C:(e % 2 + 1) * C].unsqueeze(2).to_broadcast([P, C, PACK]),
@@ -161,43 +159,38 @@ def tile_moe_adb_silu_kernel(
                 )
             brackets[e] = (gated, summed)
 
-        def round_dh(e, engine, c0, c1):
+        def round_dh(e, engine, dh_bf):
             gated, summed = brackets[e]
-            engine.tensor_tensor(dh_bf[e][:, c0:c1], gated[:, c0:c1], summed[:, c0:c1], ALU.mult)
+            engine.tensor_tensor(dh_bf[:], gated, summed, ALU.mult)
 
-        def quantise_dh(e):
-            words = keep.tile([P, C], U32, name="dh_w_%d" % e, align_bytes=64)
+        def quantise_dh(e, dh_bf):
+            words = keep.tile([P, C], U32, name="tanh_h_%d" % ((e + 1) % E), align_bytes=64)
             plane = keep.tile([P, C], U8, name="dh_s_%d" % e, align_bytes=64)
-            nc.vector.quantize_mx(words[:].bitcast(FP8X4), plane[:], dh_bf[e])
+            nc.vector.quantize_mx(words[:].bitcast(FP8X4), plane[:], dh_bf[:])
             dh_mx[e] = (words, plane)
 
-        activations(0)
-        for e in range(2):
-            round_wbt_on_scalar(e)
-            quantise_wbt(e)
-        for e in range(E - 2):
-            round_wbt_on_scalar(e + 2)
-            activations(e + 1)
-            make_brackets(e, wb_tiles[e + 1 if e > 0 else 0])
-            dh_bf[e] = wb_bf[e + 2][:, 0:PIECE]
-            round_dh(e, nc.vector, 0, VECTOR_DH)
-            if e + 2 in SHARED:
-                round_wbt(e + 2, slice(1, 2), nc.vector.tensor_copy)
-            if e > 0:
-                quantise_dh(e - 1)
-            quantise_wbt(e + 2)
-            round_dh(e, nc.gpsimd, VECTOR_DH, PIECE)
+        dh_shared = keep.tile([P, PIECE], BF16, name="dh_bf", align_bytes=64)
+        dh_last = keep.tile([P, PIECE], BF16, name="dh_last", align_bytes=64)
         before, last = E - 2, E - 1
-        activations(last)
-        make_brackets(before, wb_tiles[last])
-        dh_bf[before] = dh_bf[before - 1]
-        quantise_dh(before - 1)
-        round_dh(before, nc.gpsimd, VECTOR_DH, PIECE)
-        make_brackets(last, wb_tiles[before])
-        round_dh(before, nc.vector, 0, VECTOR_DH)
-        dh_bf[last] = keep.tile([P, PIECE], BF16, name="dh_last", align_bytes=64)[:]
-        round_dh(last, nc.vector, 0, PIECE)
-        quantise_dh(before)
+        for e in range(E):
+            activations(e)
+            round_wbt_on_scalar(e)
+            if e == 1:
+                nc.gpsimd.tensor_scalar(
+                    wb_bf[e][:].rearrange("p (t m j) -> p m t j", t=PACK, j=PACK)[:, 0:GPSIMD_COLS],
+                    wb_tiles[e][:].rearrange("p (j m t) -> p m t j", t=PACK, j=PACK)[:, 0:GPSIMD_COLS],
+                    1.0, 0.0, ALU.mult, ALU.add,
+                )
+            if e in SHARED:
+                round_wbt(e, slice(1, 2), slice(0, P), nc.vector.tensor_copy)
+            if e > 1:
+                quantise_dh(e - 2, dh_shared)
+            quantise_wbt(e)
+            if e > 0:
+                round_dh(e - 1, nc.gpsimd, dh_shared)
+            make_brackets(e)
+        quantise_dh(before, dh_shared)
+        round_dh(last, nc.vector, dh_last)
 
         wa_raw, pos_t = [[] for e in range(E)], []
 
@@ -288,9 +281,10 @@ def tile_moe_adb_silu_kernel(
             for h in range(2):
                 nc.sync.dma_start(out[q * P:(q + 1) * P, token_halves[h]], total[h])
 
-        quantise_dh(last)
         for u in range(LAST_PAIR):
             quantise_wat(0, 2, u, nc.scalar.copy, "wa_bf_0_%d" % u)
+            if u == 0:
+                quantise_dh(last, dh_last)
         for q in range(2):
             quantise_wat(q, 1, LAST_PAIR, nc.scalar.copy, "wa_bf_%d_2" % q)
         quantise_wat(2, 2, 0, nc.vector.tensor_copy, "wa_bf_0_2")

@@ -212,9 +212,13 @@ def tile_moe_adb_silu_kernel(
             elif e == 1 or e % 2 == 0:
                 host = keep.tile([P, 2 * PIECE], F32, name="wa_raw_%d" % e, align_bytes=64)
             first = 0 if tiles == 4 else e % 2 * PIECE + q0 % 2 * PACK * P
+            if (e, q0) == (last, 2):
+                shared_host, host, first = host, keep.tile([P, PACK * P], F32, name="wa_quarter", align_bytes=64), 0
             piece = host[:, first:first + tiles * PACK * P].rearrange("p (j c) -> p j c", j=PACK)
             nc.sync.dma_start(piece, wat[e].rearrange("(p j) c -> p j c", j=PACK)[:, :, q0 * P:(q0 + tiles) * P])
             wa_raw[e].append((q0, tiles, piece))
+            if (e, q0) == (last, 2):
+                host = shared_host
             if i < len(small_loads):
                 small_loads[i]()
 
@@ -237,18 +241,23 @@ def tile_moe_adb_silu_kernel(
                     own = slice(v * width + j * P, v * width + (j + 1) * P)
                     wa_mx[q0 + j, 2 * u + v] = (wa_w[:, own], wa_s[:, own])
 
+        token_halves = [slice(h * (T // 2), (h + 1) * (T // 2)) for h in range(2)]
+        list_halves = [slice(h * (T // 2 // LIST_COL), (h + 1) * (T // 2 // LIST_COL)) for h in range(2)]
         results = {}
 
-        def stage_2(q, tag):
-            base_ps = psum.tile([P, T], F32, name="s2")
+        def room(q, i, h):
+            return wb_tiles[q + i // PACK][:, i % PACK * T:(i % PACK + 1) * T][:, token_halves[h]]
+
+        def stage_2(q, tag, fetch):
+            base_ps = psum.tile([P, T], F32, name="s1" if fetch else "s2")
             nc.tensor.matmul_mx(
                 base_ps[:],
                 lhsT=wt_w[:, 2 * q * P:2 * (q + 1) * P].bitcast(FP4X4), lhsT_scale=wt_s[:, q * P:(q + 1) * P],
                 rhs=dy_w[:, 0:T].bitcast(FP8X4), rhs_scale=dy_s[:, 0:T],
                 start=True, stop=True,
             )
-            base = wb_tiles[0][:, q * T:(q + 1) * T]
-            nc.scalar.copy(base, base_ps[:])
+            if fetch == 0:
+                nc.scalar.copy(wb_tiles[q][:, 0:T], base_ps[:])
             dx = keep.tile([P, S], F32, name=tag, align_bytes=64)
             for u in range(PAIRS):
                 bank = psum.tile([P, 2 * C], F32, name="s2")
@@ -262,24 +271,23 @@ def tile_moe_adb_silu_kernel(
                         start=True, stop=True,
                     )
                 nc.scalar.copy(dx[:, 2 * u * C:2 * (u + 1) * C], bank[:])
-            results[q] = (base, dx)
-
-        token_halves = [slice(h * (T // 2), (h + 1) * (T // 2)) for h in range(2)]
-        list_halves = [slice(h * (T // 2 // LIST_COL), (h + 1) * (T // 2 // LIST_COL)) for h in range(2)]
-
-        def combine(q, middle=None):
-            base, dx = results[q]
-            total = [base[:, cols] for cols in token_halves]
-            for r in range(TOP):
+            for r in range(fetch):
                 for h in range(2):
-                    if r == 1 and middle is not None:
-                        sums = middle[:, token_halves[h]]
-                    else:
-                        sums = ring.tile([P, T // 2], F32, name="sum_%d_%d" % (r, h), bufs=1 if r < TOP - 1 else 2)[:]
-                    nc.vector.tensor_tensor(sums, dx[:].indirect(pos_t[r][:, list_halves[h]]), total[h], ALU.add)
-                    total[h] = sums
+                    nc.scalar.activation(
+                        room(q, PACK * r, h), dx[:].indirect(pos_t[r][:, list_halves[h]]), ACT.Copy
+                    )
+            results[q] = (base_ps, dx, fetch)
+
+        def combine(q):
+            base_ps, dx, fetch = results[q]
+            for i in range(TOP):
+                for h in range(2):
+                    terms = [dx[:].indirect(pos_t[r][:, list_halves[h]]) for r in range(fetch, TOP)]
+                    terms.append(base_ps[:, token_halves[h]])
+                    terms.extend(room(q, PACK * r, h) for r in range(1, fetch))
+                    nc.vector.tensor_tensor(room(q, i + 1, h), terms[i], room(q, i, h), ALU.add)
             for h in range(2):
-                nc.sync.dma_start(out[q * P:(q + 1) * P, token_halves[h]], total[h])
+                nc.sync.dma_start(out[q * P:(q + 1) * P, token_halves[h]], room(q, TOP, h))
 
         for u in range(LAST_PAIR):
             quantise_wat(0, 2, u, nc.scalar.copy, "wa_bf_0_%d" % u)
@@ -288,15 +296,14 @@ def tile_moe_adb_silu_kernel(
         for q in range(2):
             quantise_wat(q, 1, LAST_PAIR, nc.scalar.copy, "wa_bf_%d_2" % q)
         quantise_wat(2, 2, 0, nc.vector.tensor_copy, "wa_bf_0_2")
-        stage_2(0, "wa_raw_4")
-        quantise_wat(2, 1, 1, nc.scalar.copy, "wa_bf_2_1")
-        stage_2(1, "wa_bf_1_2")
+        stage_2(0, "wa_raw_4", 0)
+        quantise_wat(2, 2, 1, nc.vector.tensor_copy, "wa_bf_2_1")
         quantise_wat(2, 1, LAST_PAIR, nc.scalar.copy, "wa_bf_2_2")
         combine(0)
-        stage_2(2, "wa_bf_2_2")
-        quantise_wat(3, 1, 1, nc.scalar.copy, "wa_bf_3_1")
+        stage_2(1, "wa_quarter", 1)
         quantise_wat(3, 1, LAST_PAIR, nc.scalar.copy, "wa_bf_3_2")
-        combine(1, a_tiles[LAST_PAIR][:, PIECE:PIECE + T])
-        stage_2(3, "wa_bf_3_2")
-        combine(2, a_tiles[LAST_PAIR][:, PIECE + T:PIECE + 2 * T])
+        combine(1)
+        stage_2(2, "a_raw_4", 1)
+        stage_2(3, "wa_bf_3_2", 2)
+        combine(2)
         combine(3)

@@ -37,7 +37,7 @@ def tile_moe_adb_silu_kernel(
     with ExitStack() as ctx:
         keep = ctx.enter_context(tc.tile_pool(name="keep", bufs=1))
         ring = ctx.enter_context(tc.tile_pool(name="ring", bufs=4))
-        psum = ctx.enter_context(tc.psum_pool(name="psum", bufs=4))
+        psum = ctx.enter_context(tc.psum_pool(name="psum", bufs=8))
 
         def load_scale_rows(plane, scales, r):
             rows = scales[0].rearrange("(q r) n -> r q n", r=4)
@@ -50,8 +50,6 @@ def tile_moe_adb_silu_kernel(
         dy_s = keep.tile([P, WINDOW], U8, name="dy_s", align_bytes=64)
         nc.vector.memset(dy_s[:].bitcast(I32), 0)
         nc.vector.memset(dy_w[:, T:WINDOW].bitcast(I32), 0)
-        for r in range(4):
-            load_scale_rows(dy_s, dy_scales, r)
 
         gate_rows = keep.tile([P, P], F32, name="gate_r")
         ident = keep.tile([P, P], F32, name="ident")
@@ -78,6 +76,8 @@ def tile_moe_adb_silu_kernel(
             )
 
         load_a(0, 1)
+        for r in range(4):
+            load_scale_rows(dy_s, dy_scales, r)
         nc.sync.dma_start(gate_rows[:], gate.rearrange("r (b p) -> (r b) p", p=P)[0:P, :])
         load_wbt(0)
         load_a(1, 1)
@@ -92,14 +92,15 @@ def tile_moe_adb_silu_kernel(
         nc.vector.tensor_copy(slot_w[:], dy_w[:].indirect(offs_t[:]))
         nc.vector.tensor_copy(slot_s[:], dy_s[:].indirect(offs_t[:]))
 
-        gate_ps = psum.tile([P, P], F32, name="s2")
+        gate_ps = psum.tile([P, P], F32, name="bank")
         nc.tensor.transpose(gate_ps[:], gate_rows[:], ident[:])
         gate_cols = keep.tile([P, S // P], F32, name="gate_c")
         nc.scalar.mul(gate_cols[:], gate_ps[:, 0:S // P], -0.5)
         gate_banks = []
         blocks_per_bank = 2 * C // P
-        for u in range(PAIRS):
-            gate_bank = psum.tile([P, 2 * C], F32, name="s2")
+
+        def spread_gates(u):
+            gate_bank = psum.tile([P, 2 * C], F32, name="bank")
             for j in range(blocks_per_bank):
                 b = u * blocks_per_bank + j
                 nc.tensor.transpose(
@@ -111,7 +112,7 @@ def tile_moe_adb_silu_kernel(
 
         def activations(e):
             pairs = a_t[e].rearrange("p t (c i) -> p c t i", i=2)
-            silu_neg = ring.tile([P, C, PACK], F32, name="silu_n", bufs=3)
+            silu_neg = ring.tile([P, C, PACK], F32, name="silu_n", bufs=4)
             tanh_half = keep.tile([P, C, PACK], F32, name="tanh_h_%d" % e, align_bytes=64)
             for target, func, scale in ((silu_neg, ACT.Silu, -1.0), (tanh_half, ACT.Tanh, 0.5)):
                 nc.scalar.activation(target[:].rearrange("p (c i) t -> p c t i", i=2), pairs, func, scale=scale)
@@ -145,7 +146,7 @@ def tile_moe_adb_silu_kernel(
             for h in range(2):
                 own = slice(h * HALF, (h + 1) * HALF)
                 slots = slice(e * C + h * HALF, e * C + (h + 1) * HALF)
-                bank = psum.tile([P, PACK, HALF], F32, name="s1")
+                bank = psum.tile([P, PACK, HALF], F32, name="bank")
                 for t in range(PACK):
                     nc.tensor.matmul_mx(
                         bank[:, t, :],
@@ -173,6 +174,8 @@ def tile_moe_adb_silu_kernel(
         dh_last = keep.tile([P, PIECE], BF16, name="dh_last", align_bytes=64)
         before, last = E - 2, E - 1
         for e in range(E):
+            if e % 2 == 0:
+                spread_gates(e // 2)
             activations(e)
             round_wbt_on_scalar(e)
             if e == 1:
@@ -212,13 +215,9 @@ def tile_moe_adb_silu_kernel(
             elif e == 1 or e % 2 == 0:
                 host = keep.tile([P, 2 * PIECE], F32, name="wa_raw_%d" % e, align_bytes=64)
             first = 0 if tiles == 4 else e % 2 * PIECE + q0 % 2 * PACK * P
-            if (e, q0) == (last, 2):
-                shared_host, host, first = host, keep.tile([P, PACK * P], F32, name="wa_quarter", align_bytes=64), 0
             piece = host[:, first:first + tiles * PACK * P].rearrange("p (j c) -> p j c", j=PACK)
             nc.sync.dma_start(piece, wat[e].rearrange("(p j) c -> p j c", j=PACK)[:, :, q0 * P:(q0 + tiles) * P])
             wa_raw[e].append((q0, tiles, piece))
-            if (e, q0) == (last, 2):
-                host = shared_host
             if i < len(small_loads):
                 small_loads[i]()
 
@@ -246,21 +245,14 @@ def tile_moe_adb_silu_kernel(
         results = {}
 
         def room(q, i, h):
-            return wb_tiles[q + i // PACK][:, i % PACK * T:(i % PACK + 1) * T][:, token_halves[h]]
+            if i == PACK:
+                return wb_tiles[PACK][:, q * T:(q + 1) * T][:, token_halves[h]]
+            return wb_tiles[q][:, i * T:(i + 1) * T][:, token_halves[h]]
 
         def stage_2(q, tag, fetch):
-            base_ps = psum.tile([P, T], F32, name="s1" if fetch else "s2")
-            nc.tensor.matmul_mx(
-                base_ps[:],
-                lhsT=wt_w[:, 2 * q * P:2 * (q + 1) * P].bitcast(FP4X4), lhsT_scale=wt_s[:, q * P:(q + 1) * P],
-                rhs=dy_w[:, 0:T].bitcast(FP8X4), rhs_scale=dy_s[:, 0:T],
-                start=True, stop=True,
-            )
-            if fetch == 0:
-                nc.scalar.copy(wb_tiles[q][:, 0:T], base_ps[:])
             dx = keep.tile([P, S], F32, name=tag, align_bytes=64)
             for u in range(PAIRS):
-                bank = psum.tile([P, 2 * C], F32, name="s2")
+                bank = psum.tile([P, 2 * C], F32, name="bank")
                 for v in range(2):
                     wa_w, wa_s = wa_mx[q, 2 * u + v]
                     words, plane = dh_mx[2 * u + v]
@@ -271,20 +263,30 @@ def tile_moe_adb_silu_kernel(
                         start=True, stop=True,
                     )
                 nc.scalar.copy(dx[:, 2 * u * C:2 * (u + 1) * C], bank[:])
-            for r in range(fetch):
+            if q in (1, 2):
+                nc.scalar.activation(wb_tiles[q][:, 0:T], dx[:].indirect(pos_t[0][:]), ACT.Copy)
+            for r in range(1 if q in (1, 2) else 0, 2):
                 for h in range(2):
-                    nc.scalar.activation(
-                        room(q, PACK * r, h), dx[:].indirect(pos_t[r][:, list_halves[h]]), ACT.Copy
-                    )
-            results[q] = (base_ps, dx, fetch)
+                    if r < fetch[h]:
+                        nc.scalar.activation(
+                            room(q, PACK * r, h), dx[:].indirect(pos_t[r][:, list_halves[h]]), ACT.Copy
+                        )
+            results[q] = (dx, fetch)
 
         def combine(q):
-            base_ps, dx, fetch = results[q]
+            dx, fetch = results[q]
+            base_ps = psum.tile([P, T], F32, name="bank")
+            nc.tensor.matmul_mx(
+                base_ps[:],
+                lhsT=wt_w[:, 2 * q * P:2 * (q + 1) * P].bitcast(FP4X4), lhsT_scale=wt_s[:, q * P:(q + 1) * P],
+                rhs=dy_w[:, 0:T].bitcast(FP8X4), rhs_scale=dy_s[:, 0:T],
+                start=True, stop=True,
+            )
             for i in range(TOP):
                 for h in range(2):
-                    terms = [dx[:].indirect(pos_t[r][:, list_halves[h]]) for r in range(fetch, TOP)]
+                    terms = [dx[:].indirect(pos_t[r][:, list_halves[h]]) for r in range(fetch[h], TOP)]
                     terms.append(base_ps[:, token_halves[h]])
-                    terms.extend(room(q, PACK * r, h) for r in range(1, fetch))
+                    terms.extend(room(q, PACK * r, h) for r in range(1, fetch[h]))
                     nc.vector.tensor_tensor(room(q, i + 1, h), terms[i], room(q, i, h), ALU.add)
             for h in range(2):
                 nc.sync.dma_start(out[q * P:(q + 1) * P, token_halves[h]], room(q, TOP, h))
@@ -296,14 +298,14 @@ def tile_moe_adb_silu_kernel(
         for q in range(2):
             quantise_wat(q, 1, LAST_PAIR, nc.scalar.copy, "wa_bf_%d_2" % q)
         quantise_wat(2, 2, 0, nc.vector.tensor_copy, "wa_bf_0_2")
-        stage_2(0, "wa_raw_4", 0)
+        stage_2(0, "wa_raw_4", (1, 1))
         quantise_wat(2, 2, 1, nc.vector.tensor_copy, "wa_bf_2_1")
-        quantise_wat(2, 1, LAST_PAIR, nc.scalar.copy, "wa_bf_2_2")
+        quantise_wat(2, 1, LAST_PAIR, nc.vector.tensor_copy, "wa_bf_2_2")
+        stage_2(1, "wa_bf_1_2", (1, 1))
         combine(0)
-        stage_2(1, "wa_quarter", 1)
         quantise_wat(3, 1, LAST_PAIR, nc.scalar.copy, "wa_bf_3_2")
+        stage_2(2, "a_raw_4", (1, 2))
         combine(1)
-        stage_2(2, "a_raw_4", 1)
-        stage_2(3, "wa_bf_3_2", 2)
+        stage_2(3, "wa_bf_3_2", (2, 2))
         combine(2)
         combine(3)

@@ -70,7 +70,7 @@ def tile_moe_adb_silu_kernel(
                 a_t[e + j] = view[:, :, j * C:(j + 1) * C]
 
         def load_wbt(e):
-            wb_tiles[e] = ring.tile([P, PACK * H], F32, name="wide", bufs=E)
+            wb_tiles[e] = ring.tile([P, PACK * H], F32, name="wide", bufs=E, align_bytes=64)
             nc.sync.dma_start(
                 wb_tiles[e][:].rearrange("p (j c) -> p j c", j=PACK), wbt[e].rearrange("(p j) c -> p j c", j=PACK)
             )
@@ -223,18 +223,20 @@ def tile_moe_adb_silu_kernel(
 
         wa_mx = {}
 
-        def quantise_wat(q0, tiles, u, copy, tag):
+        def quantise_wat(q0, tiles, u, copy, tag, place=None):
             width = tiles * P
-            wa_bf = keep.tile([P, 2, width, PACK], BF16, name=tag, align_bytes=64)
+            if place is None:
+                place = keep.tile([P, 2 * width * PACK], BF16, name=tag, align_bytes=64)[:]
+            wa_bf = place.rearrange("p (v m j) -> p v m j", v=2, j=PACK)
             for v in range(2):
                 start, piece = [(first, x) for first, count, x in wa_raw[2 * u + v] if first <= q0 < first + count][0]
                 copy(
-                    wa_bf[:, v, :, :].rearrange("p (c i) j -> p c j i", i=2),
-                    piece[:, :, (q0 - start) * P:(q0 - start) * P + width].rearrange("p j (c i) -> p c j i", i=2),
+                    wa_bf[:, v, :, :].rearrange("p (c i) j -> p c j i", i=PACK),
+                    piece[:, :, (q0 - start) * P:(q0 - start) * P + width].rearrange("p j (c i) -> p c j i", i=PACK),
                 )
             wa_w = keep.tile([P, 2 * width], U32, name="wa_w_%d_%d" % (q0, u), align_bytes=64)
             wa_s = keep.tile([P, 2 * width], U8, name="wa_s_%d_%d" % (q0, u), align_bytes=64)
-            nc.vector.quantize_mx(wa_w[:].bitcast(FP8X4), wa_s[:], wa_bf[:].rearrange("p v m j -> p (v m j)"))
+            nc.vector.quantize_mx(wa_w[:].bitcast(FP8X4), wa_s[:], place)
             for v in range(2):
                 for j in range(tiles):
                     own = slice(v * width + j * P, v * width + (j + 1) * P)
@@ -273,7 +275,7 @@ def tile_moe_adb_silu_kernel(
                         )
             results[q] = (dx, fetch)
 
-        def combine(q):
+        def combine(q, after_first=None):
             dx, fetch = results[q]
             base_ps = psum.tile([P, T], F32, name="bank")
             nc.tensor.matmul_mx(
@@ -288,6 +290,8 @@ def tile_moe_adb_silu_kernel(
                     terms.append(base_ps[:, token_halves[h]])
                     terms.extend(room(q, PACK * r, h) for r in range(1, fetch[h]))
                     nc.vector.tensor_tensor(room(q, i + 1, h), terms[i], room(q, i, h), ALU.add)
+                if i == 0 and after_first is not None:
+                    after_first()
             for h in range(2):
                 nc.sync.dma_start(out[q * P:(q + 1) * P, token_halves[h]], room(q, TOP, h))
 
@@ -300,9 +304,10 @@ def tile_moe_adb_silu_kernel(
         quantise_wat(2, 2, 0, nc.vector.tensor_copy, "wa_bf_0_2")
         stage_2(0, "wa_raw_4", (1, 1))
         quantise_wat(2, 2, 1, nc.vector.tensor_copy, "wa_bf_2_1")
-        quantise_wat(2, 1, LAST_PAIR, nc.vector.tensor_copy, "wa_bf_2_2")
         stage_2(1, "wa_bf_1_2", (1, 1))
-        combine(0)
+        combine(
+            0, lambda: quantise_wat(2, 1, LAST_PAIR, nc.vector.tensor_copy, None, wb_tiles[0][:, 0:T].bitcast(BF16))
+        )
         quantise_wat(3, 1, LAST_PAIR, nc.scalar.copy, "wa_bf_3_2")
         stage_2(2, "a_raw_4", (1, 2))
         combine(1)

@@ -83,8 +83,7 @@ def tile_moe_adb_silu_kernel(
         load_a(1, 1)
         load_wbt(1)
         for e in range(2, E):
-            if e % 2 == 0:
-                load_a(e, 2)
+            load_a(e, 1)
             load_wbt(e)
 
         slot_w = keep.tile([P, S], U32, name="g_w", align_bytes=64)
@@ -247,13 +246,27 @@ def tile_moe_adb_silu_kernel(
         results = {}
 
         def room(q, i, h):
-            if i == PACK:
-                return wb_tiles[PACK][:, q * T:(q + 1) * T][:, token_halves[h]]
+            if i >= PACK:
+                return wb_tiles[i][:, q * T:(q + 1) * T][:, token_halves[h]]
             return wb_tiles[q][:, i * T:(i + 1) * T][:, token_halves[h]]
 
-        def stage_2(q, tag, fetch):
+        bases = {}
+
+        def multiply_base(q):
+            base_ps = psum.tile([P, T], F32, name="bank")
+            nc.tensor.matmul_mx(
+                base_ps[:],
+                lhsT=wt_w[:, 2 * q * P:2 * (q + 1) * P].bitcast(FP4X4), lhsT_scale=wt_s[:, q * P:(q + 1) * P],
+                rhs=dy_w[:, 0:T].bitcast(FP8X4), rhs_scale=dy_s[:, 0:T],
+                start=True, stop=True,
+            )
+            bases[q] = base_ps
+
+        def stage_2(q, tag, fetch, before_last_pair=None):
             dx = keep.tile([P, S], F32, name=tag, align_bytes=64)
             for u in range(PAIRS):
+                if u == LAST_PAIR and before_last_pair is not None:
+                    before_last_pair()
                 bank = psum.tile([P, 2 * C], F32, name="bank")
                 for v in range(2):
                     wa_w, wa_s = wa_mx[q, 2 * u + v]
@@ -265,30 +278,26 @@ def tile_moe_adb_silu_kernel(
                         start=True, stop=True,
                     )
                 nc.scalar.copy(dx[:, 2 * u * C:2 * (u + 1) * C], bank[:])
-            if q in (1, 2):
+            if q == 1:
                 nc.scalar.activation(wb_tiles[q][:, 0:T], dx[:].indirect(pos_t[0][:]), ACT.Copy)
-            for r in range(1 if q in (1, 2) else 0, 2):
+            for r in range(1 if q == 1 else 0, 2):
                 for h in range(2):
                     if r < fetch[h]:
                         nc.scalar.activation(
-                            room(q, PACK * r, h), dx[:].indirect(pos_t[r][:, list_halves[h]]), ACT.Copy
+                            room(q, PACK + r if q == 3 else PACK * r, h), dx[:].indirect(pos_t[r][:, list_halves[h]]), ACT.Copy
                         )
             results[q] = (dx, fetch)
 
         def combine(q, after_first=None):
             dx, fetch = results[q]
-            base_ps = psum.tile([P, T], F32, name="bank")
-            nc.tensor.matmul_mx(
-                base_ps[:],
-                lhsT=wt_w[:, 2 * q * P:2 * (q + 1) * P].bitcast(FP4X4), lhsT_scale=wt_s[:, q * P:(q + 1) * P],
-                rhs=dy_w[:, 0:T].bitcast(FP8X4), rhs_scale=dy_s[:, 0:T],
-                start=True, stop=True,
-            )
             for i in range(TOP):
                 for h in range(2):
                     terms = [dx[:].indirect(pos_t[r][:, list_halves[h]]) for r in range(fetch[h], TOP)]
-                    terms.append(base_ps[:, token_halves[h]])
-                    terms.extend(room(q, PACK * r, h) for r in range(1, fetch[h]))
+                    if q == 3:
+                        terms.extend(room(q, PACK + r, h) for r in range(fetch[h]))
+                    else:
+                        terms.append(bases[q][:, token_halves[h]])
+                        terms.extend(room(q, PACK * r, h) for r in range(1, fetch[h]))
                     nc.vector.tensor_tensor(room(q, i + 1, h), terms[i], room(q, i, h), ALU.add)
                 if i == 0 and after_first is not None:
                     after_first()
@@ -305,12 +314,19 @@ def tile_moe_adb_silu_kernel(
         stage_2(0, "wa_raw_4", (1, 1))
         quantise_wat(2, 2, 1, nc.vector.tensor_copy, "wa_bf_2_1")
         stage_2(1, "wa_bf_1_2", (1, 1))
+        multiply_base(0)
         combine(
             0, lambda: quantise_wat(2, 1, LAST_PAIR, nc.vector.tensor_copy, None, wb_tiles[0][:, 0:T].bitcast(BF16))
         )
         quantise_wat(3, 1, LAST_PAIR, nc.scalar.copy, "wa_bf_3_2")
-        stage_2(2, "a_raw_4", (1, 2))
+
+        def early_bases():
+            multiply_base(1)
+            multiply_base(3)
+            nc.scalar.copy(wb_tiles[3][:, 0:T], bases[3][:])
+
+        stage_2(2, "a_raw_4", (1, 2), early_bases)
         combine(1)
-        stage_2(3, "wa_bf_3_2", (2, 2))
+        stage_2(3, "wa_bf_3_2", (2, 2), lambda: multiply_base(2))
         combine(2)
         combine(3)

@@ -26,8 +26,8 @@ LAST_PAIR = PAIRS - 1
 HALF = C // 2
 PIECE = PACK * C
 WINDOW = 2048
-SHARED = (3, 4, 5)
-GPSIMD_COLS = 72
+SHARED = (2, 3, 4, 5)
+GPSIMD_COLS = 48
 
 
 def tile_moe_adb_silu_kernel(
@@ -222,24 +222,25 @@ def tile_moe_adb_silu_kernel(
 
         wa_mx = {}
 
-        def quantise_wat(q0, tiles, u, copy, tag, place=None):
+        def quantise_wat(q0, tiles, adapters, copy, tag, place=None, words_tag=None):
             width = tiles * P
             if place is None:
-                place = keep.tile([P, 2 * width * PACK], BF16, name=tag, align_bytes=64)[:]
-            wa_bf = place.rearrange("p (v m j) -> p v m j", v=2, j=PACK)
-            for v in range(2):
-                start, piece = [(first, x) for first, count, x in wa_raw[2 * u + v] if first <= q0 < first + count][0]
+                place = keep.tile([P, len(adapters) * width * PACK], BF16, name=tag, align_bytes=64)[:]
+            wa_bf = place.rearrange("p (v m j) -> p v m j", v=len(adapters), j=PACK)
+            for v, e in enumerate(adapters):
+                start, piece = [(first, x) for first, count, x in wa_raw[e] if first <= q0 < first + count][0]
                 copy(
                     wa_bf[:, v, :, :].rearrange("p (c i) j -> p c j i", i=PACK),
                     piece[:, :, (q0 - start) * P:(q0 - start) * P + width].rearrange("p j (c i) -> p c j i", i=PACK),
                 )
-            wa_w = keep.tile([P, 2 * width], U32, name="wa_w_%d_%d" % (q0, u), align_bytes=64)
-            wa_s = keep.tile([P, 2 * width], U8, name="wa_s_%d_%d" % (q0, u), align_bytes=64)
+            name = "%d_%d" % (q0, adapters[0])
+            wa_w = keep.tile([P, len(adapters) * width], U32, name=words_tag or "wa_w_" + name, align_bytes=64)
+            wa_s = keep.tile([P, len(adapters) * width], U8, name="wa_s_" + name, align_bytes=64)
             nc.vector.quantize_mx(wa_w[:].bitcast(FP8X4), wa_s[:], place)
-            for v in range(2):
+            for v, e in enumerate(adapters):
                 for j in range(tiles):
                     own = slice(v * width + j * P, v * width + (j + 1) * P)
-                    wa_mx[q0 + j, 2 * u + v] = (wa_w[:, own], wa_s[:, own])
+                    wa_mx[q0 + j, e] = (wa_w[:, own], wa_s[:, own])
 
         token_halves = [slice(h * (T // 2), (h + 1) * (T // 2)) for h in range(2)]
         list_halves = [slice(h * (T // 2 // LIST_COL), (h + 1) * (T // 2 // LIST_COL)) for h in range(2)]
@@ -305,20 +306,21 @@ def tile_moe_adb_silu_kernel(
                 nc.sync.dma_start(out[q * P:(q + 1) * P, token_halves[h]], room(q, TOP, h))
 
         for u in range(LAST_PAIR):
-            quantise_wat(0, 2, u, nc.scalar.copy, "wa_bf_0_%d" % u)
+            quantise_wat(0, 2, (2 * u, 2 * u + 1), nc.scalar.copy, "wa_bf_0_%d" % u)
             if u == 0:
                 quantise_dh(last, dh_last)
         for q in range(2):
-            quantise_wat(q, 1, LAST_PAIR, nc.scalar.copy, "wa_bf_%d_2" % q)
-        quantise_wat(2, 2, 0, nc.vector.tensor_copy, "wa_bf_0_2")
+            quantise_wat(q, 1, (before, last), nc.scalar.copy, "wa_bf_%d_2" % q)
+        quantise_wat(2, 2, (0,), nc.scalar.copy, "wa_bf_2_0", None, "dh_bf")
+        quantise_wat(2, 2, (1,), nc.vector.tensor_copy, "wa_bf_0_2")
         stage_2(0, "wa_raw_4", (1, 1))
-        quantise_wat(2, 2, 1, nc.vector.tensor_copy, "wa_bf_2_1")
+        quantise_wat(2, 2, (2, 3), nc.vector.tensor_copy, "wa_bf_2_1")
         stage_2(1, "wa_bf_1_2", (1, 1))
         multiply_base(0)
         combine(
-            0, lambda: quantise_wat(2, 1, LAST_PAIR, nc.vector.tensor_copy, None, wb_tiles[0][:, 0:T].bitcast(BF16))
+            0, lambda: quantise_wat(2, 1, (before, last), nc.vector.tensor_copy, None, wb_tiles[0][:, 0:T].bitcast(BF16))
         )
-        quantise_wat(3, 1, LAST_PAIR, nc.scalar.copy, "wa_bf_3_2")
+        quantise_wat(3, 1, (before, last), nc.scalar.copy, "wa_bf_3_2")
 
         def early_bases():
             multiply_base(1)

@@ -22,12 +22,12 @@ P = 128
 PACK = 4
 LIST_COL = 16
 PAIRS = E // 2
-LAST_PAIR = PAIRS - 1
-HALF = C // 2
 PIECE = PACK * C
 WINDOW = 2048
-SHARED = (2, 3, 4, 5)
-GPSIMD_COLS = 48
+GPSIMD_COLS = (96, 64)
+VECTOR_COLS = 36
+AHEAD = 2
+HALF_T = T // 2
 
 
 def tile_moe_adb_silu_kernel(
@@ -36,7 +36,8 @@ def tile_moe_adb_silu_kernel(
     nc = tc.nc
     with ExitStack() as ctx:
         keep = ctx.enter_context(tc.tile_pool(name="keep", bufs=1))
-        ring = ctx.enter_context(tc.tile_pool(name="ring", bufs=4))
+        ring = ctx.enter_context(tc.tile_pool(name="ring", bufs=3))
+        placed = ctx.enter_context(tc.tile_pool(name="placed", bufs=1))
         psum = ctx.enter_context(tc.psum_pool(name="psum", bufs=8))
 
         def load_scale_rows(plane, scales, r):
@@ -59,32 +60,26 @@ def tile_moe_adb_silu_kernel(
         nc.vector.memset(wt_s[:].bitcast(I32), 0)
 
         a_rows = a.rearrange("(p t) s -> p t s", t=PACK)
-        a_tiles, a_t, wb_tiles = [], {}, {}
+        a_t, wb_raw = {}, {}
 
-        def load_a(e, count):
-            if e % 2 == 0:
-                a_tiles.append(keep.tile([P, 2 * PIECE], F32, name="a_raw_%d" % e, align_bytes=64))
-            view = a_tiles[e // 2][:, e % 2 * PIECE:(e % 2 + count) * PIECE].rearrange("p (t s) -> p t s", t=PACK)
-            nc.sync.dma_start(view, a_rows[:, :, e * C:(e + count) * C])
-            for j in range(count):
-                a_t[e + j] = view[:, :, j * C:(j + 1) * C]
+        def load_a(e):
+            a_t[e] = keep.tile([P, PIECE], F32, name="a_raw_%d" % e, align_bytes=64)
+            nc.sync.dma_start(a_t[e][:].rearrange("p (t s) -> p t s", t=PACK), a_rows[:, :, e * C:(e + 1) * C])
 
         def load_wbt(e):
-            wb_tiles[e] = ring.tile([P, PACK * H], F32, name="wide", bufs=E, align_bytes=64)
-            nc.sync.dma_start(
-                wb_tiles[e][:].rearrange("p (j c) -> p j c", j=PACK), wbt[e].rearrange("(p j) c -> p j c", j=PACK)
-            )
+            wb_raw[e] = keep.tile([P, PACK * H], F32, name="wb_raw_%d" % e, align_bytes=64)
+            nc.sync.dma_start(wb_raw[e][:], wbt[e].rearrange("(p j) c -> p (j c)", j=PACK))
 
-        load_a(0, 1)
+        load_a(0)
         for r in range(4):
             load_scale_rows(dy_s, dy_scales, r)
         nc.sync.dma_start(gate_rows[:], gate.rearrange("r (b p) -> (r b) p", p=P)[0:P, :])
-        load_wbt(0)
-        load_a(1, 1)
-        load_wbt(1)
-        for e in range(2, E):
-            load_a(e, 1)
+        for e in range(E):
+            if e < AHEAD:
+                load_a(e + 1)
             load_wbt(e)
+            if AHEAD <= e < E - 1:
+                load_a(e + 1)
 
         slot_w = keep.tile([P, S], U32, name="g_w", align_bytes=64)
         slot_s = keep.tile([P, S], U8, name="g_s", align_bytes=64)
@@ -94,7 +89,6 @@ def tile_moe_adb_silu_kernel(
         gate_ps = psum.tile([P, P], F32, name="bank")
         nc.tensor.transpose(gate_ps[:], gate_rows[:], ident[:])
         gate_cols = keep.tile([P, S // P], F32, name="gate_c")
-        nc.scalar.mul(gate_cols[:], gate_ps[:, 0:S // P], -0.5)
         gate_banks = []
         blocks_per_bank = 2 * C // P
 
@@ -107,25 +101,28 @@ def tile_moe_adb_silu_kernel(
                 )
             gate_banks.append(gate_bank)
 
-        activated, wb_bf, wb_mx, brackets, dh_mx = {}, {}, {}, {}, {}
+        activated, wb_bf, wb_mx, dh_mx = {}, {}, {}, {}
 
         def activations(e):
-            pairs = a_t[e].rearrange("p t (c i) -> p c t i", i=2)
-            silu_neg = ring.tile([P, C, PACK], F32, name="silu_n", bufs=4)
-            tanh_half = keep.tile([P, C, PACK], F32, name="tanh_h_%d" % e, align_bytes=64)
-            for target, func, scale in ((silu_neg, ACT.Silu, -1.0), (tanh_half, ACT.Tanh, 0.5)):
-                nc.scalar.activation(target[:].rearrange("p (c i) t -> p c t i", i=2), pairs, func, scale=scale)
+            silu_neg = keep.tile([P, PIECE], F32, name="silu_n_%d" % e, align_bytes=64)
+            tanh_half = ring.tile([P, PIECE], F32, name="tanh_h")
+            calls = [(silu_neg, ACT.Silu, -1.0), (tanh_half, ACT.Tanh, 0.5)]
+            for target, func, scale in calls if e == 0 else reversed(calls):
+                nc.scalar.activation(target[:], a_t[e][:], func, scale=scale)
             activated[e] = (silu_neg, tanh_half)
 
-        def round_wbt(e, groups, cols, copy):
+        def round_wbt(e, cols, copy):
             copy(
-                wb_bf[e][:].rearrange("p (u w m j) -> p u m j w", u=2, w=2, j=PACK)[:, groups, cols],
-                wb_tiles[e][:].rearrange("p (j m u w) -> p u m j w", j=PACK, u=2, w=2)[:, groups, cols],
+                wb_bf[e][:].rearrange("p (u w m j) -> p u m j w", u=2, w=2, j=PACK)[:, :, cols],
+                wb_raw[e][:].rearrange("p (j m u w) -> p u m j w", j=PACK, u=2, w=2)[:, :, cols],
             )
 
-        def round_wbt_on_scalar(e):
-            wb_bf[e] = keep.tile([P, PACK * H], BF16, name="wb_bf_%d" % (max(e - 1, 0) % 3), align_bytes=64)
-            round_wbt(e, slice(0, 1 if e in SHARED else 2), slice(GPSIMD_COLS if e == 1 else 0, P), nc.scalar.copy)
+        def round_wbt_on_gpsimd(e, cols):
+            nc.gpsimd.tensor_scalar(
+                wb_bf[e][:].rearrange("p (t m j) -> p m t j", t=PACK, j=PACK)[:, cols],
+                wb_raw[e][:].rearrange("p (j m t) -> p m t j", t=PACK, j=PACK)[:, cols],
+                1.0, 0.0, ALU.mult, ALU.add,
+            )
 
         def quantise_wbt(e):
             wb_w = ring.tile([P, H], U32, name="wb_w", align_bytes=64, bufs=2)
@@ -136,65 +133,72 @@ def tile_moe_adb_silu_kernel(
         def make_brackets(e):
             silu_neg, tanh_half = activated[e]
             wb_w, wb_s = wb_mx[e]
-            gated, summed = wb_tiles[e][:, 0:PIECE], wb_tiles[e][:, PIECE:2 * PIECE]
+            gated, summed = wb_raw[e][:, 0:PIECE], wb_raw[e][:, PIECE:2 * PIECE]
             nc.vector.scalar_tensor_tensor(
-                gated.rearrange("p (c t) -> p c t", t=PACK), tanh_half[:], 1.0,
-                gate_banks[e // 2][:, (e % 2) * C:(e % 2 + 1) * C].unsqueeze(2).to_broadcast([P, C, PACK]),
+                gated.rearrange("p (t c) -> p t c", t=PACK), tanh_half[:].rearrange("p (t c) -> p t c", t=PACK), 1.0,
+                gate_banks[e // 2][:, (e % 2) * C:(e % 2 + 1) * C].unsqueeze(1).to_broadcast([P, PACK, C]),
                 ALU.add, ALU.mult,
             )
+            slots = slice(e * C, (e + 1) * C)
             for h in range(2):
-                own = slice(h * HALF, (h + 1) * HALF)
-                slots = slice(e * C + h * HALF, e * C + (h + 1) * HALF)
-                bank = psum.tile([P, PACK, HALF], F32, name="bank")
-                for t in range(PACK):
+                bank = psum.tile([P, 2 * C], F32, name="bank")
+                for w in range(2):
+                    t = 2 * h + w
                     nc.tensor.matmul_mx(
-                        bank[:, t, :],
+                        bank[:, w * C:(w + 1) * C],
                         lhsT=wb_w[:, t * P:(t + 1) * P].bitcast(FP8X4), lhsT_scale=wb_s[:, t * P:(t + 1) * P],
                         rhs=slot_w[:, slots].bitcast(FP8X4), rhs_scale=slot_s[:, slots],
                         start=True, stop=True,
                     )
+                own = slice(2 * h * C, 2 * (h + 1) * C)
                 nc.vector.scalar_tensor_tensor(
-                    summed.rearrange("p (c t) -> p c t", t=PACK)[:, own, :], silu_neg[:, own, :], 1.0,
-                    bank[:].rearrange("p t c -> p c t"), ALU.subtract, ALU.mult,
+                    summed[:, own], silu_neg[:, own], 1.0, bank[:], ALU.subtract, ALU.mult
                 )
-            brackets[e] = (gated, summed)
 
-        def round_dh(e, engine, dh_bf):
-            gated, summed = brackets[e]
-            engine.tensor_tensor(dh_bf[:], gated, summed, ALU.mult)
+        def round_dh(e, engine, dh_bf, run):
+            gated, summed = wb_raw[e][:, 0:PIECE], wb_raw[e][:, PIECE:2 * PIECE]
+            engine.tensor_tensor(
+                dh_bf.rearrange("p (c i t) -> p c t i", i=run, t=PACK),
+                gated.rearrange("p (t c i) -> p c t i", i=run, t=PACK),
+                summed.rearrange("p (t c i) -> p c t i", i=run, t=PACK),
+                ALU.mult,
+            )
 
-        def quantise_dh(e, dh_bf):
-            words = keep.tile([P, C], U32, name="tanh_h_%d" % ((e + 1) % E), align_bytes=64)
+        def quantise_dh(e, dh_bf, tag=None):
+            words = keep.tile([P, C], U32, name=tag or "silu_n_%d" % (e + 1), align_bytes=64)[:]
             plane = keep.tile([P, C], U8, name="dh_s_%d" % e, align_bytes=64)
-            nc.vector.quantize_mx(words[:].bitcast(FP8X4), plane[:], dh_bf[:])
+            nc.vector.quantize_mx(words.bitcast(FP8X4), plane[:], dh_bf)
             dh_mx[e] = (words, plane)
 
-        dh_shared = keep.tile([P, PIECE], BF16, name="dh_bf", align_bytes=64)
-        dh_last = keep.tile([P, PIECE], BF16, name="dh_last", align_bytes=64)
         before, last = E - 2, E - 1
+        activations(0)
+        nc.scalar.mul(gate_cols[:], gate_ps[:, 0:S // P], -0.5)
         for e in range(E):
             if e % 2 == 0:
                 spread_gates(e // 2)
-            activations(e)
-            round_wbt_on_scalar(e)
-            if e == 1:
-                nc.gpsimd.tensor_scalar(
-                    wb_bf[e][:].rearrange("p (t m j) -> p m t j", t=PACK, j=PACK)[:, 0:GPSIMD_COLS],
-                    wb_tiles[e][:].rearrange("p (j m t) -> p m t j", t=PACK, j=PACK)[:, 0:GPSIMD_COLS],
-                    1.0, 0.0, ALU.mult, ALU.add,
-                )
-            if e in SHARED:
-                round_wbt(e, slice(1, 2), slice(0, P), nc.vector.tensor_copy)
+            if e < AHEAD:
+                activations(e + 1)
+            wb_bf[e] = keep.tile([P, PACK * H], BF16, name="wb_bf_%d" % (0 if e < 2 else 1 + e % 2), align_bytes=64)
+            if e < 2:
+                round_wbt_on_gpsimd(e, slice(0, GPSIMD_COLS[e]))
+                round_wbt(e, slice(GPSIMD_COLS[e], P), nc.scalar.copy)
+            else:
+                round_wbt(e, slice(VECTOR_COLS if e > 2 else 0, P), nc.scalar.copy)
+                if e > 2:
+                    round_wbt(e, slice(0, VECTOR_COLS), nc.vector.tensor_copy)
+                if e < last:
+                    activations(e + 1)
             if e > 1:
                 quantise_dh(e - 2, dh_shared)
             quantise_wbt(e)
+            if e == 1:
+                dh_shared = wb_bf[1][:, 0:PIECE]
             if e > 0:
-                round_dh(e - 1, nc.gpsimd, dh_shared)
+                round_dh(e - 1, nc.gpsimd, dh_shared, 1)
             make_brackets(e)
         quantise_dh(before, dh_shared)
-        round_dh(last, nc.vector, dh_last)
 
-        wa_raw, pos_t = [[] for e in range(E)], []
+        wa_raw, pos_t = {}, []
 
         def load_list(pos):
             list_tile = keep.tile([P, T // LIST_COL], U16, name="pos_%d" % len(pos_t))
@@ -204,131 +208,127 @@ def tile_moe_adb_silu_kernel(
         small_loads = [lambda r=r: load_scale_rows(wt_s, wt_scales, r) for r in range(4)]
         small_loads.append(lambda: nc.sync.dma_start(wt_w[:].bitcast(I32), wt_words[0].bitcast(I32)))
         small_loads.extend(lambda pos=pos: load_list(pos) for pos in (pos1, pos2, pos3))
-        wa_pieces = [(e, 0, 4) for e in range(2)]
-        wa_pieces.extend((e, 0, 2) for e in range(2, E))
-        wa_pieces.extend((e, 2, 2) for e in range(2, last))
-        wa_pieces.extend((last, q, 1) for q in (2, 3))
-        for i, (e, q0, tiles) in enumerate(wa_pieces):
-            if e == 0 or (q0 == 2 and e % 2 == 0):
-                host = a_tiles[e // 2]
-            elif e == 1 or e % 2 == 0:
-                host = keep.tile([P, 2 * PIECE], F32, name="wa_raw_%d" % e, align_bytes=64)
-            first = 0 if tiles == 4 else e % 2 * PIECE + q0 % 2 * PACK * P
-            piece = host[:, first:first + tiles * PACK * P].rearrange("p (j c) -> p j c", j=PACK)
-            nc.sync.dma_start(piece, wat[e].rearrange("(p j) c -> p j c", j=PACK)[:, :, q0 * P:(q0 + tiles) * P])
-            wa_raw[e].append((q0, tiles, piece))
+        for i in range(2 * E):
+            g, e = divmod(i, E)
+            if g == 1:
+                wa_raw[g, e] = a_t[e][:]
+            elif e == last:
+                wa_raw[g, e] = placed.tile([P, PIECE], F32, name="wa_raw_last", offset=4 * PIECE)[:]
+            else:
+                wa_raw[g, e] = keep.tile([P, PIECE], F32, name="wa_raw_%d" % e, align_bytes=64)[:]
+            nc.sync.dma_start(
+                wa_raw[g, e].rearrange("p (j c) -> p j c", j=PACK),
+                wat[e].rearrange("(p j) c -> p j c", j=PACK)[:, :, g * C:(g + 1) * C],
+            )
             if i < len(small_loads):
                 small_loads[i]()
 
-        wa_mx = {}
+        wa_bf, wa_mx = {}, {}
 
-        def quantise_wat(q0, tiles, adapters, copy, tag, place=None, words_tag=None):
-            width = tiles * P
-            if place is None:
-                place = keep.tile([P, len(adapters) * width * PACK], BF16, name=tag, align_bytes=64)[:]
-            wa_bf = place.rearrange("p (v m j) -> p v m j", v=len(adapters), j=PACK)
-            for v, e in enumerate(adapters):
-                start, piece = [(first, x) for first, count, x in wa_raw[e] if first <= q0 < first + count][0]
-                copy(
-                    wa_bf[:, v, :, :].rearrange("p (c i) j -> p c j i", i=PACK),
-                    piece[:, :, (q0 - start) * P:(q0 - start) * P + width].rearrange("p j (c i) -> p c j i", i=PACK),
+        def round_wat(g, e, copy, tag=None):
+            if e % 2 == 0:
+                wa_bf[g, e // 2] = keep.tile(
+                    [P, 2 * PIECE], BF16, name=tag or "wa_bf_%d_%d" % (g, e // 2), align_bytes=64
                 )
-            name = "%d_%d" % (q0, adapters[0])
-            wa_w = keep.tile([P, len(adapters) * width], U32, name=words_tag or "wa_w_" + name, align_bytes=64)
-            wa_s = keep.tile([P, len(adapters) * width], U8, name="wa_s_" + name, align_bytes=64)
-            nc.vector.quantize_mx(wa_w[:].bitcast(FP8X4), wa_s[:], place)
-            for v, e in enumerate(adapters):
-                for j in range(tiles):
-                    own = slice(v * width + j * P, v * width + (j + 1) * P)
-                    wa_mx[q0 + j, e] = (wa_w[:, own], wa_s[:, own])
+            copy(
+                wa_bf[g, e // 2][:, e % 2 * PIECE:(e % 2 + 1) * PIECE].rearrange("p (c i j) -> p c j i", i=PACK, j=PACK),
+                wa_raw[g, e].rearrange("p (j c i) -> p c j i", i=PACK, j=PACK),
+            )
 
-        token_halves = [slice(h * (T // 2), (h + 1) * (T // 2)) for h in range(2)]
-        list_halves = [slice(h * (T // 2 // LIST_COL), (h + 1) * (T // 2 // LIST_COL)) for h in range(2)]
-        results = {}
+        def quantise_wat(g, u, tag=None):
+            words = keep.tile([P, 2 * C], U32, name=tag or "wa_w_%d_%d" % (g, u), align_bytes=64)[:]
+            plane = keep.tile([P, 2 * C], U8, name="wa_s_%d_%d" % (g, u), align_bytes=64)
+            nc.vector.quantize_mx(words.bitcast(FP8X4), plane[:], wa_bf[g, u][:])
+            wa_mx[g, u] = (words, plane)
 
-        def room(q, i, h):
-            if i >= PACK:
-                return wb_tiles[i][:, q * T:(q + 1) * T][:, token_halves[h]]
-            return wb_tiles[q][:, i * T:(i + 1) * T][:, token_halves[h]]
+        dx, bases = {}, {}
 
-        bases = {}
+        def multiply_pair(q, u):
+            bank = psum.tile([P, 2 * C], F32, name="bank")
+            wa_w, wa_s = wa_mx[q // 2, u]
+            for v in range(2):
+                words, plane = dh_mx[2 * u + v]
+                own = slice(v * C + q % 2 * P, v * C + (q % 2 + 1) * P)
+                nc.tensor.matmul_mx(
+                    bank[:, v * C:(v + 1) * C],
+                    lhsT=wa_w[:, own].bitcast(FP8X4), lhsT_scale=wa_s[:, own],
+                    rhs=words.bitcast(FP8X4), rhs_scale=plane[:],
+                    start=True, stop=True,
+                )
+            nc.scalar.copy(dx[q][:, 2 * u * C:2 * (u + 1) * C], bank[:])
 
         def multiply_base(q):
-            base_ps = psum.tile([P, T], F32, name="bank")
+            bases[q] = psum.tile([P, T], F32, name="bank")
             nc.tensor.matmul_mx(
-                base_ps[:],
+                bases[q][:],
                 lhsT=wt_w[:, 2 * q * P:2 * (q + 1) * P].bitcast(FP4X4), lhsT_scale=wt_s[:, q * P:(q + 1) * P],
                 rhs=dy_w[:, 0:T].bitcast(FP8X4), rhs_scale=dy_s[:, 0:T],
                 start=True, stop=True,
             )
-            bases[q] = base_ps
 
-        def stage_2(q, tag, fetch, before_last_pair=None):
-            dx = keep.tile([P, S], F32, name=tag, align_bytes=64)
-            for u in range(PAIRS):
-                if u == LAST_PAIR and before_last_pair is not None:
-                    before_last_pair()
-                bank = psum.tile([P, 2 * C], F32, name="bank")
-                for v in range(2):
-                    wa_w, wa_s = wa_mx[q, 2 * u + v]
-                    words, plane = dh_mx[2 * u + v]
-                    nc.tensor.matmul_mx(
-                        bank[:, v * C:(v + 1) * C],
-                        lhsT=wa_w.bitcast(FP8X4), lhsT_scale=wa_s,
-                        rhs=words[:].bitcast(FP8X4), rhs_scale=plane[:],
-                        start=True, stop=True,
-                    )
-                nc.scalar.copy(dx[:, 2 * u * C:2 * (u + 1) * C], bank[:])
-            if q == 1:
-                nc.scalar.activation(wb_tiles[q][:, 0:T], dx[:].indirect(pos_t[0][:]), ACT.Copy)
-            for r in range(1 if q == 1 else 0, 2):
-                for h in range(2):
-                    if r < fetch[h]:
-                        nc.scalar.activation(
-                            room(q, PACK + r if q == 3 else PACK * r, h), dx[:].indirect(pos_t[r][:, list_halves[h]]), ACT.Copy
-                        )
-            results[q] = (dx, fetch)
+        halves = [slice(h * HALF_T, (h + 1) * HALF_T) for h in range(2)]
+        list_halves = [slice(h * HALF_T // LIST_COL, (h + 1) * HALF_T // LIST_COL) for h in range(2)]
 
-        def combine(q, after_first=None):
-            dx, fetch = results[q]
-            for i in range(TOP):
-                for h in range(2):
-                    terms = [dx[:].indirect(pos_t[r][:, list_halves[h]]) for r in range(fetch[h], TOP)]
-                    if q == 3:
-                        terms.extend(room(q, PACK + r, h) for r in range(fetch[h]))
-                    else:
-                        terms.append(bases[q][:, token_halves[h]])
-                        terms.extend(room(q, PACK * r, h) for r in range(1, fetch[h]))
-                    nc.vector.tensor_tensor(room(q, i + 1, h), terms[i], room(q, i, h), ALU.add)
-                if i == 0 and after_first is not None:
-                    after_first()
+        def room(q, i):
+            if i == PACK:
+                return wb_raw[PACK][:, q * T:(q + 1) * T]
+            return wb_raw[q][:, i * T:(i + 1) * T]
+
+        def fetch(q, r, split):
+            for cols, entries in zip(halves, list_halves) if split else [(slice(0, T), slice(0, T // LIST_COL))]:
+                nc.scalar.activation(room(q, r)[:, cols], dx[q][:].indirect(pos_t[r][:, entries]), ACT.Copy)
+
+        def combine(q, first_sum, after_first=None):
             for h in range(2):
-                nc.sync.dma_start(out[q * P:(q + 1) * P, token_halves[h]], room(q, TOP, h))
+                nc.vector.tensor_tensor(first_sum[:, halves[h]], bases[q][:, halves[h]], room(q, 0)[:, halves[h]], ALU.add)
+            if after_first is not None:
+                after_first()
+            for h in range(2):
+                nc.vector.tensor_tensor(
+                    room(q, 2)[:, halves[h]], dx[q][:].indirect(pos_t[2][:, list_halves[h]]), first_sum[:, halves[h]], ALU.add
+                )
+            for h in range(2):
+                nc.vector.tensor_tensor(room(q, 3)[:, halves[h]], room(q, 1)[:, halves[h]], room(q, 2)[:, halves[h]], ALU.add)
+                nc.sync.dma_start(out[q * P:(q + 1) * P, halves[h]], room(q, 3)[:, halves[h]])
 
-        for u in range(LAST_PAIR):
-            quantise_wat(0, 2, (2 * u, 2 * u + 1), nc.scalar.copy, "wa_bf_0_%d" % u)
-            if u == 0:
-                quantise_dh(last, dh_last)
-        for q in range(2):
-            quantise_wat(q, 1, (before, last), nc.scalar.copy, "wa_bf_%d_2" % q)
-        quantise_wat(2, 2, (0,), nc.scalar.copy, "wa_bf_2_0", None, "dh_bf")
-        quantise_wat(2, 2, (1,), nc.vector.tensor_copy, "wa_bf_0_2")
-        stage_2(0, "wa_raw_4", (1, 1))
-        quantise_wat(2, 2, (2, 3), nc.vector.tensor_copy, "wa_bf_2_1")
-        stage_2(1, "wa_bf_1_2", (1, 1))
+        for e in range(E):
+            round_wat(0, e, nc.scalar.copy)
+        quantise_wat(0, 0)
+        dh_last = keep.tile([P, PIECE], BF16, name="wa_bf_0_0", align_bytes=64)
+        round_dh(last, nc.vector, dh_last[:], 2)
+        quantise_wat(0, 1)
+        quantise_dh(last, dh_last[:], "wa_bf_0_1")
+        quantise_wat(0, 2)
+        dx[0] = placed.tile([P, S], F32, name="dx_0", offset=0)
+        dx[1] = placed.tile([P, S], F32, name="dx_1", offset=4 * S)
+        for q, u in ((0, 0), (1, 0), (0, 1), (1, 1), (0, 2)):
+            multiply_pair(q, u)
+        fetch(0, 0, True)
+        multiply_pair(1, 2)
         multiply_base(0)
-        combine(
-            0, lambda: quantise_wat(2, 1, (before, last), nc.vector.tensor_copy, None, wb_tiles[0][:, 0:T].bitcast(BF16))
-        )
-        quantise_wat(3, 1, (before, last), nc.scalar.copy, "wa_bf_3_2")
-
-        def early_bases():
-            multiply_base(1)
-            multiply_base(3)
-            nc.scalar.copy(wb_tiles[3][:, 0:T], bases[3][:])
-
-        stage_2(2, "a_raw_4", (1, 2), early_bases)
-        combine(1)
-        stage_2(3, "wa_bf_3_2", (2, 2), lambda: multiply_base(2))
-        combine(2)
-        combine(3)
+        multiply_base(1)
+        fetch(0, 1, False)
+        for e in range(3):
+            round_wat(1, e, nc.vector.tensor_copy)
+        quantise_wat(1, 0, "a_raw_2")
+        round_wat(1, 3, nc.vector.tensor_copy)
+        round_wat(1, before, nc.vector.tensor_copy)
+        quantise_wat(1, 1, "a_raw_4")
+        round_wat(1, last, nc.vector.tensor_copy)
+        combine(0, wa_raw[1, last][:, 0:T], lambda: quantise_wat(1, 2))
+        fetch(1, 0, False)
+        fetch(1, 1, False)
+        combine(1, room(0, 1))
+        dx[2] = keep.tile([P, S], F32, name="dx_2", align_bytes=64)
+        dx[3] = keep.tile([P, S], F32, name="dx_3", align_bytes=64)
+        for q, u in ((2, 0), (2, 1), (3, 0), (3, 1), (2, 2)):
+            multiply_pair(q, u)
+        fetch(2, 0, True)
+        multiply_pair(3, 2)
+        multiply_base(2)
+        multiply_base(3)
+        fetch(2, 1, False)
+        combine(2, room(2, PACK))
+        fetch(3, 0, True)
+        fetch(3, 1, True)
+        combine(3, room(3, PACK))

@@ -24,9 +24,9 @@ LIST_COL = 16
 PAIRS = E // 2
 PIECE = PACK * C
 WINDOW = 2048
-GPSIMD_COLS = (96, 64)
+GPSIMD_COLS = 56
 VECTOR_COLS = 36
-AHEAD = 2
+AHEAD = 3
 HALF_T = T // 2
 
 
@@ -74,7 +74,18 @@ def tile_moe_adb_silu_kernel(
         for r in range(4):
             load_scale_rows(dy_s, dy_scales, r)
         nc.sync.dma_start(gate_rows[:], gate.rearrange("r (b p) -> (r b) p", p=P)[0:P, :])
-        for e in range(E):
+        wb_raw[0] = keep.tile([P, PACK * H], F32, name="wb_raw_0", align_bytes=64)
+
+        def load_first_wbt(g):
+            nc.sync.dma_start(
+                wb_raw[0][:].rearrange("p (j c) -> p j c", j=PACK)[:, :, g * C:(g + 1) * C],
+                wbt[0].rearrange("(p j) c -> p j c", j=PACK)[:, :, g * C:(g + 1) * C],
+            )
+
+        load_first_wbt(0)
+        load_a(1)
+        load_first_wbt(1)
+        for e in range(1, E):
             if e < AHEAD:
                 load_a(e + 1)
             load_wbt(e)
@@ -179,14 +190,17 @@ def tile_moe_adb_silu_kernel(
             if e < AHEAD:
                 activations(e + 1)
             wb_bf[e] = keep.tile([P, PACK * H], BF16, name="wb_bf_%d" % (0 if e < 2 else 1 + e % 2), align_bytes=64)
-            if e < 2:
-                round_wbt_on_gpsimd(e, slice(0, GPSIMD_COLS[e]))
-                round_wbt(e, slice(GPSIMD_COLS[e], P), nc.scalar.copy)
+            if e == 0:
+                for g in range(2):
+                    round_wbt_on_gpsimd(e, slice(g * P // 2, (g + 1) * P // 2))
+            elif e == 1:
+                round_wbt_on_gpsimd(e, slice(0, GPSIMD_COLS))
+                round_wbt(e, slice(GPSIMD_COLS, P), nc.scalar.copy)
             else:
                 round_wbt(e, slice(VECTOR_COLS if e > 2 else 0, P), nc.scalar.copy)
                 if e > 2:
                     round_wbt(e, slice(0, VECTOR_COLS), nc.vector.tensor_copy)
-                if e < last:
+                if AHEAD <= e < last:
                     activations(e + 1)
             if e > 1:
                 quantise_dh(e - 2, dh_shared)
@@ -194,7 +208,7 @@ def tile_moe_adb_silu_kernel(
             if e == 1:
                 dh_shared = wb_bf[1][:, 0:PIECE]
             if e > 0:
-                round_dh(e - 1, nc.gpsimd, dh_shared, 1)
+                round_dh(e - 1, nc.gpsimd, dh_shared, 4)
             make_brackets(e)
         quantise_dh(before, dh_shared)
 
@@ -278,18 +292,25 @@ def tile_moe_adb_silu_kernel(
             for cols, entries in zip(halves, list_halves) if split else [(slice(0, T), slice(0, T // LIST_COL))]:
                 nc.scalar.activation(room(q, r)[:, cols], dx[q][:].indirect(pos_t[r][:, entries]), ACT.Copy)
 
-        def combine(q, first_sum, after_first=None):
+        def add(target, left, right, h):
+            nc.vector.tensor_tensor(target[:, halves[h]], left, right[:, halves[h]], ALU.add)
+
+        def fetched(q, r, h):
+            return dx[q][:].indirect(pos_t[r][:, list_halves[h]])
+
+        def store(q, total, h):
+            nc.sync.dma_start(out[q * P:(q + 1) * P, halves[h]], total[:, halves[h]])
+
+        def combine(q, first_sum, total, before_last=None):
             for h in range(2):
-                nc.vector.tensor_tensor(first_sum[:, halves[h]], bases[q][:, halves[h]], room(q, 0)[:, halves[h]], ALU.add)
-            if after_first is not None:
-                after_first()
+                add(first_sum, bases[q][:, halves[h]], room(q, 0), h)
             for h in range(2):
-                nc.vector.tensor_tensor(
-                    room(q, 2)[:, halves[h]], dx[q][:].indirect(pos_t[2][:, list_halves[h]]), first_sum[:, halves[h]], ALU.add
-                )
+                add(room(q, 2), fetched(q, 2, h), first_sum, h)
+            if before_last is not None:
+                before_last()
             for h in range(2):
-                nc.vector.tensor_tensor(room(q, 3)[:, halves[h]], room(q, 1)[:, halves[h]], room(q, 2)[:, halves[h]], ALU.add)
-                nc.sync.dma_start(out[q * P:(q + 1) * P, halves[h]], room(q, 3)[:, halves[h]])
+                add(total, room(q, 1)[:, halves[h]], room(q, 2), h)
+                store(q, total, h)
 
         for e in range(E):
             round_wat(0, e, nc.scalar.copy)
@@ -314,21 +335,32 @@ def tile_moe_adb_silu_kernel(
         round_wat(1, 3, nc.vector.tensor_copy)
         round_wat(1, before, nc.vector.tensor_copy)
         quantise_wat(1, 1, "a_raw_4")
-        round_wat(1, last, nc.vector.tensor_copy)
-        combine(0, wa_raw[1, last][:, 0:T], lambda: quantise_wat(1, 2))
+        first_sum = keep.tile([P, T], F32, name="wa_bf_1_1", align_bytes=64)
+        combine(0, first_sum, wa_raw[1, last], lambda: round_wat(1, last, nc.vector.tensor_copy))
+        quantise_wat(1, 2)
         fetch(1, 0, False)
         fetch(1, 1, False)
-        combine(1, room(0, 1))
+        first_sum = keep.tile([P, T], F32, name="wa_bf_1_2", align_bytes=64)
+        combine(1, first_sum, room(1, 3))
         dx[2] = keep.tile([P, S], F32, name="dx_2", align_bytes=64)
         dx[3] = keep.tile([P, S], F32, name="dx_3", align_bytes=64)
-        for q, u in ((2, 0), (2, 1), (3, 0), (3, 1), (2, 2)):
+        for q, u in ((2, 0), (2, 1), (3, 0), (3, 1)):
             multiply_pair(q, u)
+        multiply_base(3)
+        nc.scalar.copy(room(3, PACK), bases[3][:])
+        multiply_pair(2, 2)
         fetch(2, 0, True)
         multiply_pair(3, 2)
         multiply_base(2)
-        multiply_base(3)
         fetch(2, 1, False)
-        combine(2, room(2, PACK))
+        combine(2, room(2, PACK), room(2, 3))
         fetch(3, 0, True)
-        fetch(3, 1, True)
-        combine(3, room(3, PACK))
+        nc.scalar.activation(room(3, 1)[:, halves[0]], fetched(3, 1, 0), ACT.Copy)
+        for h in range(2):
+            add(room(3, 2), fetched(3, 2, h), room(3, PACK), h)
+        add(room(3, 3), room(3, 0)[:, halves[0]], room(3, 2), 0)
+        add(room(3, 3), fetched(3, 1, 1), room(3, 2), 1)
+        add(room(3, PACK), room(3, 1)[:, halves[0]], room(3, 3), 0)
+        store(3, room(3, PACK), 0)
+        add(room(3, PACK), room(3, 0)[:, halves[1]], room(3, 3), 1)
+        store(3, room(3, PACK), 1)

@@ -25,8 +25,7 @@ PAIRS = E // 2
 PIECE = PACK * C
 WINDOW = 2048
 GPSIMD_COLS = 56
-VECTOR_COLS = 36
-AHEAD = 3
+VECTOR_COLS = 48
 HALF_T = T // 2
 
 
@@ -74,22 +73,9 @@ def tile_moe_adb_silu_kernel(
         for r in range(4):
             load_scale_rows(dy_s, dy_scales, r)
         nc.sync.dma_start(gate_rows[:], gate.rearrange("r (b p) -> (r b) p", p=P)[0:P, :])
-        wb_raw[0] = keep.tile([P, PACK * H], F32, name="wb_raw_0", align_bytes=64)
-
-        def load_first_wbt(g):
-            nc.sync.dma_start(
-                wb_raw[0][:].rearrange("p (j c) -> p j c", j=PACK)[:, :, g * C:(g + 1) * C],
-                wbt[0].rearrange("(p j) c -> p j c", j=PACK)[:, :, g * C:(g + 1) * C],
-            )
-
-        load_first_wbt(0)
-        load_a(1)
-        load_first_wbt(1)
-        for e in range(1, E):
-            if e < AHEAD:
-                load_a(e + 1)
+        for e in range(E):
             load_wbt(e)
-            if AHEAD <= e < E - 1:
+            if e < E - 1:
                 load_a(e + 1)
 
         slot_w = keep.tile([P, S], U32, name="g_w", align_bytes=64)
@@ -187,21 +173,17 @@ def tile_moe_adb_silu_kernel(
         for e in range(E):
             if e % 2 == 0:
                 spread_gates(e // 2)
-            if e < AHEAD:
-                activations(e + 1)
             wb_bf[e] = keep.tile([P, PACK * H], BF16, name="wb_bf_%d" % (0 if e < 2 else 1 + e % 2), align_bytes=64)
             if e == 0:
-                for g in range(2):
-                    round_wbt_on_gpsimd(e, slice(g * P // 2, (g + 1) * P // 2))
+                round_wbt(e, slice(0, P), nc.scalar.copy)
             elif e == 1:
                 round_wbt_on_gpsimd(e, slice(0, GPSIMD_COLS))
                 round_wbt(e, slice(GPSIMD_COLS, P), nc.scalar.copy)
             else:
-                round_wbt(e, slice(VECTOR_COLS if e > 2 else 0, P), nc.scalar.copy)
-                if e > 2:
-                    round_wbt(e, slice(0, VECTOR_COLS), nc.vector.tensor_copy)
-                if AHEAD <= e < last:
-                    activations(e + 1)
+                round_wbt(e, slice(VECTOR_COLS, P), nc.scalar.copy)
+                round_wbt(e, slice(0, VECTOR_COLS), nc.vector.tensor_copy)
+            if e < last:
+                activations(e + 1)
             if e > 1:
                 quantise_dh(e - 2, dh_shared)
             quantise_wbt(e)

@@ -190,7 +190,7 @@ def tile_moe_adb_silu_kernel(
             if e == 1:
                 dh_shared = wb_bf[1][:, 0:PIECE]
             if e > 0:
-                round_dh(e - 1, nc.gpsimd, dh_shared, 4)
+                round_dh(e - 1, nc.gpsimd, dh_shared, 8)
             make_brackets(e)
         quantise_dh(before, dh_shared)
 

@@ -24,7 +24,7 @@ LIST_COL = 16
 PAIRS = E // 2
 PIECE = PACK * C
 WINDOW = 2048
-GPSIMD_COLS = 56
+GPSIMD_COLS = 88
 VECTOR_COLS = 48
 HALF_T = T // 2
 
@@ -114,11 +114,15 @@ def tile_moe_adb_silu_kernel(
                 wb_raw[e][:].rearrange("p (j m u w) -> p u m j w", j=PACK, u=2, w=2)[:, :, cols],
             )
 
+        def by_lines(e, cols):
+            return (
+                wb_bf[e][:].rearrange("p (t m j) -> p m j t", t=PACK, j=PACK)[:, cols],
+                wb_raw[e][:].rearrange("p (j m t) -> p m j t", t=PACK, j=PACK)[:, cols],
+            )
+
         def round_wbt_on_gpsimd(e, cols):
             nc.gpsimd.tensor_scalar(
-                wb_bf[e][:].rearrange("p (t m j) -> p m t j", t=PACK, j=PACK)[:, cols],
-                wb_raw[e][:].rearrange("p (j m t) -> p m t j", t=PACK, j=PACK)[:, cols],
-                1.0, 0.0, ALU.mult, ALU.add,
+                *by_lines(e, cols), 1.0, 0.0, ALU.mult, ALU.add
             )
 
         def quantise_wbt(e):
@@ -175,12 +179,12 @@ def tile_moe_adb_silu_kernel(
                 spread_gates(e // 2)
             wb_bf[e] = keep.tile([P, PACK * H], BF16, name="wb_bf_%d" % (0 if e < 2 else 1 + e % 2), align_bytes=64)
             if e == 0:
-                round_wbt(e, slice(0, P), nc.scalar.copy)
+                nc.scalar.copy(*by_lines(e, slice(0, P)))
             elif e == 1:
                 round_wbt_on_gpsimd(e, slice(0, GPSIMD_COLS))
-                round_wbt(e, slice(GPSIMD_COLS, P), nc.scalar.copy)
+                nc.scalar.copy(*by_lines(e, slice(GPSIMD_COLS, P)))
             else:
-                round_wbt(e, slice(VECTOR_COLS, P), nc.scalar.copy)
+                nc.scalar.copy(*by_lines(e, slice(VECTOR_COLS, P)))
                 round_wbt(e, slice(0, VECTOR_COLS), nc.vector.tensor_copy)
             if e < last:
                 activations(e + 1)

@@ -205,23 +205,26 @@ def tile_moe_adb_silu_kernel(
             nc.sync.dma_start(list_tile[:], pos)
             pos_t.append(list_tile)
 
-        small_loads = [lambda r=r: load_scale_rows(wt_s, wt_scales, r) for r in range(4)]
-        small_loads.append(lambda: nc.sync.dma_start(wt_w[:].bitcast(I32), wt_words[0].bitcast(I32)))
-        small_loads.extend(lambda pos=pos: load_list(pos) for pos in (pos1, pos2, pos3))
-        for i in range(2 * E):
-            g, e = divmod(i, E)
-            if g == 1:
-                wa_raw[g, e] = a_t[e][:]
-            elif e == last:
-                wa_raw[g, e] = placed.tile([P, PIECE], F32, name="wa_raw_last", offset=4 * PIECE)[:]
-            else:
-                wa_raw[g, e] = keep.tile([P, PIECE], F32, name="wa_raw_%d" % e, align_bytes=64)[:]
-            nc.sync.dma_start(
-                wa_raw[g, e].rearrange("p (j c) -> p j c", j=PACK),
-                wat[e].rearrange("(p j) c -> p j c", j=PACK)[:, :, g * C:(g + 1) * C],
-            )
-            if i < len(small_loads):
-                small_loads[i]()
+        def load_half(g, e, host):
+            wa_raw[g, e] = host.rearrange("p (j c) -> p j c", j=PACK)
+            nc.sync.dma_start(wa_raw[g, e], wat[e].rearrange("(p j) c -> p j c", j=PACK)[:, :, g * C:(g + 1) * C])
+
+        for e in range(2):
+            wa_whole = keep.tile([P, PACK * K], F32, name="wa_raw_%d" % e, align_bytes=64)
+            nc.sync.dma_start(wa_whole[:], wat[e].rearrange("(p j) c -> p (j c)", j=PACK))
+            for g in range(2):
+                wa_raw[g, e] = wa_whole[:].rearrange("p (j c) -> p j c", j=PACK)[:, :, g * C:(g + 1) * C]
+        for e in range(2, last):
+            load_half(0, e, keep.tile([P, PIECE], F32, name="wa_raw_%d" % e, align_bytes=64)[:])
+        load_half(0, last, placed.tile([P, PIECE], F32, name="wa_raw_last", offset=4 * PIECE)[:])
+        for pos in (pos1, pos2, pos3):
+            load_list(pos)
+        load_half(1, 2, a_t[2][:])
+        for r in range(4):
+            load_scale_rows(wt_s, wt_scales, r)
+        nc.sync.dma_start(wt_w[:].bitcast(I32), wt_words[0].bitcast(I32))
+        for e in range(3, E):
+            load_half(1, e, a_t[e][:])
 
         wa_bf, wa_mx = {}, {}
 
@@ -232,7 +235,7 @@ def tile_moe_adb_silu_kernel(
                 )
             copy(
                 wa_bf[g, e // 2][:, e % 2 * PIECE:(e % 2 + 1) * PIECE].rearrange("p (c i j) -> p c j i", i=PACK, j=PACK),
-                wa_raw[g, e].rearrange("p (j c i) -> p c j i", i=PACK, j=PACK),
+                wa_raw[g, e].rearrange("p j (c i) -> p c j i", i=PACK),
             )
 
         def quantise_wat(g, u, tag=None):
@@ -287,9 +290,11 @@ def tile_moe_adb_silu_kernel(
         def store(q, total, h):
             nc.sync.dma_start(out[q * P:(q + 1) * P, halves[h]], total[:, halves[h]])
 
-        def combine(q, first_sum, total, before_last=None):
+        def combine(q, first_sum, total, after_first=None, before_last=None):
             for h in range(2):
                 add(first_sum, bases[q][:, halves[h]], room(q, 0), h)
+            if after_first is not None:
+                after_first()
             for h in range(2):
                 add(room(q, 2), fetched(q, 2, h), first_sum, h)
             if before_last is not None:
@@ -306,6 +311,7 @@ def tile_moe_adb_silu_kernel(
         quantise_wat(0, 1)
         quantise_dh(last, dh_last[:], "wa_bf_0_1")
         quantise_wat(0, 2)
+        round_wat(1, 0, nc.vector.tensor_copy, "wa_bf_0_2")
         dx[0] = placed.tile([P, S], F32, name="dx_0", offset=0)
         dx[1] = placed.tile([P, S], F32, name="dx_1", offset=4 * S)
         for q, u in ((0, 0), (1, 0), (0, 1), (1, 1), (0, 2)):
@@ -315,14 +321,16 @@ def tile_moe_adb_silu_kernel(
         multiply_base(0)
         multiply_base(1)
         fetch(0, 1, False)
-        for e in range(3):
+        for e in (1, 2):
             round_wat(1, e, nc.vector.tensor_copy)
         quantise_wat(1, 0, "a_raw_2")
         round_wat(1, 3, nc.vector.tensor_copy)
-        round_wat(1, before, nc.vector.tensor_copy)
-        quantise_wat(1, 1, "a_raw_4")
-        first_sum = keep.tile([P, T], F32, name="wa_bf_1_1", align_bytes=64)
-        combine(0, first_sum, wa_raw[1, last], lambda: round_wat(1, last, nc.vector.tensor_copy))
+
+        def last_roundings():
+            for e in (before, last):
+                round_wat(1, e, nc.vector.tensor_copy)
+
+        combine(0, a_t[3], a_t[last], lambda: quantise_wat(1, 1), last_roundings)
         quantise_wat(1, 2)
         fetch(1, 0, False)
         fetch(1, 1, False)

@@ -24,8 +24,8 @@ LIST_COL = 16
 PAIRS = E // 2
 PIECE = PACK * C
 WINDOW = 2048
-GPSIMD_COLS = 88
-VECTOR_COLS = 48
+GPSIMD_COLS = 96
+VECTOR_COLS = 36
 HALF_T = T // 2
 
 
@@ -209,21 +209,17 @@ def tile_moe_adb_silu_kernel(
             wa_raw[g, e] = host.rearrange("p (j c) -> p j c", j=PACK)
             nc.sync.dma_start(wa_raw[g, e], wat[e].rearrange("(p j) c -> p j c", j=PACK)[:, :, g * C:(g + 1) * C])
 
-        for e in range(2):
-            wa_whole = keep.tile([P, PACK * K], F32, name="wa_raw_%d" % e, align_bytes=64)
-            nc.sync.dma_start(wa_whole[:], wat[e].rearrange("(p j) c -> p (j c)", j=PACK))
-            for g in range(2):
-                wa_raw[g, e] = wa_whole[:].rearrange("p (j c) -> p j c", j=PACK)[:, :, g * C:(g + 1) * C]
-        for e in range(2, last):
+        for e in range(last):
             load_half(0, e, keep.tile([P, PIECE], F32, name="wa_raw_%d" % e, align_bytes=64)[:])
         load_half(0, last, placed.tile([P, PIECE], F32, name="wa_raw_last", offset=4 * PIECE)[:])
         for pos in (pos1, pos2, pos3):
             load_list(pos)
-        load_half(1, 2, a_t[2][:])
+        for e in range(before):
+            load_half(1, e, a_t[e][:])
         for r in range(4):
             load_scale_rows(wt_s, wt_scales, r)
         nc.sync.dma_start(wt_w[:].bitcast(I32), wt_words[0].bitcast(I32))
-        for e in range(3, E):
+        for e in (before, last):
             load_half(1, e, a_t[e][:])
 
         wa_bf, wa_mx = {}, {}
@@ -292,11 +288,11 @@ def tile_moe_adb_silu_kernel(
 
         def combine(q, first_sum, total, after_first=None, before_last=None):
             for h in range(2):
-                add(first_sum, bases[q][:, halves[h]], room(q, 0), h)
+                add(first_sum, fetched(q, 2, h), room(q, 0), h)
             if after_first is not None:
                 after_first()
             for h in range(2):
-                add(room(q, 2), fetched(q, 2, h), first_sum, h)
+                add(room(q, 2), bases[q][:, halves[h]], first_sum, h)
             if before_last is not None:
                 before_last()
             for h in range(2):

@@ -26,6 +26,7 @@ PIECE = PACK * C
 WINDOW = 2048
 GPSIMD_COLS = 96
 VECTOR_COLS = 36
+WHOLE = 1
 HALF_T = T // 2
 
 
@@ -205,52 +206,93 @@ def tile_moe_adb_silu_kernel(
             nc.sync.dma_start(list_tile[:], pos)
             pos_t.append(list_tile)
 
-        def load_half(g, e, host):
-            wa_raw[g, e] = host.rearrange("p (j c) -> p j c", j=PACK)
-            nc.sync.dma_start(wa_raw[g, e], wat[e].rearrange("(p j) c -> p j c", j=PACK)[:, :, g * C:(g + 1) * C])
+        def load_columns(e, first, count, host):
+            view = host.rearrange("p (j c) -> p j c", j=PACK)
+            nc.sync.dma_start(view, wat[e].rearrange("(p j) c -> p j c", j=PACK)[:, :, first:first + count])
+            return view
 
-        for e in range(last):
-            load_half(0, e, keep.tile([P, PIECE], F32, name="wa_raw_%d" % e, align_bytes=64)[:])
-        load_half(0, last, placed.tile([P, PIECE], F32, name="wa_raw_last", offset=4 * PIECE)[:])
+        for e in range(WHOLE):
+            wa_whole = keep.tile([P, PACK * K], F32, name="wa_raw_%d" % e, align_bytes=64)
+            nc.sync.dma_start(wa_whole[:], wat[e].rearrange("(p j) c -> p (j c)", j=PACK))
+            for g in range(2):
+                wa_raw[g, e] = wa_whole[:].rearrange("p (j c) -> p j c", j=PACK)[:, :, g * C:(g + 1) * C]
+        for e in range(WHOLE, last):
+            wa_raw[0, e] = load_columns(e, 0, C, keep.tile([P, PIECE], F32, name="wa_raw_%d" % e, align_bytes=64)[:])
+        quarter_tiles, quarters = {}, {}
+
+        def load_quarter(q):
+            if q == 1:
+                quarter_tiles[q] = placed.tile([P, PACK * P], F32, name="wa_last_1", offset=4 * S - 8 * P)
+            else:
+                quarter_tiles[q] = keep.tile([P, PACK * P], F32, name="wa_last_%d" % q, align_bytes=64)
+            quarters[q] = load_columns(last, q * P, P, quarter_tiles[q][:])
+
+        for q in range(2):
+            load_quarter(q)
         for pos in (pos1, pos2, pos3):
             load_list(pos)
-        for e in range(before):
-            load_half(1, e, a_t[e][:])
+        for e in range(WHOLE, 3):
+            wa_raw[1, e] = load_columns(e, C, C, a_t[e][:])
         for r in range(4):
             load_scale_rows(wt_s, wt_scales, r)
         nc.sync.dma_start(wt_w[:].bitcast(I32), wt_words[0].bitcast(I32))
-        for e in (before, last):
-            load_half(1, e, a_t[e][:])
+        for e in range(3, last):
+            wa_raw[1, e] = load_columns(e, C, C, a_t[e][:])
+        for q in range(2, 4):
+            load_quarter(q)
 
         wa_bf, wa_mx = {}, {}
 
-        def round_wat(g, e, copy, tag=None):
-            if e % 2 == 0:
-                wa_bf[g, e // 2] = keep.tile(
-                    [P, 2 * PIECE], BF16, name=tag or "wa_bf_%d_%d" % (g, e // 2), align_bytes=64
-                )
+        def stage(g, u, tag):
+            wa_bf[g, u] = keep.tile([P, 2 * PIECE], BF16, name=tag, align_bytes=64)
+
+        def round_wat(g, e, copy):
             copy(
                 wa_bf[g, e // 2][:, e % 2 * PIECE:(e % 2 + 1) * PIECE].rearrange("p (c i j) -> p c j i", i=PACK, j=PACK),
                 wa_raw[g, e].rearrange("p j (c i) -> p c j i", i=PACK),
             )
 
+        def round_before(g, copy):
+            copy(
+                wa_bf[g, 2][:].rearrange("p (q v c i j) -> p v q c j i", q=2, v=2, i=PACK, j=PACK)[:, 0],
+                wa_raw[g, before].rearrange("p j (q c i) -> p q c j i", q=2, i=PACK),
+            )
+
+        def round_quarter(q, copy):
+            first = (2 * (q % 2) + 1) * PACK * P
+            copy(
+                wa_bf[q // 2, 2][:, first:first + PACK * P].rearrange("p (c i j) -> p c j i", i=PACK, j=PACK),
+                quarters[q].rearrange("p j (c i) -> p c j i", i=PACK),
+            )
+
         def quantise_wat(g, u, tag=None):
-            words = keep.tile([P, 2 * C], U32, name=tag or "wa_w_%d_%d" % (g, u), align_bytes=64)[:]
+            words = keep.tile([P, 2 * C], U32, name=tag or "wa_w_%d_%d" % (g, u), align_bytes=64)
             plane = keep.tile([P, 2 * C], U8, name="wa_s_%d_%d" % (g, u), align_bytes=64)
-            nc.vector.quantize_mx(words.bitcast(FP8X4), plane[:], wa_bf[g, u][:])
-            wa_mx[g, u] = (words, plane)
+            nc.vector.quantize_mx(words[:].bitcast(FP8X4), plane[:], wa_bf[g, u][:])
+            for v in range(2):
+                for j in range(2):
+                    own = slice(v * C + j * P, v * C + (j + 1) * P)
+                    wa_mx[2 * g + j, 2 * u + v] = (words[:, own], plane[:, own])
+
+        def quantise_last_pair(q, tag=None):
+            words = keep.tile([P, C], U32, name=tag or "wa_w_last_%d" % q, align_bytes=64)
+            plane = keep.tile([P, C], U8, name="wa_s_last_%d" % q, align_bytes=64)
+            nc.vector.quantize_mx(
+                words[:].bitcast(FP8X4), plane[:], wa_bf[q // 2, 2][:, q % 2 * PIECE:(q % 2 + 1) * PIECE]
+            )
+            for v in range(2):
+                wa_mx[q, before + v] = (words[:, v * P:(v + 1) * P], plane[:, v * P:(v + 1) * P])
 
         dx, bases = {}, {}
 
         def multiply_pair(q, u):
             bank = psum.tile([P, 2 * C], F32, name="bank")
-            wa_w, wa_s = wa_mx[q // 2, u]
             for v in range(2):
+                wa_w, wa_s = wa_mx[q, 2 * u + v]
                 words, plane = dh_mx[2 * u + v]
-                own = slice(v * C + q % 2 * P, v * C + (q % 2 + 1) * P)
                 nc.tensor.matmul_mx(
                     bank[:, v * C:(v + 1) * C],
-                    lhsT=wa_w[:, own].bitcast(FP8X4), lhsT_scale=wa_s[:, own],
+                    lhsT=wa_w.bitcast(FP8X4), lhsT_scale=wa_s,
                     rhs=words.bitcast(FP8X4), rhs_scale=plane[:],
                     start=True, stop=True,
                 )
@@ -286,55 +328,70 @@ def tile_moe_adb_silu_kernel(
         def store(q, total, h):
             nc.sync.dma_start(out[q * P:(q + 1) * P, halves[h]], total[:, halves[h]])
 
-        def combine(q, first_sum, total, after_first=None, before_last=None):
-            for h in range(2):
-                add(first_sum, fetched(q, 2, h), room(q, 0), h)
-            if after_first is not None:
-                after_first()
-            for h in range(2):
-                add(room(q, 2), bases[q][:, halves[h]], first_sum, h)
-            if before_last is not None:
-                before_last()
-            for h in range(2):
-                add(total, room(q, 1)[:, halves[h]], room(q, 2), h)
-                store(q, total, h)
+        def add_third_list(q, target, between=None):
+            add(target, fetched(q, 2, 0), room(q, 0), 0)
+            if between is not None:
+                between()
+            add(target, fetched(q, 2, 1), room(q, 0), 1)
 
-        for e in range(E):
+        def add_base(q, target, partial, between=None):
+            add(target, bases[q][:, halves[0]], partial, 0)
+            if between is not None:
+                between()
+            add(target, bases[q][:, halves[1]], partial, 1)
+
+        def add_second_list(q, target, partial):
+            for h in range(2):
+                add(target, room(q, 1)[:, halves[h]], partial, h)
+                store(q, target, h)
+
+        for u in range(PAIRS):
+            stage(0, u, "wa_bf_0_%d" % u)
+        for e in range(before):
             round_wat(0, e, nc.scalar.copy)
+        round_before(0, nc.scalar.copy)
+        for q in range(2):
+            round_quarter(q, nc.scalar.copy)
         quantise_wat(0, 0)
         dh_last = keep.tile([P, PIECE], BF16, name="wa_bf_0_0", align_bytes=64)
         round_dh(last, nc.vector, dh_last[:], 2)
         quantise_wat(0, 1)
         quantise_dh(last, dh_last[:], "wa_bf_0_1")
-        quantise_wat(0, 2)
-        round_wat(1, 0, nc.vector.tensor_copy, "wa_bf_0_2")
+        stage(1, 0, "wa_bf_0_0")
+        round_wat(1, 0, nc.vector.tensor_copy)
+        for q in range(2):
+            quantise_last_pair(q)
+        round_wat(1, 1, nc.vector.tensor_copy)
+        wa_bf[1, 1] = placed.tile([P, 2 * PIECE], BF16, name="wa_bf_1_1", align_bytes=64, offset=8 * S + 4 * PIECE)
+        round_wat(1, 2, nc.vector.tensor_copy)
+        quantise_wat(1, 0, "a_raw_2")
         dx[0] = placed.tile([P, S], F32, name="dx_0", offset=0)
         dx[1] = placed.tile([P, S], F32, name="dx_1", offset=4 * S)
         for q, u in ((0, 0), (1, 0), (0, 1), (1, 1), (0, 2)):
             multiply_pair(q, u)
         fetch(0, 0, True)
         multiply_pair(1, 2)
+        fetch(0, 1, False)
         multiply_base(0)
         multiply_base(1)
-        fetch(0, 1, False)
-        for e in (1, 2):
-            round_wat(1, e, nc.vector.tensor_copy)
-        quantise_wat(1, 0, "a_raw_2")
+        partial = keep.tile([P, T], F32, name="wa_bf_0_0", align_bytes=64)
+        add_third_list(0, partial)
         round_wat(1, 3, nc.vector.tensor_copy)
-
-        def last_roundings():
-            for e in (before, last):
-                round_wat(1, e, nc.vector.tensor_copy)
-
-        combine(0, a_t[3], a_t[last], lambda: quantise_wat(1, 1), last_roundings)
-        quantise_wat(1, 2)
+        add_base(0, a_t[3], partial)
+        quantise_wat(1, 1)
+        stage(1, 2, "wa_bf_1_2")
+        round_before(1, nc.vector.tensor_copy)
+        add_second_list(0, a_t[before], a_t[3])
         fetch(1, 0, False)
         fetch(1, 1, False)
-        first_sum = keep.tile([P, T], F32, name="wa_bf_1_2", align_bytes=64)
-        combine(1, first_sum, room(1, 3))
-        dx[2] = keep.tile([P, S], F32, name="dx_2", align_bytes=64)
-        dx[3] = keep.tile([P, S], F32, name="dx_3", align_bytes=64)
-        for q, u in ((2, 0), (2, 1), (3, 0), (3, 1)):
+        round_quarter(2, nc.vector.tensor_copy)
+        add_third_list(1, quarter_tiles[2], lambda: quantise_last_pair(2))
+        round_quarter(3, nc.vector.tensor_copy)
+        add_base(1, quarter_tiles[3], quarter_tiles[2], lambda: quantise_last_pair(3))
+        add_second_list(1, room(1, 3), quarter_tiles[3])
+        dx[2] = placed.tile([P, S], F32, name="dx_2", offset=8 * S)
+        dx[3] = placed.tile([P, S], F32, name="dx_3", offset=12 * S)
+        for q, u in ((2, 0), (3, 0), (2, 1), (3, 1)):
             multiply_pair(q, u)
         multiply_base(3)
         nc.scalar.copy(room(3, PACK), bases[3][:])
@@ -343,7 +400,9 @@ def tile_moe_adb_silu_kernel(
         multiply_pair(3, 2)
         multiply_base(2)
         fetch(2, 1, False)
-        combine(2, room(2, PACK), room(2, 3))
+        add_third_list(2, room(2, PACK))
+        add_base(2, room(2, 2), room(2, PACK))
+        add_second_list(2, room(2, 3), room(2, 2))
         fetch(3, 0, True)
         nc.scalar.activation(room(3, 1)[:, halves[0]], fetched(3, 1, 0), ACT.Copy)
         for h in range(2):

from contextlib import ExitStack

import concourse.mybir as mybir
from concourse.masks import make_identity

K, T, E, C, H, N, TOP = 512, 512, 6, 256, 512, 512, 3
S = E * C
FLOPS = 2 * N * K * T + 2 * S * (N * H + H * K)

F32 = mybir.dt.float32
BF16 = mybir.dt.bfloat16
I32 = mybir.dt.int32
U32 = mybir.dt.uint32
U16 = mybir.dt.uint16
U8 = mybir.dt.uint8
FP8X4 = mybir.dt.float8_e4m3fn_x4
FP4X4 = mybir.dt.float4_e2m1fn_x4
ALU = mybir.AluOpType
ACT = mybir.ActivationFunctionType

P = 128
PACK = 4
LIST_COL = 16
PAIRS = E // 2
PIECE = PACK * C
WINDOW = 2048
GPSIMD_COLS = 96
VECTOR_COLS = 36
WHOLE = 1
HALF_T = T // 2


def tile_moe_adb_silu_kernel(
    tc, dy_words, dy_scales, wt_words, wt_scales, wbt, wat, a, gate, offs, pos1, pos2, pos3, out
):
    nc = tc.nc
    with ExitStack() as ctx:
        keep = ctx.enter_context(tc.tile_pool(name="keep", bufs=1))
        ring = ctx.enter_context(tc.tile_pool(name="ring", bufs=3))
        placed = ctx.enter_context(tc.tile_pool(name="placed", bufs=1))
        psum = ctx.enter_context(tc.psum_pool(name="psum", bufs=8))

        def load_scale_rows(plane, scales, r):
            rows = scales[0].rearrange("(q r) n -> r q n", r=4)
            nc.sync.dma_start(plane[r:P:32, 0:T].bitcast(I32), rows[r].bitcast(I32))

        offs_t = keep.tile([P, S // LIST_COL], U16, name="offs_t")
        nc.sync.dma_start(offs_t[:], offs)
        dy_w = keep.tile([P, WINDOW], U32, name="dy_w", align_bytes=64)
        nc.sync.dma_start(dy_w[:, 0:T].bitcast(I32), dy_words[0].rearrange("p t d -> p (t d)").bitcast(I32))
        dy_s = keep.tile([P, WINDOW], U8, name="dy_s", align_bytes=64)
        nc.vector.memset(dy_s[:].bitcast(I32), 0)
        nc.vector.memset(dy_w[:, T:WINDOW].bitcast(I32), 0)

        gate_rows = keep.tile([P, P], F32, name="gate_r")
        ident = keep.tile([P, P], F32, name="ident")
        make_identity(nc, ident[:])
        wt_w = keep.tile([P, 2 * K], U8, name="wt_w", align_bytes=64)
        wt_s = keep.tile([P, K], U8, name="wt_s", align_bytes=64)
        nc.vector.memset(wt_s[:].bitcast(I32), 0)

        a_rows = a.rearrange("(p t) s -> p t s", t=PACK)
        a_t, wb_raw = {}, {}

        def load_a(e):
            a_t[e] = keep.tile([P, PIECE], F32, name="a_raw_%d" % e, align_bytes=64)
            nc.sync.dma_start(a_t[e][:].rearrange("p (t s) -> p t s", t=PACK), a_rows[:, :, e * C:(e + 1) * C])

        def load_wbt(e):
            wb_raw[e] = keep.tile([P, PACK * H], F32, name="wb_raw_%d" % e, align_bytes=64)
            nc.sync.dma_start(wb_raw[e][:], wbt[e].rearrange("(p j) c -> p (j c)", j=PACK))

        load_a(0)
        for r in range(4):
            load_scale_rows(dy_s, dy_scales, r)
        nc.sync.dma_start(gate_rows[:], gate.rearrange("r (b p) -> (r b) p", p=P)[0:P, :])
        for e in range(E):
            load_wbt(e)
            if e < E - 1:
                load_a(e + 1)

        slot_w = keep.tile([P, S], U32, name="g_w", align_bytes=64)
        slot_s = keep.tile([P, S], U8, name="g_s", align_bytes=64)
        nc.vector.tensor_copy(slot_w[:], dy_w[:].indirect(offs_t[:]))
        nc.vector.tensor_copy(slot_s[:], dy_s[:].indirect(offs_t[:]))

        gate_ps = psum.tile([P, P], F32, name="bank")
        nc.tensor.transpose(gate_ps[:], gate_rows[:], ident[:])
        gate_cols = keep.tile([P, S // P], F32, name="gate_c")
        gate_banks = []
        blocks_per_bank = 2 * C // P

        def spread_gates(u):
            gate_bank = psum.tile([P, 2 * C], F32, name="bank")
            for j in range(blocks_per_bank):
                b = u * blocks_per_bank + j
                nc.tensor.transpose(
                    gate_bank[:, j * P:(j + 1) * P], gate_cols[:, b:b + 1].to_broadcast([P, P]), ident[:]
                )
            gate_banks.append(gate_bank)

        activated, wb_bf, wb_mx, dh_mx = {}, {}, {}, {}

        def activations(e):
            silu_neg = keep.tile([P, PIECE], F32, name="silu_n_%d" % e, align_bytes=64)
            tanh_half = ring.tile([P, PIECE], F32, name="tanh_h")
            calls = [(silu_neg, ACT.Silu, -1.0), (tanh_half, ACT.Tanh, 0.5)]
            for target, func, scale in calls if e == 0 else reversed(calls):
                nc.scalar.activation(target[:], a_t[e][:], func, scale=scale)
            activated[e] = (silu_neg, tanh_half)

        def round_wbt(e, cols, copy):
            copy(
                wb_bf[e][:].rearrange("p (u w m j) -> p u m j w", u=2, w=2, j=PACK)[:, :, cols],
                wb_raw[e][:].rearrange("p (j m u w) -> p u m j w", j=PACK, u=2, w=2)[:, :, cols],
            )

        def by_lines(e, cols):
            return (
                wb_bf[e][:].rearrange("p (t m j) -> p m j t", t=PACK, j=PACK)[:, cols],
                wb_raw[e][:].rearrange("p (j m t) -> p m j t", t=PACK, j=PACK)[:, cols],
            )

        def round_wbt_on_gpsimd(e, cols):
            nc.gpsimd.tensor_scalar(
                *by_lines(e, cols), 1.0, 0.0, ALU.mult, ALU.add
            )

        def quantise_wbt(e):
            wb_w = ring.tile([P, H], U32, name="wb_w", align_bytes=64, bufs=2)
            wb_s = ring.tile([P, H], U8, name="wb_s", align_bytes=64, bufs=2)
            nc.vector.quantize_mx(wb_w[:].bitcast(FP8X4), wb_s[:], wb_bf[e][:])
            wb_mx[e] = (wb_w, wb_s)

        def make_brackets(e):
            silu_neg, tanh_half = activated[e]
            wb_w, wb_s = wb_mx[e]
            gated, summed = wb_raw[e][:, 0:PIECE], wb_raw[e][:, PIECE:2 * PIECE]
            nc.vector.scalar_tensor_tensor(
                gated.rearrange("p (t c) -> p t c", t=PACK), tanh_half[:].rearrange("p (t c) -> p t c", t=PACK), 1.0,
                gate_banks[e // 2][:, (e % 2) * C:(e % 2 + 1) * C].unsqueeze(1).to_broadcast([P, PACK, C]),
                ALU.add, ALU.mult,
            )
            slots = slice(e * C, (e + 1) * C)
            for h in range(2):
                bank = psum.tile([P, 2 * C], F32, name="bank")
                for w in range(2):
                    t = 2 * h + w
                    nc.tensor.matmul_mx(
                        bank[:, w * C:(w + 1) * C],
                        lhsT=wb_w[:, t * P:(t + 1) * P].bitcast(FP8X4), lhsT_scale=wb_s[:, t * P:(t + 1) * P],
                        rhs=slot_w[:, slots].bitcast(FP8X4), rhs_scale=slot_s[:, slots],
                        start=True, stop=True,
                    )
                own = slice(2 * h * C, 2 * (h + 1) * C)
                nc.vector.scalar_tensor_tensor(
                    summed[:, own], silu_neg[:, own], 1.0, bank[:], ALU.subtract, ALU.mult
                )

        def round_dh(e, engine, dh_bf, run):
            gated, summed = wb_raw[e][:, 0:PIECE], wb_raw[e][:, PIECE:2 * PIECE]
            engine.tensor_tensor(
                dh_bf.rearrange("p (c i t) -> p c t i", i=run, t=PACK),
                gated.rearrange("p (t c i) -> p c t i", i=run, t=PACK),
                summed.rearrange("p (t c i) -> p c t i", i=run, t=PACK),
                ALU.mult,
            )

        def quantise_dh(e, dh_bf, tag=None):
            words = keep.tile([P, C], U32, name=tag or "silu_n_%d" % (e + 1), align_bytes=64)[:]
            plane = keep.tile([P, C], U8, name="dh_s_%d" % e, align_bytes=64)
            nc.vector.quantize_mx(words.bitcast(FP8X4), plane[:], dh_bf)
            dh_mx[e] = (words, plane)

        before, last = E - 2, E - 1
        activations(0)
        nc.scalar.mul(gate_cols[:], gate_ps[:, 0:S // P], -0.5)
        for e in range(E):
            if e % 2 == 0:
                spread_gates(e // 2)
            wb_bf[e] = keep.tile([P, PACK * H], BF16, name="wb_bf_%d" % (0 if e < 2 else 1 + e % 2), align_bytes=64)
            if e == 0:
                nc.scalar.copy(*by_lines(e, slice(0, P)))
            elif e == 1:
                round_wbt_on_gpsimd(e, slice(0, GPSIMD_COLS))
                nc.scalar.copy(*by_lines(e, slice(GPSIMD_COLS, P)))
            else:
                nc.scalar.copy(*by_lines(e, slice(VECTOR_COLS, P)))
                round_wbt(e, slice(0, VECTOR_COLS), nc.vector.tensor_copy)
            if e < last:
                activations(e + 1)
            if e > 1:
                quantise_dh(e - 2, dh_shared)
            quantise_wbt(e)
            if e == 1:
                dh_shared = wb_bf[1][:, 0:PIECE]
            if e > 0:
                round_dh(e - 1, nc.gpsimd, dh_shared, 8)
            make_brackets(e)
        quantise_dh(before, dh_shared)

        wa_raw, pos_t = {}, []

        def load_list(pos):
            list_tile = keep.tile([P, T // LIST_COL], U16, name="pos_%d" % len(pos_t))
            nc.sync.dma_start(list_tile[:], pos)
            pos_t.append(list_tile)

        def load_columns(e, first, count, host):
            view = host.rearrange("p (j c) -> p j c", j=PACK)
            nc.sync.dma_start(view, wat[e].rearrange("(p j) c -> p j c", j=PACK)[:, :, first:first + count])
            return view

        for e in range(WHOLE):
            wa_whole = keep.tile([P, PACK * K], F32, name="wa_raw_%d" % e, align_bytes=64)
            nc.sync.dma_start(wa_whole[:], wat[e].rearrange("(p j) c -> p (j c)", j=PACK))
            for g in range(2):
                wa_raw[g, e] = wa_whole[:].rearrange("p (j c) -> p j c", j=PACK)[:, :, g * C:(g + 1) * C]
        for e in range(WHOLE, last):
            wa_raw[0, e] = load_columns(e, 0, C, keep.tile([P, PIECE], F32, name="wa_raw_%d" % e, align_bytes=64)[:])
        quarter_tiles, quarters = {}, {}

        def load_quarter(q):
            if q == 1:
                quarter_tiles[q] = placed.tile([P, PACK * P], F32, name="wa_last_1", offset=4 * S - 8 * P)
            else:
                quarter_tiles[q] = keep.tile([P, PACK * P], F32, name="wa_last_%d" % q, align_bytes=64)
            quarters[q] = load_columns(last, q * P, P, quarter_tiles[q][:])

        for q in range(2):
            load_quarter(q)
        for pos in (pos1, pos2, pos3):
            load_list(pos)
        for e in range(WHOLE, 3):
            wa_raw[1, e] = load_columns(e, C, C, a_t[e][:])
        for r in range(4):
            load_scale_rows(wt_s, wt_scales, r)
        nc.sync.dma_start(wt_w[:].bitcast(I32), wt_words[0].bitcast(I32))
        for e in range(3, last):
            wa_raw[1, e] = load_columns(e, C, C, a_t[e][:])
        for q in range(2, 4):
            load_quarter(q)

        wa_bf, wa_mx = {}, {}

        def stage(g, u, tag):
            wa_bf[g, u] = keep.tile([P, 2 * PIECE], BF16, name=tag, align_bytes=64)

        def round_wat(g, e, copy):
            copy(
                wa_bf[g, e // 2][:, e % 2 * PIECE:(e % 2 + 1) * PIECE].rearrange("p (c i j) -> p c j i", i=PACK, j=PACK),
                wa_raw[g, e].rearrange("p j (c i) -> p c j i", i=PACK),
            )

        def round_before(g, copy):
            copy(
                wa_bf[g, 2][:].rearrange("p (q v c i j) -> p v q c j i", q=2, v=2, i=PACK, j=PACK)[:, 0],
                wa_raw[g, before].rearrange("p j (q c i) -> p q c j i", q=2, i=PACK),
            )

        def round_quarter(q, copy):
            first = (2 * (q % 2) + 1) * PACK * P
            copy(
                wa_bf[q // 2, 2][:, first:first + PACK * P].rearrange("p (c i j) -> p c j i", i=PACK, j=PACK),
                quarters[q].rearrange("p j (c i) -> p c j i", i=PACK),
            )

        def quantise_wat(g, u, tag=None):
            words = keep.tile([P, 2 * C], U32, name=tag or "wa_w_%d_%d" % (g, u), align_bytes=64)
            plane = keep.tile([P, 2 * C], U8, name="wa_s_%d_%d" % (g, u), align_bytes=64)
            nc.vector.quantize_mx(words[:].bitcast(FP8X4), plane[:], wa_bf[g, u][:])
            for v in range(2):
                for j in range(2):
                    own = slice(v * C + j * P, v * C + (j + 1) * P)
                    wa_mx[2 * g + j, 2 * u + v] = (words[:, own], plane[:, own])

        def quantise_last_pair(q, tag=None):
            words = keep.tile([P, C], U32, name=tag or "wa_w_last_%d" % q, align_bytes=64)
            plane = keep.tile([P, C], U8, name="wa_s_last_%d" % q, align_bytes=64)
            nc.vector.quantize_mx(
                words[:].bitcast(FP8X4), plane[:], wa_bf[q // 2, 2][:, q % 2 * PIECE:(q % 2 + 1) * PIECE]
            )
            for v in range(2):
                wa_mx[q, before + v] = (words[:, v * P:(v + 1) * P], plane[:, v * P:(v + 1) * P])

        dx, bases = {}, {}

        def multiply_pair(q, u):
            bank = psum.tile([P, 2 * C], F32, name="bank")
            for v in range(2):
                wa_w, wa_s = wa_mx[q, 2 * u + v]
                words, plane = dh_mx[2 * u + v]
                nc.tensor.matmul_mx(
                    bank[:, v * C:(v + 1) * C],
                    lhsT=wa_w.bitcast(FP8X4), lhsT_scale=wa_s,
                    rhs=words.bitcast(FP8X4), rhs_scale=plane[:],
                    start=True, stop=True,
                )
            nc.scalar.copy(dx[q][:, 2 * u * C:2 * (u + 1) * C], bank[:])

        def multiply_base(q):
            bases[q] = psum.tile([P, T], F32, name="bank")
            nc.tensor.matmul_mx(
                bases[q][:],
                lhsT=wt_w[:, 2 * q * P:2 * (q + 1) * P].bitcast(FP4X4), lhsT_scale=wt_s[:, q * P:(q + 1) * P],
                rhs=dy_w[:, 0:T].bitcast(FP8X4), rhs_scale=dy_s[:, 0:T],
                start=True, stop=True,
            )

        halves = [slice(h * HALF_T, (h + 1) * HALF_T) for h in range(2)]
        list_halves = [slice(h * HALF_T // LIST_COL, (h + 1) * HALF_T // LIST_COL) for h in range(2)]

        def room(q, i):
            if i == PACK:
                return wb_raw[PACK][:, q * T:(q + 1) * T]
            return wb_raw[q][:, i * T:(i + 1) * T]

        def fetch(q, r, split):
            for cols, entries in zip(halves, list_halves) if split else [(slice(0, T), slice(0, T // LIST_COL))]:
                nc.scalar.activation(room(q, r)[:, cols], dx[q][:].indirect(pos_t[r][:, entries]), ACT.Copy)

        def add(target, left, right, h):
            nc.vector.tensor_tensor(target[:, halves[h]], left, right[:, halves[h]], ALU.add)

        def fetched(q, r, h):
            return dx[q][:].indirect(pos_t[r][:, list_halves[h]])

        def store(q, total, h):
            nc.sync.dma_start(out[q * P:(q + 1) * P, halves[h]], total[:, halves[h]])

        def add_third_list(q, target, between=None):
            add(target, fetched(q, 2, 0), room(q, 0), 0)
            if between is not None:
                between()
            add(target, fetched(q, 2, 1), room(q, 0), 1)

        def add_base(q, target, partial, between=None):
            add(target, bases[q][:, halves[0]], partial, 0)
            if between is not None:
                between()
            add(target, bases[q][:, halves[1]], partial, 1)

        def add_second_list(q, target, partial):
            for h in range(2):
                add(target, room(q, 1)[:, halves[h]], partial, h)
                store(q, target, h)

        for u in range(PAIRS):
            stage(0, u, "wa_bf_0_%d" % u)
        for e in range(before):
            round_wat(0, e, nc.scalar.copy)
        round_before(0, nc.scalar.copy)
        for q in range(2):
            round_quarter(q, nc.scalar.copy)
        quantise_wat(0, 0)
        dh_last = keep.tile([P, PIECE], BF16, name="wa_bf_0_0", align_bytes=64)
        round_dh(last, nc.vector, dh_last[:], 2)
        quantise_wat(0, 1)
        quantise_dh(last, dh_last[:], "wa_bf_0_1")
        stage(1, 0, "wa_bf_0_0")
        round_wat(1, 0, nc.vector.tensor_copy)
        for q in range(2):
            quantise_last_pair(q)
        round_wat(1, 1, nc.vector.tensor_copy)
        wa_bf[1, 1] = placed.tile([P, 2 * PIECE], BF16, name="wa_bf_1_1", align_bytes=64, offset=8 * S + 4 * PIECE)
        round_wat(1, 2, nc.vector.tensor_copy)
        quantise_wat(1, 0, "a_raw_2")
        dx[0] = placed.tile([P, S], F32, name="dx_0", offset=0)
        dx[1] = placed.tile([P, S], F32, name="dx_1", offset=4 * S)
        for q, u in ((0, 0), (1, 0), (0, 1), (1, 1), (0, 2)):
            multiply_pair(q, u)
        fetch(0, 0, True)
        multiply_pair(1, 2)
        fetch(0, 1, False)
        multiply_base(0)
        multiply_base(1)
        partial = keep.tile([P, T], F32, name="wa_bf_0_0", align_bytes=64)
        add_third_list(0, partial)
        round_wat(1, 3, nc.vector.tensor_copy)
        add_base(0, a_t[3], partial)
        quantise_wat(1, 1)
        stage(1, 2, "wa_bf_1_2")
        round_before(1, nc.vector.tensor_copy)
        add_second_list(0, a_t[before], a_t[3])
        fetch(1, 0, False)
        fetch(1, 1, False)
        round_quarter(2, nc.vector.tensor_copy)
        add_third_list(1, quarter_tiles[2], lambda: quantise_last_pair(2))
        round_quarter(3, nc.vector.tensor_copy)
        add_base(1, quarter_tiles[3], quarter_tiles[2], lambda: quantise_last_pair(3))
        add_second_list(1, room(1, 3), quarter_tiles[3])
        dx[2] = placed.tile([P, S], F32, name="dx_2", offset=8 * S)
        dx[3] = placed.tile([P, S], F32, name="dx_3", offset=12 * S)
        for q, u in ((2, 0), (3, 0), (2, 1), (3, 1)):
            multiply_pair(q, u)
        multiply_base(3)
        nc.scalar.copy(room(3, PACK), bases[3][:])
        multiply_pair(2, 2)
        fetch(2, 0, True)
        multiply_pair(3, 2)
        multiply_base(2)
        fetch(2, 1, False)
        add_third_list(2, room(2, PACK))
        add_base(2, room(2, 2), room(2, PACK))
        add_second_list(2, room(2, 3), room(2, 2))
        fetch(3, 0, True)
        nc.scalar.activation(room(3, 1)[:, halves[0]], fetched(3, 1, 0), ACT.Copy)
        for h in range(2):
            add(room(3, 2), fetched(3, 2, h), room(3, PACK), h)
        add(room(3, 3), room(3, 0)[:, halves[0]], room(3, 2), 0)
        add(room(3, 3), fetched(3, 1, 1), room(3, 2), 1)
        add(room(3, PACK), room(3, 1)[:, halves[0]], room(3, 3), 0)
        store(3, room(3, PACK), 0)
        add(room(3, PACK), room(3, 0)[:, halves[1]], room(3, 3), 1)
        store(3, room(3, PACK), 1)
